import numpy as np
import ml_dtypes


def mxq(x, axis, fmt="e4m3"):
    dtype, down = {"e4m3": (ml_dtypes.float8_e4m3fn, 7), "e5m2": (ml_dtypes.float8_e5m2, 14)}[fmt]
    v = np.moveaxis(np.asarray(x, np.float32).astype(ml_dtypes.bfloat16).astype(np.float64), axis, -1)
    blocks = v.reshape(v.shape[:-1] + (-1, 32))
    amax = np.abs(blocks).max(-1, keepdims=True)
    byte = np.maximum(np.where(amax > 0, np.frexp(amax)[1] - 1 + 127, 0) - down, 1)
    scale = np.exp2(byte - 127.0)
    codes = (blocks / scale).astype(np.float32).astype(dtype).astype(np.float64)
    return np.moveaxis((codes * scale).reshape(v.shape), -1, axis)


WIDE = False


def mx_kscale(k):
    if not WIDE:
        return np.ones(k)
    levels = np.array([18, -18])
    if k % 512:
        return np.exp2(np.random.permutation(np.resize(levels, k // 32))).repeat(32)
    a = np.empty((k // 512, 16))
    for p in range(k // 512):
        a[p, :8] = np.random.permutation(np.resize(levels, 8))
        for g in range(8):
            far = levels[np.abs(levels - a[p, g]) >= 10]
            a[p, g + 8] = far[np.random.randint(len(far))]
    return np.exp2(a.ravel()).repeat(32)


def f64(x):
    return np.asarray(x).astype(np.float64)


def striped(idx):
    return np.tile(np.asarray(idx).reshape(-1, 16).T, (8, 1)).astype(np.uint16)


def unstriped(offs):
    return offs[:16].T.reshape(-1).astype(np.int64)


B, N, T, D, R = 1, 512, 2048, 512, 1024
PAGE = 32


def setup_inputs():
    n = np.random.standard_normal
    pages = np.random.permutation(T // PAGE)[:B * N // PAGE]
    idx = (pages[:, None] * PAGE + np.arange(PAGE)[None, :]).reshape(-1)
    s = mx_kscale(D)[:, None]
    z = mx_kscale(R)[:, None]
    x = n((B, D, R))
    return {
        "xT": (x * s).astype(np.float32),
        "wT": (n((D, T)) * (1.00 / np.sqrt(D)) / s).astype(np.float32),
        "vT": (n((D, T)) / np.sqrt(D) / s).astype(np.float32),
        "wt": (np.random.uniform(0.5, 1.5, (B, R, 1)) * 1.0 / np.sqrt(R) * z).astype(np.float32),
        "xm": (x.transpose(0, 2, 1) / z).astype(np.float32),
        "offs": striped(idx),
    }


def reference(xT, wT, vT, wt, xm, offs):
    idx = unstriped(offs)
    pick = lambda x: x[:, idx].reshape(x.shape[0], B, N).transpose(1, 0, 2)
    xq = mxq(f64(xT), 1, "e4m3").transpose(0, 2, 1)
    a = xq @ mxq(pick(f64(wT)), 1, "e4m3")
    av = xq @ mxq(pick(f64(vT)), 1, "e4m3")
    p = 1.0 / (1.0 + np.exp(-a))
    g = f64(wt) * p * (1.0 - p) * av
    dw = mxq(f64(xm), 1, "e4m3").transpose(0, 2, 1) @ mxq(g, 1, "e5m2")
    gw = np.zeros((D, T))
    gw[:, idx] = dw.transpose(1, 0, 2).reshape(D, B * N)
    return gw

@@ -1,0 +1,194 @@
+from contextlib import ExitStack
+
+import concourse.mybir as mybir
+
+D, R, T, N = 512, 1024, 2048, 512
+FLOPS = 3 * 2 * R * D * N
+
+F32 = mybir.dt.float32
+BF16 = mybir.dt.bfloat16
+U32 = mybir.dt.uint32
+U16 = mybir.dt.uint16
+U8 = mybir.dt.uint8
+E4M3 = mybir.dt.float8_e4m3fn_x4
+E5M2 = mybir.dt.float8_e5m2_x4
+ALU = mybir.AluOpType
+ACT = mybir.ActivationFunctionType
+
+P = 128
+PACK = 4
+K_PASS = P * PACK
+ROW_PASSES = R // K_PASS
+SLOT_BLOCK = 128
+SLOT_BLOCKS = N // SLOT_BLOCK
+D_BLOCKS = D // P
+
+
+def tile_attend_ghv_nce_kernel(tc, xT, wT, vT, wt, xm, offs, out):
+    nc = tc.nc
+    with ExitStack() as ctx:
+        keep = ctx.enter_context(tc.tile_pool(name="keep", bufs=1))
+        ring = ctx.enter_context(tc.tile_pool(name="ring", bufs=3))
+        unit_psum = ctx.enter_context(tc.psum_pool(name="unit_psum", bufs=4))
+        out_psum = ctx.enter_context(tc.psum_pool(name="out_psum", bufs=1))
+
+        def quantised(name, width):
+            codes = keep.tile([P, width], U32, name=name + "_codes", align_bytes=64)
+            scales = keep.tile([P, width], U8, name=name + "_scales", align_bytes=64)
+            return codes, scales
+
+        def quantise(pair, cols, grouped, fmt):
+            nc.vector.quantize_mx(out=pair[0][:, cols].bitcast(fmt), scales=pair[1][:, cols], in_=grouped)
+
+        def mx(dst, lhs, lhs_cols, rhs, rhs_cols, rhs_fmt, start, stop):
+            nc.tensor.matmul_mx(
+                out=dst,
+                lhsT=lhs[0][:, lhs_cols].bitcast(E4M3), lhsT_scale=lhs[1][:, lhs_cols],
+                rhs=rhs[0][:, rhs_cols].bitcast(rhs_fmt), rhs_scale=rhs[1][:, rhs_cols],
+                start=start, stop=stop,
+            )
+
+        def interleave(copy, grouped, planes):
+            copy(out=grouped.rearrange("p (c i t) -> p c t i", i=4, t=PACK),
+                 in_=planes.rearrange("p t (c i) -> p c t i", i=4))
+
+        offsets = keep.tile([P, N // 16], U16, name="offsets")
+        x_raw = [keep.tile([P, PACK, K_PASS], F32, name="x_raw%d" % g) for g in range(ROW_PASSES)]
+        m_raw = [keep.tile([P, PACK, D], F32, name="m_raw%d" % g) for g in range(ROW_PASSES)]
+        w_planes = [keep.tile([P, T], F32, name="w_plane%d" % j) for j in range(PACK)]
+        v_planes = [keep.tile([P, T], F32, name="v_plane%d" % j) for j in range(PACK)]
+        wt_raw = keep.tile([P, ROW_PASSES, PACK], F32, name="wt_raw")
+        x_rows = xT[0].rearrange("(p j) r -> p j r", j=PACK)
+        w_rows = wT.rearrange("(p j) c -> p j c", j=PACK)
+        v_rows = vT.rearrange("(p j) c -> p j c", j=PACK)
+        m_rows = xm[0].rearrange("(g p t) d -> g p t d", p=P, t=PACK)
+
+        nc.sync.dma_start(out=x_raw[0][:], in_=x_rows[:, :, 0:K_PASS])
+        nc.sync.dma_start(offsets[:], offs)
+        for j in range(PACK):
+            nc.sync.dma_start(out=w_planes[j][:], in_=w_rows[:, j, :])
+        nc.sync.dma_start(out=wt_raw[:], in_=wt[0].rearrange("(g p t) o -> p g (t o)", p=P, t=PACK))
+        nc.sync.dma_start(out=x_raw[1][:], in_=x_rows[:, :, K_PASS:R])
+        for j in range(PACK):
+            nc.sync.dma_start(out=v_planes[j][:], in_=v_rows[:, j, :])
+        for g in range(ROW_PASSES):
+            nc.sync.dma_start(out=m_raw[g][:], in_=m_rows[g])
+
+        windows = [keep.tile([P, T], F32, name="window%d" % b) for b in range(D_BLOCKS)]
+        for b in range(D_BLOCKS):
+            nc.vector.memset(windows[b][:], 0.0)
+
+        x_q = [quantised("x%d" % g, K_PASS) for g in range(ROW_PASSES)]
+        m_q = [quantised("m%d" % g, D) for g in range(ROW_PASSES)]
+        g_q = [quantised("g%d" % g, N) for g in range(ROW_PASSES)]
+        w_q = quantised("w", N)
+        v_q = quantised("v", N)
+
+        def cast_x(g):
+            grouped = keep.tile([P, K_PASS * PACK], BF16, name="x_grouped%d" % g, align_bytes=64)
+            nc.vector.tensor_copy(
+                out=grouped[:].rearrange("p (t m j) -> p m j t", t=PACK, j=PACK),
+                in_=x_raw[g][:].rearrange("p j (m t) -> p m j t", t=PACK))
+            return grouped
+
+        def gather(picked, planes, j):
+            nc.vector.tensor_copy(picked[:, j, :], planes[j][:].indirect(offsets[:]))
+
+        def slot_cols(s):
+            return slice(s * SLOT_BLOCK, (s + 1) * SLOT_BLOCK)
+
+        def group_block(name, copy, picked, s):
+            grouped = keep.tile([P, SLOT_BLOCK * PACK], BF16, name="%s_grouped%d" % (name, s), align_bytes=64)
+            interleave(copy, grouped[:], picked[:, :, slot_cols(s)])
+            return grouped
+
+        def scores(g, s, table_q):
+            bank = unit_psum.tile([P, PACK, SLOT_BLOCK], F32, name="bank")
+            for t in range(PACK):
+                mx(bank[:, t, :], x_q[g], slice(t * P, (t + 1) * P), table_q, slot_cols(s), E4M3, True, True)
+            return bank
+
+        whole = slice(0, K_PASS)
+        x_grouped = cast_x(0)
+        w_picked = keep.tile([P, PACK, N], F32, name="w_picked")
+        v_picked = keep.tile([P, PACK, N], F32, name="v_picked")
+        gather(w_picked, w_planes, 0)
+        quantise(x_q[0], whole, x_grouped[:], E4M3)
+        for j in range(1, PACK):
+            gather(w_picked, w_planes, j)
+        w_grouped = [None] * SLOT_BLOCKS
+        for s in range(SLOT_BLOCKS + 1):
+            if s < SLOT_BLOCKS:
+                w_grouped[s] = group_block("w", nc.vector.tensor_copy, w_picked, s)
+            if s > 0:
+                quantise(w_q, slot_cols(s - 1), w_grouped[s - 1][:], E4M3)
+
+        wt_quarter = keep.tile([P, ROW_PASSES, PACK], F32, name="wt_quarter")
+        nc.vector.tensor_scalar(out=wt_quarter[:], in0=wt_raw[:], scalar1=-0.25, scalar2=None, op0=ALU.mult)
+        x_grouped = cast_x(1)
+
+        slope = [[None] * SLOT_BLOCKS for g in range(ROW_PASSES)]
+
+        def slope_unit(g, s):
+            bank = scores(g, s, w_q)
+            th = ring.tile([P, SLOT_BLOCK, PACK], F32, name="th")
+            nc.scalar.activation(out=th[:], in_=bank[:].rearrange("p t i -> p i t"), func=ACT.Tanh, scale=0.5)
+            sq = ring.tile([P, SLOT_BLOCK, PACK], F32, name="sq")
+            nc.scalar.activation(out=sq[:], in_=th[:], func=ACT.Square)
+            u = keep.tile([P, SLOT_BLOCK, PACK], F32, name="slope%d_%d" % (g, s))
+            nc.vector.scalar_tensor_tensor(
+                out=u[:], in0=sq[:], scalar=1.0,
+                in1=wt_quarter[:, g:g + 1, :].to_broadcast([P, SLOT_BLOCK, PACK]),
+                op0=ALU.subtract, op1=ALU.mult)
+            slope[g][s] = u
+
+        slope_unit(0, 0)
+        quantise(x_q[1], whole, x_grouped[:], E4M3)
+        slope_unit(0, 1)
+        gather(v_picked, v_planes, 0)
+        slope_unit(0, 2)
+        slope_unit(0, 3)
+        gather(v_picked, v_planes, 1)
+        slope_unit(1, 0)
+        slope_unit(1, 1)
+        gather(v_picked, v_planes, 2)
+        slope_unit(1, 2)
+        slope_unit(1, 3)
+        gather(v_picked, v_planes, 3)
+
+        v_grouped = [group_block("v", nc.vector.tensor_copy if s == 0 else nc.scalar.copy, v_picked, s)
+                     for s in range(SLOT_BLOCKS)]
+        m_grouped = []
+        for g in range(ROW_PASSES):
+            grouped = keep.tile([P, D * PACK], BF16, name="m_grouped%d" % g, align_bytes=64)
+            interleave(nc.scalar.copy, grouped[:], m_raw[g][:])
+            m_grouped.append(grouped)
+
+        acc = [out_psum.tile([P, N], F32, name="acc%d" % b) for b in range(D_BLOCKS)]
+        units = [(g, s) for g in range(ROW_PASSES) for s in range(SLOT_BLOCKS)]
+        quantise(v_q, slot_cols(0), v_grouped[0][:], E4M3)
+        pending = None
+        for g, s in units:
+            if g == 0 and s + 1 < SLOT_BLOCKS:
+                quantise(v_q, slot_cols(s + 1), v_grouped[s + 1][:], E4M3)
+            bank = scores(g, s, v_q)
+            g_grouped = ring.tile([P, SLOT_BLOCK, PACK], BF16, name="g_grouped", align_bytes=64)
+            nc.vector.tensor_tensor(out=g_grouped[:], in0=bank[:].rearrange("p t i -> p i t"),
+                                    in1=slope[g][s][:], op=ALU.mult)
+            if pending is not None:
+                quantise(g_q[pending[0]], slot_cols(pending[1]), pending[2][:].rearrange("p i t -> p (i t)"), E5M2)
+            if (g, s) == (1, 0):
+                quantise(m_q[0], whole, m_grouped[0][:], E4M3)
+                for b in range(D_BLOCKS):
+                    mx(acc[b][:], m_q[0], slice(b * P, (b + 1) * P), g_q[0], whole, E5M2, True, False)
+            if (g, s) == (1, 2):
+                quantise(m_q[1], whole, m_grouped[1][:], E4M3)
+            pending = (g, s, g_grouped)
+        quantise(g_q[pending[0]], slot_cols(pending[1]), pending[2][:].rearrange("p i t -> p (i t)"), E5M2)
+
+        for b in range(D_BLOCKS):
+            mx(acc[b][:], m_q[1], slice(b * P, (b + 1) * P), g_q[1], whole, E5M2, False, True)
+            dense = ring.tile([P, N], F32, name="dense")
+            nc.scalar.copy(out=dense[:], in_=acc[b][:])
+            nc.vector.tensor_copy(windows[b][:].indirect(offsets[:]), dense[:])
+            nc.sync.dma_start(out=out[b * P:(b + 1) * P, :], in_=windows[b][:])

@@ -8,6 +8,7 @@ FLOPS = 3 * 2 * R * D * N
 F32 = mybir.dt.float32
 BF16 = mybir.dt.bfloat16
 U32 = mybir.dt.uint32
+I32 = mybir.dt.int32
 U16 = mybir.dt.uint16
 U8 = mybir.dt.uint8
 E4M3 = mybir.dt.float8_e4m3fn_x4
@@ -22,6 +23,7 @@ ROW_PASSES = R // K_PASS
 SLOT_BLOCK = 128
 SLOT_BLOCKS = N // SLOT_BLOCK
 D_BLOCKS = D // P
+WINDOWS = 3
 
 
 def tile_attend_ghv_nce_kernel(tc, xT, wT, vT, wt, xm, offs, out):
@@ -74,9 +76,10 @@ def tile_attend_ghv_nce_kernel(tc, xT, wT, vT, wt, xm, offs, out):
         for g in range(ROW_PASSES):
             nc.sync.dma_start(out=m_raw[g][:], in_=m_rows[g])
 
-        windows = [keep.tile([P, T], F32, name="window%d" % b) for b in range(D_BLOCKS)]
-        for b in range(D_BLOCKS):
-            nc.vector.memset(windows[b][:], 0.0)
+        windows = [keep.tile([P, T], F32, name="window%d" % b) for b in range(WINDOWS)]
+        nc.gpsimd.memset(windows[0][:], 0.0)
+        for b in range(1, WINDOWS):
+            nc.vector.memset(windows[b][:].bitcast(I32), 0)
 
         x_q = [quantised("x%d" % g, K_PASS) for g in range(ROW_PASSES)]
         m_q = [quantised("m%d" % g, D) for g in range(ROW_PASSES)]
@@ -91,8 +94,8 @@ def tile_attend_ghv_nce_kernel(tc, xT, wT, vT, wt, xm, offs, out):
                 in_=x_raw[g][:].rearrange("p j (m t) -> p m j t", t=PACK))
             return grouped
 
-        def gather(picked, planes, j):
-            nc.vector.tensor_copy(picked[:, j, :], planes[j][:].indirect(offsets[:]))
+        def gather(picked, planes, j, lo=0, hi=N):
+            nc.vector.tensor_copy(picked[:, j, lo:hi], planes[j][:].indirect(offsets[:, lo // 16:hi // 16]))
 
         def slot_cols(s):
             return slice(s * SLOT_BLOCK, (s + 1) * SLOT_BLOCK)
@@ -114,14 +117,22 @@ def tile_attend_ghv_nce_kernel(tc, xT, wT, vT, wt, xm, offs, out):
         v_picked = keep.tile([P, PACK, N], F32, name="v_picked")
         gather(w_picked, w_planes, 0)
         quantise(x_q[0], whole, x_grouped[:], E4M3)
-        for j in range(1, PACK):
+        for j in range(1, PACK - 1):
             gather(w_picked, w_planes, j)
-        w_grouped = [None] * SLOT_BLOCKS
-        for s in range(SLOT_BLOCKS + 1):
-            if s < SLOT_BLOCKS:
-                w_grouped[s] = group_block("w", nc.vector.tensor_copy, w_picked, s)
-            if s > 0:
-                quantise(w_q, slot_cols(s - 1), w_grouped[s - 1][:], E4M3)
+
+        def last_plane(name, picked, planes, pair):
+            gather(picked, planes, PACK - 1, 0, N // 2)
+            first = group_block(name, nc.vector.tensor_copy, picked, 0)
+            second = group_block(name, nc.scalar.copy, picked, 1)
+            gather(picked, planes, PACK - 1, N // 2, N)
+            quantise(pair, slot_cols(0), first[:], E4M3)
+            return [first, second]
+
+        w_grouped = last_plane("w", w_picked, w_planes, w_q)
+        w_grouped.append(group_block("w", nc.vector.tensor_copy, w_picked, 2))
+        w_grouped.append(group_block("w", nc.scalar.copy, w_picked, 3))
+        for s in range(1, SLOT_BLOCKS):
+            quantise(w_q, slot_cols(s), w_grouped[s][:], E4M3)
 
         wt_quarter = keep.tile([P, ROW_PASSES, PACK], F32, name="wt_quarter")
         nc.vector.tensor_scalar(out=wt_quarter[:], in0=wt_raw[:], scalar1=-0.25, scalar2=None, op0=ALU.mult)
@@ -133,7 +144,7 @@ def tile_attend_ghv_nce_kernel(tc, xT, wT, vT, wt, xm, offs, out):
             bank = scores(g, s, w_q)
             th = ring.tile([P, SLOT_BLOCK, PACK], F32, name="th")
             nc.scalar.activation(out=th[:], in_=bank[:].rearrange("p t i -> p i t"), func=ACT.Tanh, scale=0.5)
-            sq = ring.tile([P, SLOT_BLOCK, PACK], F32, name="sq")
+            sq = keep.tile([P, SLOT_BLOCK, PACK], F32, name="sq%d_%d" % (g, s))
             nc.scalar.activation(out=sq[:], in_=th[:], func=ACT.Square)
             u = keep.tile([P, SLOT_BLOCK, PACK], F32, name="slope%d_%d" % (g, s))
             nc.vector.scalar_tensor_tensor(
@@ -142,53 +153,68 @@ def tile_attend_ghv_nce_kernel(tc, xT, wT, vT, wt, xm, offs, out):
                 op0=ALU.subtract, op1=ALU.mult)
             slope[g][s] = u
 
-        slope_unit(0, 0)
         quantise(x_q[1], whole, x_grouped[:], E4M3)
-        slope_unit(0, 1)
+        slope_unit(0, 0)
         gather(v_picked, v_planes, 0)
+        slope_unit(0, 1)
         slope_unit(0, 2)
-        slope_unit(0, 3)
         gather(v_picked, v_planes, 1)
+        slope_unit(0, 3)
         slope_unit(1, 0)
-        slope_unit(1, 1)
         gather(v_picked, v_planes, 2)
+        slope_unit(1, 1)
         slope_unit(1, 2)
+        v_grouped = last_plane("v", v_picked, v_planes, v_q)
+        v_grouped.append(group_block("v", nc.scalar.copy, v_picked, 2))
+        v_grouped.append(group_block("v", nc.scalar.copy, v_picked, 3))
         slope_unit(1, 3)
-        gather(v_picked, v_planes, 3)
 
-        v_grouped = [group_block("v", nc.vector.tensor_copy if s == 0 else nc.scalar.copy, v_picked, s)
-                     for s in range(SLOT_BLOCKS)]
-        m_grouped = []
-        for g in range(ROW_PASSES):
-            grouped = keep.tile([P, D * PACK], BF16, name="m_grouped%d" % g, align_bytes=64)
-            interleave(nc.scalar.copy, grouped[:], m_raw[g][:])
-            m_grouped.append(grouped)
+        def cast_m(g, lo, hi):
+            grouped = keep.tile([P, (hi - lo) * PACK], BF16, name="m_grouped%d_%d" % (g, lo), align_bytes=64)
+            interleave(nc.scalar.copy, grouped[:], m_raw[g][:, :, lo:hi])
+            return grouped
+
+        m_parts = [(0, P), (P, 2 * P), (2 * P, D)]
+        m_grouped = {}
+        for lo, hi in m_parts:
+            for g in range(ROW_PASSES):
+                m_grouped[g, lo] = cast_m(g, lo, hi)
+
+        def quantise_m(g, part):
+            lo, hi = m_parts[part]
+            quantise(m_q[g], slice(lo, hi), m_grouped[g, lo][:], E4M3)
 
         acc = [out_psum.tile([P, N], F32, name="acc%d" % b) for b in range(D_BLOCKS)]
+
+        def product(b, g):
+            mx(acc[b][:], m_q[g], slice(b * P, (b + 1) * P), g_q[g], whole, E5M2, g == 0, g == ROW_PASSES - 1)
+
         units = [(g, s) for g in range(ROW_PASSES) for s in range(SLOT_BLOCKS)]
-        quantise(v_q, slot_cols(0), v_grouped[0][:], E4M3)
         pending = None
         for g, s in units:
+            bank = scores(g, s, v_q)
             if g == 0 and s + 1 < SLOT_BLOCKS:
                 quantise(v_q, slot_cols(s + 1), v_grouped[s + 1][:], E4M3)
-            bank = scores(g, s, v_q)
             g_grouped = ring.tile([P, SLOT_BLOCK, PACK], BF16, name="g_grouped", align_bytes=64)
             nc.vector.tensor_tensor(out=g_grouped[:], in0=bank[:].rearrange("p t i -> p i t"),
                                     in1=slope[g][s][:], op=ALU.mult)
             if pending is not None:
                 quantise(g_q[pending[0]], slot_cols(pending[1]), pending[2][:].rearrange("p i t -> p (i t)"), E5M2)
-            if (g, s) == (1, 0):
-                quantise(m_q[0], whole, m_grouped[0][:], E4M3)
-                for b in range(D_BLOCKS):
-                    mx(acc[b][:], m_q[0], slice(b * P, (b + 1) * P), g_q[0], whole, E5M2, True, False)
-            if (g, s) == (1, 2):
-                quantise(m_q[1], whole, m_grouped[1][:], E4M3)
+            if (g, s) == (1, 1):
+                quantise_m(0, 0)
+                product(0, 0)
             pending = (g, s, g_grouped)
+        quantise_m(1, 0)
         quantise(g_q[pending[0]], slot_cols(pending[1]), pending[2][:].rearrange("p i t -> p (i t)"), E5M2)
 
         for b in range(D_BLOCKS):
-            mx(acc[b][:], m_q[1], slice(b * P, (b + 1) * P), g_q[1], whole, E5M2, False, True)
+            if b > 0:
+                product(b, 0)
+            product(b, 1)
+            if b + 1 < len(m_parts):
+                for g in range(ROW_PASSES):
+                    quantise_m(g, b + 1)
             dense = ring.tile([P, N], F32, name="dense")
             nc.scalar.copy(out=dense[:], in_=acc[b][:])
-            nc.vector.tensor_copy(windows[b][:].indirect(offsets[:]), dense[:])
-            nc.sync.dma_start(out=out[b * P:(b + 1) * P, :], in_=windows[b][:])
+            nc.vector.tensor_copy(windows[b % WINDOWS][:].indirect(offsets[:]), dense[:])
+            nc.sync.dma_start(out=out[b * P:(b + 1) * P, :], in_=windows[b % WINDOWS][:])

@@ -51,8 +51,8 @@ def tile_attend_ghv_nce_kernel(tc, xT, wT, vT, wt, xm, offs, out):
             )
 
         def interleave(copy, grouped, planes):
-            copy(out=grouped.rearrange("p (c i t) -> p c t i", i=4, t=PACK),
-                 in_=planes.rearrange("p t (c i) -> p c t i", i=4))
+            copy(out=grouped.rearrange("p (c i t) -> p c t i", i=2, t=PACK),
+                 in_=planes.rearrange("p t (c i) -> p c t i", i=2))
 
         offsets = keep.tile([P, N // 16], U16, name="offsets")
         x_raw = [keep.tile([P, PACK, K_PASS], F32, name="x_raw%d" % g) for g in range(ROW_PASSES)]
@@ -65,12 +65,13 @@ def tile_attend_ghv_nce_kernel(tc, xT, wT, vT, wt, xm, offs, out):
         v_rows = vT.rearrange("(p j) c -> p j c", j=PACK)
         m_rows = xm[0].rearrange("(g p t) d -> g p t d", p=P, t=PACK)
 
-        nc.sync.dma_start(out=x_raw[0][:], in_=x_rows[:, :, 0:K_PASS])
+        nc.scalar.dma_start(out=wt_raw[:], in_=wt[0].rearrange("(g p t) o -> p g (t o)", p=P, t=PACK))
+        nc.sync.dma_start(out=w_planes[0][:], in_=w_rows[:, 0, :])
         nc.sync.dma_start(offsets[:], offs)
-        for j in range(PACK):
+        for j in range(1, PACK):
             nc.sync.dma_start(out=w_planes[j][:], in_=w_rows[:, j, :])
-        nc.sync.dma_start(out=wt_raw[:], in_=wt[0].rearrange("(g p t) o -> p g (t o)", p=P, t=PACK))
-        nc.sync.dma_start(out=x_raw[1][:], in_=x_rows[:, :, K_PASS:R])
+        for g in range(ROW_PASSES):
+            nc.sync.dma_start(out=x_raw[g][:], in_=x_rows[:, :, g * K_PASS:(g + 1) * K_PASS])
         for j in range(PACK):
             nc.sync.dma_start(out=v_planes[j][:], in_=v_rows[:, j, :])
         for g in range(ROW_PASSES):
@@ -87,98 +88,92 @@ def tile_attend_ghv_nce_kernel(tc, xT, wT, vT, wt, xm, offs, out):
         w_q = quantised("w", N)
         v_q = quantised("v", N)
 
-        def cast_x(g):
-            grouped = keep.tile([P, K_PASS * PACK], BF16, name="x_grouped%d" % g, align_bytes=64)
-            nc.vector.tensor_copy(
-                out=grouped[:].rearrange("p (t m j) -> p m j t", t=PACK, j=PACK),
-                in_=x_raw[g][:].rearrange("p j (m t) -> p m j t", t=PACK))
+        def cast_x(copy, g, h):
+            grouped = keep.tile([P, 2 * P * PACK], BF16, name="x_grouped%d_%d" % (g, h), align_bytes=64)
+            copy(out=grouped[:].rearrange("p (t m j) -> p m j t", t=2, j=PACK),
+                 in_=x_raw[g][:].rearrange("p j (m t) -> p m j t", t=PACK)[:, :, :, 2 * h:2 * h + 2])
             return grouped
+
+        def quantise_x(g, h, grouped):
+            quantise(x_q[g], slice(2 * h * P, (2 * h + 2) * P), grouped[:], E4M3)
 
         def gather(picked, planes, j, lo=0, hi=N):
             nc.vector.tensor_copy(picked[:, j, lo:hi], planes[j][:].indirect(offsets[:, lo // 16:hi // 16]))
 
-        def slot_cols(s):
-            return slice(s * SLOT_BLOCK, (s + 1) * SLOT_BLOCK)
-
-        def group_block(name, copy, picked, s):
-            grouped = keep.tile([P, SLOT_BLOCK * PACK], BF16, name="%s_grouped%d" % (name, s), align_bytes=64)
-            interleave(copy, grouped[:], picked[:, :, slot_cols(s)])
+        def group(name, copy, picked, lo, hi):
+            grouped = keep.tile([P, (hi - lo) * PACK], BF16, name="%s_grouped%d" % (name, lo), align_bytes=64)
+            interleave(copy, grouped[:], picked[:, :, lo:hi])
             return grouped
-
-        def scores(g, s, table_q):
-            bank = unit_psum.tile([P, PACK, SLOT_BLOCK], F32, name="bank")
-            for t in range(PACK):
-                mx(bank[:, t, :], x_q[g], slice(t * P, (t + 1) * P), table_q, slot_cols(s), E4M3, True, True)
-            return bank
 
         whole = slice(0, K_PASS)
-        x_grouped = cast_x(0)
-        w_picked = keep.tile([P, PACK, N], F32, name="w_picked")
-        v_picked = keep.tile([P, PACK, N], F32, name="v_picked")
-        gather(w_picked, w_planes, 0)
-        quantise(x_q[0], whole, x_grouped[:], E4M3)
-        for j in range(1, PACK - 1):
-            gather(w_picked, w_planes, j)
-
-        def last_plane(name, picked, planes, pair):
-            gather(picked, planes, PACK - 1, 0, N // 2)
-            first = group_block(name, nc.vector.tensor_copy, picked, 0)
-            second = group_block(name, nc.scalar.copy, picked, 1)
-            gather(picked, planes, PACK - 1, N // 2, N)
-            quantise(pair, slot_cols(0), first[:], E4M3)
-            return [first, second]
-
-        w_grouped = last_plane("w", w_picked, w_planes, w_q)
-        w_grouped.append(group_block("w", nc.vector.tensor_copy, w_picked, 2))
-        w_grouped.append(group_block("w", nc.scalar.copy, w_picked, 3))
-        for s in range(1, SLOT_BLOCKS):
-            quantise(w_q, slot_cols(s), w_grouped[s][:], E4M3)
-
+        half = N // 2
         wt_quarter = keep.tile([P, ROW_PASSES, PACK], F32, name="wt_quarter")
         nc.vector.tensor_scalar(out=wt_quarter[:], in0=wt_raw[:], scalar1=-0.25, scalar2=None, op0=ALU.mult)
-        x_grouped = cast_x(1)
+        w_picked = keep.tile([P, PACK, N], F32, name="w_picked")
+        v_picked = keep.tile([P, PACK, N], F32, name="v_picked")
+        for j in range(PACK - 1):
+            gather(w_picked, w_planes, j)
+        gather(w_picked, w_planes, PACK - 1, 0, half)
+        w_low = group("w", nc.scalar.copy, w_picked, 0, half)
+        gather(w_picked, w_planes, PACK - 1, half, N)
+        w_high = group("w", nc.vector.tensor_copy, w_picked, half, N)
+        quantise(w_q, slice(0, half), w_low[:], E4M3)
+        quantise(w_q, slice(half, N), w_high[:], E4M3)
 
-        slope = [[None] * SLOT_BLOCKS for g in range(ROW_PASSES)]
 
-        def slope_unit(g, s):
-            bank = scores(g, s, w_q)
-            th = ring.tile([P, SLOT_BLOCK, PACK], F32, name="th")
-            nc.scalar.activation(out=th[:], in_=bank[:].rearrange("p t i -> p i t"), func=ACT.Tanh, scale=0.5)
-            sq = keep.tile([P, SLOT_BLOCK, PACK], F32, name="sq%d_%d" % (g, s))
-            nc.scalar.activation(out=sq[:], in_=th[:], func=ACT.Square)
-            u = keep.tile([P, SLOT_BLOCK, PACK], F32, name="slope%d_%d" % (g, s))
-            nc.vector.scalar_tensor_tensor(
-                out=u[:], in0=sq[:], scalar=1.0,
-                in1=wt_quarter[:, g:g + 1, :].to_broadcast([P, SLOT_BLOCK, PACK]),
-                op0=ALU.subtract, op1=ALU.mult)
-            slope[g][s] = u
+        tanh_half = [keep.tile([P, PACK, N], F32, name="tanh_half%d" % g) for g in range(ROW_PASSES)]
+        squared = {}
+        slope = {}
 
-        quantise(x_q[1], whole, x_grouped[:], E4M3)
-        slope_unit(0, 0)
-        gather(v_picked, v_planes, 0)
-        slope_unit(0, 1)
-        slope_unit(0, 2)
-        gather(v_picked, v_planes, 1)
-        slope_unit(0, 3)
-        slope_unit(1, 0)
-        gather(v_picked, v_planes, 2)
-        slope_unit(1, 1)
-        slope_unit(1, 2)
-        v_grouped = last_plane("v", v_picked, v_planes, v_q)
-        v_grouped.append(group_block("v", nc.scalar.copy, v_picked, 2))
-        v_grouped.append(group_block("v", nc.scalar.copy, v_picked, 3))
-        slope_unit(1, 3)
+        def slope_start(g, t):
+            bank = unit_psum.tile([P, N], F32, name="bank")
+            mx(bank[:], x_q[g], slice(t * P, (t + 1) * P), w_q, whole, E4M3, True, True)
+            nc.scalar.activation(out=tanh_half[g][:, t, :], in_=bank[:], func=ACT.Tanh, scale=0.5)
 
-        def cast_m(g, lo, hi):
-            grouped = keep.tile([P, (hi - lo) * PACK], BF16, name="m_grouped%d_%d" % (g, lo), align_bytes=64)
-            interleave(nc.scalar.copy, grouped[:], m_raw[g][:, :, lo:hi])
-            return grouped
+        def square(g, h):
+            squared[g, h] = keep.tile([P, 2, N], F32, name="w_plane%d" % (2 * g + h))
+            nc.scalar.activation(out=squared[g, h][:], in_=tanh_half[g][:, 2 * h:2 * h + 2, :], func=ACT.Square)
+
+        def slope_finish(g, h):
+            for t in (2 * h, 2 * h + 1):
+                nc.vector.tensor_scalar(out=slope[g][:, t, :], in0=squared[g, h][:, t - 2 * h, :], scalar1=1.0,
+                                        scalar2=wt_quarter[:, g, t:t + 1], op0=ALU.subtract, op1=ALU.mult)
+
+        x_low = cast_x(nc.vector.tensor_copy, 0, 0)
+        x_high = cast_x(nc.scalar.copy, 0, 1)
+        quantise_x(0, 0, x_low)
+        quantise_x(0, 1, x_high)
+        x_low = cast_x(nc.vector.tensor_copy, 1, 0)
+        x_high = cast_x(nc.vector.tensor_copy, 1, 1)
+        quantise_x(1, 0, x_low)
+        quantise_x(1, 1, x_high)
+        for t in range(3):
+            slope_start(0, t)
+        slope[0] = tanh_half[0]
+        square(0, 0)
+        slope_finish(0, 0)
+        slope_start(0, 3)
+        slope_start(1, 0)
+        square(0, 1)
+        slope_finish(0, 1)
+        slope_start(1, 1)
+        slope_start(1, 2)
+        square(1, 0)
+        slope_start(1, 3)
+        square(1, 1)
+        for j in range(PACK - 1):
+            gather(v_picked, v_planes, j)
+        gather(v_picked, v_planes, PACK - 1, 0, half)
+        v_grouped = [group("v", nc.vector.tensor_copy, v_picked, 0, SLOT_BLOCK),
+                     group("v", nc.scalar.copy, v_picked, SLOT_BLOCK, half)]
+        gather(v_picked, v_planes, PACK - 1, half, N)
+        v_grouped += [group("v", nc.scalar.copy, v_picked, s * SLOT_BLOCK, (s + 1) * SLOT_BLOCK) for s in (2, 3)]
 
         m_parts = [(0, P), (P, 2 * P), (2 * P, D)]
         m_grouped = {}
         for lo, hi in m_parts:
             for g in range(ROW_PASSES):
-                m_grouped[g, lo] = cast_m(g, lo, hi)
+                m_grouped[g, lo] = group("m%d" % g, nc.scalar.copy, m_raw[g], lo, hi)
 
         def quantise_m(g, part):
             lo, hi = m_parts[part]
@@ -189,23 +184,45 @@ def tile_attend_ghv_nce_kernel(tc, xT, wT, vT, wt, xm, offs, out):
         def product(b, g):
             mx(acc[b][:], m_q[g], slice(b * P, (b + 1) * P), g_q[g], whole, E5M2, g == 0, g == ROW_PASSES - 1)
 
-        units = [(g, s) for g in range(ROW_PASSES) for s in range(SLOT_BLOCKS)]
-        pending = None
-        for g, s in units:
-            bank = scores(g, s, v_q)
-            if g == 0 and s + 1 < SLOT_BLOCKS:
+        def slot_cols(s):
+            return slice(s * SLOT_BLOCK, (s + 1) * SLOT_BLOCK)
+
+        g_grouped = [keep.tile([P, N * PACK], BF16, name="g_grouped%d" % g, align_bytes=64) for g in range(ROW_PASSES)]
+
+        def gradient_unit(g, s):
+            bank = unit_psum.tile([P, PACK, SLOT_BLOCK], F32, name="bank")
+            for t in range(PACK):
+                mx(bank[:, t, :], x_q[g], slice(t * P, (t + 1) * P), v_q, slot_cols(s), E4M3, True, True)
+            nc.vector.tensor_tensor(
+                out=g_grouped[g][:, s * SLOT_BLOCK * PACK:(s + 1) * SLOT_BLOCK * PACK].rearrange(
+                    "p (c i t) -> p c t i", i=2, t=PACK),
+                in0=bank[:].rearrange("p t (c i) -> p c t i", i=2),
+                in1=slope[g][:, :, slot_cols(s)].rearrange("p t (c i) -> p c t i", i=2),
+                op=ALU.mult)
+
+        def quantise_g(g, lo, hi):
+            quantise(g_q[g], slice(lo * SLOT_BLOCK, hi * SLOT_BLOCK),
+                     g_grouped[g][:, lo * SLOT_BLOCK * PACK:hi * SLOT_BLOCK * PACK], E5M2)
+
+        quantise(v_q, slot_cols(0), v_grouped[0][:], E4M3)
+        slope[1] = keep.tile([P, PACK, N], F32, name="v_plane%d" % (PACK - 1))
+        slope_finish(1, 0)
+        for s in range(SLOT_BLOCKS):
+            if s + 1 < SLOT_BLOCKS:
                 quantise(v_q, slot_cols(s + 1), v_grouped[s + 1][:], E4M3)
-            g_grouped = ring.tile([P, SLOT_BLOCK, PACK], BF16, name="g_grouped", align_bytes=64)
-            nc.vector.tensor_tensor(out=g_grouped[:], in0=bank[:].rearrange("p t i -> p i t"),
-                                    in1=slope[g][s][:], op=ALU.mult)
-            if pending is not None:
-                quantise(g_q[pending[0]], slot_cols(pending[1]), pending[2][:].rearrange("p i t -> p (i t)"), E5M2)
-            if (g, s) == (1, 1):
-                quantise_m(0, 0)
-                product(0, 0)
-            pending = (g, s, g_grouped)
+            gradient_unit(0, s)
+        slope_finish(1, 1)
+        gradient_unit(1, 0)
+        quantise_g(0, 0, 4)
+        gradient_unit(1, 1)
+        quantise_m(0, 0)
+        product(0, 0)
+        gradient_unit(1, 2)
+        quantise_g(1, 0, 2)
+        gradient_unit(1, 3)
+        quantise_g(1, 2, 3)
         quantise_m(1, 0)
-        quantise(g_q[pending[0]], slot_cols(pending[1]), pending[2][:].rearrange("p i t -> p (i t)"), E5M2)
+        quantise_g(1, 3, 4)
 
         for b in range(D_BLOCKS):
             if b > 0:
@@ -215,6 +232,8 @@ def tile_attend_ghv_nce_kernel(tc, xT, wT, vT, wt, xm, offs, out):
                 for g in range(ROW_PASSES):
                     quantise_m(g, b + 1)
             dense = ring.tile([P, N], F32, name="dense")
-            nc.scalar.copy(out=dense[:], in_=acc[b][:])
-            nc.vector.tensor_copy(windows[b % WINDOWS][:].indirect(offsets[:]), dense[:])
-            nc.sync.dma_start(out=out[b * P:(b + 1) * P, :], in_=windows[b % WINDOWS][:])
+            window = windows[b % WINDOWS]
+            for lo, hi in ([(0, half), (half, N)] if b == 0 else [(0, N)]):
+                nc.scalar.copy(out=dense[:, lo:hi], in_=acc[b][:, lo:hi])
+                nc.vector.tensor_copy(window[:].indirect(offsets[:, lo // 16:hi // 16]), dense[:, lo:hi])
+            nc.sync.dma_start(out=out[b * P:(b + 1) * P, :], in_=window[:])

@@ -23,7 +23,7 @@ ROW_PASSES = R // K_PASS
 SLOT_BLOCK = 128
 SLOT_BLOCKS = N // SLOT_BLOCK
 D_BLOCKS = D // P
-WINDOWS = 3
+WINDOWS = 4
 
 
 def tile_attend_ghv_nce_kernel(tc, xT, wT, vT, wt, xm, offs, out):
@@ -78,9 +78,9 @@ def tile_attend_ghv_nce_kernel(tc, xT, wT, vT, wt, xm, offs, out):
             nc.sync.dma_start(out=m_raw[g][:], in_=m_rows[g])
 
         windows = [keep.tile([P, T], F32, name="window%d" % b) for b in range(WINDOWS)]
-        nc.gpsimd.memset(windows[0][:], 0.0)
-        for b in range(1, WINDOWS):
-            nc.vector.memset(windows[b][:].bitcast(I32), 0)
+        for b in range(WINDOWS):
+            engine = nc.gpsimd if b % 2 else nc.vector
+            engine.memset(windows[b][:].bitcast(I32), 0)
 
         x_q = [quantised("x%d" % g, K_PASS) for g in range(ROW_PASSES)]
         m_q = [quantised("m%d" % g, D) for g in range(ROW_PASSES)]
@@ -107,8 +107,6 @@ def tile_attend_ghv_nce_kernel(tc, xT, wT, vT, wt, xm, offs, out):
 
         whole = slice(0, K_PASS)
         half = N // 2
-        wt_quarter = keep.tile([P, ROW_PASSES, PACK], F32, name="wt_quarter")
-        nc.vector.tensor_scalar(out=wt_quarter[:], in0=wt_raw[:], scalar1=-0.25, scalar2=None, op0=ALU.mult)
         w_picked = keep.tile([P, PACK, N], F32, name="w_picked")
         v_picked = keep.tile([P, PACK, N], F32, name="v_picked")
         for j in range(PACK - 1):
@@ -132,12 +130,19 @@ def tile_attend_ghv_nce_kernel(tc, xT, wT, vT, wt, xm, offs, out):
 
         def square(g, h):
             squared[g, h] = keep.tile([P, 2, N], F32, name="w_plane%d" % (2 * g + h))
-            nc.scalar.activation(out=squared[g, h][:], in_=tanh_half[g][:, 2 * h:2 * h + 2, :], func=ACT.Square)
+            pair = tanh_half[g][:, 2 * h:2 * h + 2, :]
+            if (g, h) == (0, 0):
+                nc.vector.tensor_tensor(out=squared[g, h][:], in0=pair, in1=pair, op=ALU.mult)
+            else:
+                nc.scalar.activation(out=squared[g, h][:], in_=pair, func=ACT.Square)
 
-        def slope_finish(g, h):
-            for t in (2 * h, 2 * h + 1):
-                nc.vector.tensor_scalar(out=slope[g][:, t, :], in0=squared[g, h][:, t - 2 * h, :], scalar1=1.0,
-                                        scalar2=wt_quarter[:, g, t:t + 1], op0=ALU.subtract, op1=ALU.mult)
+        def slope_finish(g, h, slot):
+            wt_quarter = keep.tile([P, 2], F32, name=slot)
+            nc.vector.tensor_scalar(out=wt_quarter[:], in0=wt_raw[:, g, 2 * h:2 * h + 2], scalar1=-0.25, scalar2=None,
+                                    op0=ALU.mult)
+            for e in range(2):
+                nc.vector.tensor_scalar(out=slope[g][:, 2 * h + e, :], in0=squared[g, h][:, e, :], scalar1=1.0,
+                                        scalar2=wt_quarter[:, e:e + 1], op0=ALU.subtract, op1=ALU.mult)
 
         x_low = cast_x(nc.vector.tensor_copy, 0, 0)
         x_high = cast_x(nc.scalar.copy, 0, 1)
@@ -151,11 +156,11 @@ def tile_attend_ghv_nce_kernel(tc, xT, wT, vT, wt, xm, offs, out):
             slope_start(0, t)
         slope[0] = tanh_half[0]
         square(0, 0)
-        slope_finish(0, 0)
+        slope_finish(0, 0, "wt_quarter0")
         slope_start(0, 3)
         slope_start(1, 0)
         square(0, 1)
-        slope_finish(0, 1)
+        slope_finish(0, 1, "wt_quarter1")
         slope_start(1, 1)
         slope_start(1, 2)
         square(1, 0)
@@ -163,6 +168,8 @@ def tile_attend_ghv_nce_kernel(tc, xT, wT, vT, wt, xm, offs, out):
         square(1, 1)
         for j in range(PACK - 1):
             gather(v_picked, v_planes, j)
+        slope[1] = keep.tile([P, PACK, N], F32, name="v_plane2")
+        slope_finish(1, 0, "wt_quarter2")
         gather(v_picked, v_planes, PACK - 1, 0, half)
         v_grouped = [group("v", nc.vector.tensor_copy, v_picked, 0, SLOT_BLOCK),
                      group("v", nc.scalar.copy, v_picked, SLOT_BLOCK, half)]
@@ -205,13 +212,11 @@ def tile_attend_ghv_nce_kernel(tc, xT, wT, vT, wt, xm, offs, out):
                      g_grouped[g][:, lo * SLOT_BLOCK * PACK:hi * SLOT_BLOCK * PACK], E5M2)
 
         quantise(v_q, slot_cols(0), v_grouped[0][:], E4M3)
-        slope[1] = keep.tile([P, PACK, N], F32, name="v_plane%d" % (PACK - 1))
-        slope_finish(1, 0)
+        slope_finish(1, 1, "v_plane3")
         for s in range(SLOT_BLOCKS):
             if s + 1 < SLOT_BLOCKS:
                 quantise(v_q, slot_cols(s + 1), v_grouped[s + 1][:], E4M3)
             gradient_unit(0, s)
-        slope_finish(1, 1)
         gradient_unit(1, 0)
         quantise_g(0, 0, 4)
         gradient_unit(1, 1)

@@ -83,7 +83,7 @@ def tile_attend_ghv_nce_kernel(tc, xT, wT, vT, wt, xm, offs, out):
             engine.memset(windows[b][:].bitcast(I32), 0)
 
         x_q = [quantised("x%d" % g, K_PASS) for g in range(ROW_PASSES)]
-        m_q = [quantised("m%d" % g, D) for g in range(ROW_PASSES)]
+        m_q = quantised("m", ROW_PASSES * D)
         g_q = [quantised("g%d" % g, N) for g in range(ROW_PASSES)]
         w_q = quantised("w", N)
         v_q = quantised("v", N)
@@ -170,42 +170,67 @@ def tile_attend_ghv_nce_kernel(tc, xT, wT, vT, wt, xm, offs, out):
             gather(v_picked, v_planes, j)
         slope[1] = keep.tile([P, PACK, N], F32, name="v_plane2")
         slope_finish(1, 0, "wt_quarter2")
+        def slot_cols(s):
+            return slice(s * SLOT_BLOCK, (s + 1) * SLOT_BLOCK)
+
+        def group_v(copy, s):
+            return group("v", copy, v_picked, s * SLOT_BLOCK, (s + 1) * SLOT_BLOCK)
+
         gather(v_picked, v_planes, PACK - 1, 0, half)
-        v_grouped = [group("v", nc.vector.tensor_copy, v_picked, 0, SLOT_BLOCK),
-                     group("v", nc.scalar.copy, v_picked, SLOT_BLOCK, half)]
+        v_grouped = [group_v(nc.vector.tensor_copy, 0), group_v(nc.scalar.copy, 1)]
         gather(v_picked, v_planes, PACK - 1, half, N)
-        v_grouped += [group("v", nc.scalar.copy, v_picked, s * SLOT_BLOCK, (s + 1) * SLOT_BLOCK) for s in (2, 3)]
+        v_upper = keep.tile([P, 2, SLOT_BLOCK * PACK], BF16, name="v_upper", align_bytes=64)
+        for e in range(2):
+            interleave(nc.scalar.copy, v_upper[:, e, :], v_picked[:, :, slot_cols(2 + e)])
 
-        m_parts = [(0, P), (P, 2 * P), (2 * P, D)]
+        m_parts = [(0, 1), (1, 2), (2, D_BLOCKS)]
         m_grouped = {}
-        for lo, hi in m_parts:
-            for g in range(ROW_PASSES):
-                m_grouped[g, lo] = group("m%d" % g, nc.scalar.copy, m_raw[g], lo, hi)
 
-        def quantise_m(g, part):
+        def group_m(part, g):
             lo, hi = m_parts[part]
-            quantise(m_q[g], slice(lo, hi), m_grouped[g, lo][:], E4M3)
+            if part not in m_grouped:
+                m_grouped[part] = keep.tile([P, hi - lo, ROW_PASSES, P * PACK], BF16, name="m_grouped%d" % part,
+                                            align_bytes=64)
+            for b in range(lo, hi):
+                interleave(nc.scalar.copy, m_grouped[part][:, b - lo, g, :], m_raw[g][:, :, b * P:(b + 1) * P])
+
+        def quantise_m(part):
+            lo, hi = m_parts[part]
+            quantise(m_q, slice(lo * ROW_PASSES * P, hi * ROW_PASSES * P),
+                     m_grouped[part][:].rearrange("p b g c -> p (b g c)"), E4M3)
 
         acc = [out_psum.tile([P, N], F32, name="acc%d" % b) for b in range(D_BLOCKS)]
 
         def product(b, g):
-            mx(acc[b][:], m_q[g], slice(b * P, (b + 1) * P), g_q[g], whole, E5M2, g == 0, g == ROW_PASSES - 1)
+            first = (b * ROW_PASSES + g) * P
+            mx(acc[b][:], m_q, slice(first, first + P), g_q[g], whole, E5M2, g == 0, g == ROW_PASSES - 1)
 
-        def slot_cols(s):
-            return slice(s * SLOT_BLOCK, (s + 1) * SLOT_BLOCK)
-
-        g_grouped = [keep.tile([P, N * PACK], BF16, name="g_grouped%d" % g, align_bytes=64) for g in range(ROW_PASSES)]
-
-        def gradient_unit(g, s):
+        def scores(g, s):
             bank = unit_psum.tile([P, PACK, SLOT_BLOCK], F32, name="bank")
             for t in range(PACK):
                 mx(bank[:, t, :], x_q[g], slice(t * P, (t + 1) * P), v_q, slot_cols(s), E4M3, True, True)
+            return bank
+
+        g_grouped = [keep.tile([P, N * PACK], BF16, name="g_grouped%d" % g, align_bytes=64) for g in range(ROW_PASSES)]
+
+        def g_cols(g, s):
+            return g_grouped[g][:, s * SLOT_BLOCK * PACK:(s + 1) * SLOT_BLOCK * PACK]
+
+        def gradient_unit(g, s):
+            bank = scores(g, s)
             nc.vector.tensor_tensor(
-                out=g_grouped[g][:, s * SLOT_BLOCK * PACK:(s + 1) * SLOT_BLOCK * PACK].rearrange(
-                    "p (c i t) -> p c t i", i=2, t=PACK),
+                out=g_cols(g, s).rearrange("p (c i t) -> p c t i", i=2, t=PACK),
                 in0=bank[:].rearrange("p t (c i) -> p c t i", i=2),
                 in1=slope[g][:, :, slot_cols(s)].rearrange("p t (c i) -> p c t i", i=2),
                 op=ALU.mult)
+
+        def gradient_unit_gpsimd(g, s):
+            bank = scores(g, s)
+            av = keep.tile([P, SLOT_BLOCK, PACK], F32, name="av%d_%d" % (g, s))
+            nc.scalar.copy(out=av[:], in_=bank[:].rearrange("p t c -> p c t"))
+            nc.gpsimd.tensor_tensor(
+                out=g_cols(g, s).rearrange("p (c t) -> p c t", t=PACK),
+                in0=av[:], in1=slope[g][:, :, slot_cols(s)].rearrange("p t c -> p c t"), op=ALU.mult)
 
         def quantise_g(g, lo, hi):
             quantise(g_q[g], slice(lo * SLOT_BLOCK, hi * SLOT_BLOCK),
@@ -213,29 +238,33 @@ def tile_attend_ghv_nce_kernel(tc, xT, wT, vT, wt, xm, offs, out):
 
         quantise(v_q, slot_cols(0), v_grouped[0][:], E4M3)
         slope_finish(1, 1, "v_plane3")
-        for s in range(SLOT_BLOCKS):
-            if s + 1 < SLOT_BLOCKS:
-                quantise(v_q, slot_cols(s + 1), v_grouped[s + 1][:], E4M3)
-            gradient_unit(0, s)
-        gradient_unit(1, 0)
-        quantise_g(0, 0, 4)
-        gradient_unit(1, 1)
-        quantise_m(0, 0)
-        product(0, 0)
+        quantise(v_q, slot_cols(1), v_grouped[1][:], E4M3)
+        gradient_unit(0, 0)
+        gradient_unit_gpsimd(1, 0)
+        quantise(v_q, slice(half, N), v_upper[:].rearrange("p e c -> p (e c)"), E4M3)
+        gradient_unit(0, 1)
+        gradient_unit_gpsimd(1, 1)
+        group_m(0, 0)
+        group_m(0, 1)
+        gradient_unit(0, 2)
+        gradient_unit(0, 3)
         gradient_unit(1, 2)
-        quantise_g(1, 0, 2)
+        quantise_g(0, 0, 4)
+        quantise_m(0)
         gradient_unit(1, 3)
-        quantise_g(1, 2, 3)
-        quantise_m(1, 0)
-        quantise_g(1, 3, 4)
+        product(0, 0)
+        quantise_g(1, 0, 2)
+        quantise_g(1, 2, 4)
+        for part in range(1, len(m_parts)):
+            for g in range(ROW_PASSES):
+                group_m(part, g)
 
         for b in range(D_BLOCKS):
             if b > 0:
                 product(b, 0)
             product(b, 1)
             if b + 1 < len(m_parts):
-                for g in range(ROW_PASSES):
-                    quantise_m(g, b + 1)
+                quantise_m(b + 1)
             dense = ring.tile([P, N], F32, name="dense")
             window = windows[b % WINDOWS]
             for lo, hi in ([(0, half), (half, N)] if b == 0 else [(0, N)]):

@@ -50,22 +50,23 @@ def tile_attend_ghv_nce_kernel(tc, xT, wT, vT, wt, xm, offs, out):
                 start=start, stop=stop,
             )
 
-        def interleave(copy, grouped, planes):
-            copy(out=grouped.rearrange("p (c i t) -> p c t i", i=2, t=PACK),
-                 in_=planes.rearrange("p t (c i) -> p c t i", i=2))
+        def interleave(copy, grouped, planes, run=2):
+            copy(out=grouped.rearrange("p (c i t) -> p c t i", i=run, t=PACK),
+                 in_=planes.rearrange("p t (c i) -> p c t i", i=run))
 
         offsets = keep.tile([P, N // 16], U16, name="offsets")
         x_raw = [keep.tile([P, PACK, K_PASS], F32, name="x_raw%d" % g) for g in range(ROW_PASSES)]
         m_raw = [keep.tile([P, PACK, D], F32, name="m_raw%d" % g) for g in range(ROW_PASSES)]
         w_planes = [keep.tile([P, T], F32, name="w_plane%d" % j) for j in range(PACK)]
         v_planes = [keep.tile([P, T], F32, name="v_plane%d" % j) for j in range(PACK)]
-        wt_raw = keep.tile([P, ROW_PASSES, PACK], F32, name="wt_raw")
+        wt_padded = keep.tile([P, ROW_PASSES, 2 * PACK], F32, name="wt_padded")
+        wt_raw = wt_padded[:, :, 0:PACK]
         x_rows = xT[0].rearrange("(p j) r -> p j r", j=PACK)
         w_rows = wT.rearrange("(p j) c -> p j c", j=PACK)
         v_rows = vT.rearrange("(p j) c -> p j c", j=PACK)
         m_rows = xm[0].rearrange("(g p t) d -> g p t d", p=P, t=PACK)
 
-        nc.scalar.dma_start(out=wt_raw[:], in_=wt[0].rearrange("(g p t) o -> p g (t o)", p=P, t=PACK))
+        nc.scalar.dma_start(out=wt_raw, in_=wt[0].rearrange("(g p t) o -> p g (t o)", p=P, t=PACK))
         nc.sync.dma_start(out=w_planes[0][:], in_=w_rows[:, 0, :])
         nc.sync.dma_start(offsets[:], offs)
         for j in range(1, PACK):
@@ -100,24 +101,20 @@ def tile_attend_ghv_nce_kernel(tc, xT, wT, vT, wt, xm, offs, out):
         def gather(picked, planes, j, lo=0, hi=N):
             nc.vector.tensor_copy(picked[:, j, lo:hi], planes[j][:].indirect(offsets[:, lo // 16:hi // 16]))
 
-        def group(name, copy, picked, lo, hi):
-            grouped = keep.tile([P, (hi - lo) * PACK], BF16, name="%s_grouped%d" % (name, lo), align_bytes=64)
-            interleave(copy, grouped[:], picked[:, :, lo:hi])
-            return grouped
-
         whole = slice(0, K_PASS)
         half = N // 2
-        w_picked = keep.tile([P, PACK, N], F32, name="w_picked")
         v_picked = keep.tile([P, PACK, N], F32, name="v_picked")
+        w_picked = keep.tile([P, PACK, N], F32, name="w_picked")
+        w_grouped = [keep.tile([P, half * PACK], BF16, name="w_grouped%d" % h, align_bytes=64) for h in range(2)]
         for j in range(PACK - 1):
             gather(w_picked, w_planes, j)
         gather(w_picked, w_planes, PACK - 1, 0, half)
-        w_low = group("w", nc.scalar.copy, w_picked, 0, half)
+        interleave(nc.scalar.copy, w_grouped[0][:], w_picked[:, :, 0:half])
         gather(w_picked, w_planes, PACK - 1, half, N)
-        w_high = group("w", nc.vector.tensor_copy, w_picked, half, N)
-        quantise(w_q, slice(0, half), w_low[:], E4M3)
-        quantise(w_q, slice(half, N), w_high[:], E4M3)
+        interleave(nc.vector.tensor_copy, w_grouped[1][:], w_picked[:, :, half:N])
 
+        def quantise_w(h):
+            quantise(w_q, slice(h * half, (h + 1) * half), w_grouped[h][:], E4M3)
 
         tanh_half = [keep.tile([P, PACK, N], F32, name="tanh_half%d" % g) for g in range(ROW_PASSES)]
         squared = {}
@@ -128,60 +125,69 @@ def tile_attend_ghv_nce_kernel(tc, xT, wT, vT, wt, xm, offs, out):
             mx(bank[:], x_q[g], slice(t * P, (t + 1) * P), w_q, whole, E4M3, True, True)
             nc.scalar.activation(out=tanh_half[g][:, t, :], in_=bank[:], func=ACT.Tanh, scale=0.5)
 
-        def square(g, h):
-            squared[g, h] = keep.tile([P, 2, N], F32, name="w_plane%d" % (2 * g + h))
-            pair = tanh_half[g][:, 2 * h:2 * h + 2, :]
-            if (g, h) == (0, 0):
-                nc.vector.tensor_tensor(out=squared[g, h][:], in0=pair, in1=pair, op=ALU.mult)
+        def square(g, lo, hi, slot):
+            tile = keep.tile([P, hi - lo, N], F32, name=slot)
+            planes = tanh_half[g][:, lo:hi, :]
+            if (g, lo) == (0, 0):
+                nc.vector.tensor_tensor(out=tile[:], in0=planes, in1=planes, op=ALU.mult)
             else:
-                nc.scalar.activation(out=squared[g, h][:], in_=pair, func=ACT.Square)
+                nc.scalar.activation(out=tile[:], in_=planes, func=ACT.Square)
+            for t in range(lo, hi):
+                squared[g, t] = tile[:, t - lo, :]
 
-        def slope_finish(g, h, slot):
-            wt_quarter = keep.tile([P, 2], F32, name=slot)
-            nc.vector.tensor_scalar(out=wt_quarter[:], in0=wt_raw[:, g, 2 * h:2 * h + 2], scalar1=-0.25, scalar2=None,
-                                    op0=ALU.mult)
-            for e in range(2):
-                nc.vector.tensor_scalar(out=slope[g][:, 2 * h + e, :], in0=squared[g, h][:, e, :], scalar1=1.0,
-                                        scalar2=wt_quarter[:, e:e + 1], op0=ALU.subtract, op1=ALU.mult)
+        def slope_finish(g, t):
+            nc.vector.tensor_scalar(out=slope[g][:, t, :], in0=squared[g, t], scalar1=1.0,
+                                    scalar2=wt_quarter[:, g, t:t + 1], op0=ALU.subtract, op1=ALU.mult)
 
+        def slope_finish_scalar(g, t):
+            nc.scalar.activation(out=slope[g][:, t, :], in_=squared[g, t], func=ACT.Identity,
+                                 scale=wt_quarter[:, g, t:t + 1], bias=wt_peak[:, g, t:t + 1])
+
+        wt_peak = keep.tile([P, ROW_PASSES, PACK], F32, name="wt_peak")
+        nc.vector.tensor_scalar(out=wt_peak[:], in0=wt_raw, scalar1=0.25, scalar2=None, op0=ALU.mult)
+        wt_quarter = keep.tile([P, ROW_PASSES, PACK], F32, name="wt_quarter")
+        nc.vector.tensor_scalar(out=wt_quarter[:], in0=wt_raw, scalar1=-0.25, scalar2=None, op0=ALU.mult)
+        quantise_w(0)
         x_low = cast_x(nc.vector.tensor_copy, 0, 0)
         x_high = cast_x(nc.scalar.copy, 0, 1)
+        quantise_w(1)
         quantise_x(0, 0, x_low)
         quantise_x(0, 1, x_high)
         x_low = cast_x(nc.vector.tensor_copy, 1, 0)
         x_high = cast_x(nc.vector.tensor_copy, 1, 1)
         quantise_x(1, 0, x_low)
         quantise_x(1, 1, x_high)
-        for t in range(3):
-            slope_start(0, t)
         slope[0] = tanh_half[0]
-        square(0, 0)
-        slope_finish(0, 0, "wt_quarter0")
-        slope_start(0, 3)
+        for t in range(PACK):
+            slope_start(0, t)
+        square(0, 0, 2, "w_plane0")
         slope_start(1, 0)
-        square(0, 1)
-        slope_finish(0, 1, "wt_quarter1")
-        slope_start(1, 1)
-        slope_start(1, 2)
-        square(1, 0)
-        slope_start(1, 3)
-        square(1, 1)
+        square(0, 2, 4, "w_plane1")
+        for t in range(1, PACK):
+            slope_start(1, t)
+        square(1, 0, 2, "w_plane2")
+        square(1, 2, 4, "w_plane3")
+        for t in range(PACK):
+            slope_finish(0, t)
         for j in range(PACK - 1):
             gather(v_picked, v_planes, j)
-        slope[1] = keep.tile([P, PACK, N], F32, name="v_plane2")
-        slope_finish(1, 0, "wt_quarter2")
+
         def slot_cols(s):
             return slice(s * SLOT_BLOCK, (s + 1) * SLOT_BLOCK)
 
-        def group_v(copy, s):
-            return group("v", copy, v_picked, s * SLOT_BLOCK, (s + 1) * SLOT_BLOCK)
-
-        gather(v_picked, v_planes, PACK - 1, 0, half)
-        v_grouped = [group_v(nc.vector.tensor_copy, 0), group_v(nc.scalar.copy, 1)]
-        gather(v_picked, v_planes, PACK - 1, half, N)
+        v_lower = [keep.tile([P, SLOT_BLOCK * PACK], BF16, name="v_lower%d" % s, align_bytes=64) for s in range(2)]
         v_upper = keep.tile([P, 2, SLOT_BLOCK * PACK], BF16, name="v_upper", align_bytes=64)
+        gather(v_picked, v_planes, PACK - 1, 0, half)
+        interleave(nc.vector.tensor_copy, v_lower[0][:], v_picked[:, :, slot_cols(0)])
+        interleave(nc.scalar.copy, v_lower[1][:], v_picked[:, :, slot_cols(1)])
+        quantise(v_q, slot_cols(0), v_lower[0][:], E4M3)
+        gather(v_picked, v_planes, PACK - 1, half, N)
         for e in range(2):
             interleave(nc.scalar.copy, v_upper[:, e, :], v_picked[:, :, slot_cols(2 + e)])
+        quantise(v_q, slot_cols(1), v_lower[1][:], E4M3)
+        slope[1] = keep.tile([P, PACK, N], F32, name="v_plane3")
+        for t in range(PACK):
+            slope_finish_scalar(1, t)
 
         m_parts = [(0, 1), (1, 2), (2, D_BLOCKS)]
         m_grouped = {}
@@ -224,35 +230,24 @@ def tile_attend_ghv_nce_kernel(tc, xT, wT, vT, wt, xm, offs, out):
                 in1=slope[g][:, :, slot_cols(s)].rearrange("p t (c i) -> p c t i", i=2),
                 op=ALU.mult)
 
-        def gradient_unit_gpsimd(g, s):
-            bank = scores(g, s)
-            av = keep.tile([P, SLOT_BLOCK, PACK], F32, name="av%d_%d" % (g, s))
-            nc.scalar.copy(out=av[:], in_=bank[:].rearrange("p t c -> p c t"))
-            nc.gpsimd.tensor_tensor(
-                out=g_cols(g, s).rearrange("p (c t) -> p c t", t=PACK),
-                in0=av[:], in1=slope[g][:, :, slot_cols(s)].rearrange("p t c -> p c t"), op=ALU.mult)
-
         def quantise_g(g, lo, hi):
             quantise(g_q[g], slice(lo * SLOT_BLOCK, hi * SLOT_BLOCK),
                      g_grouped[g][:, lo * SLOT_BLOCK * PACK:hi * SLOT_BLOCK * PACK], E5M2)
 
-        quantise(v_q, slot_cols(0), v_grouped[0][:], E4M3)
-        slope_finish(1, 1, "v_plane3")
-        quantise(v_q, slot_cols(1), v_grouped[1][:], E4M3)
         gradient_unit(0, 0)
-        gradient_unit_gpsimd(1, 0)
         quantise(v_q, slice(half, N), v_upper[:].rearrange("p e c -> p (e c)"), E4M3)
-        gradient_unit(0, 1)
-        gradient_unit_gpsimd(1, 1)
         group_m(0, 0)
         group_m(0, 1)
-        gradient_unit(0, 2)
-        gradient_unit(0, 3)
-        gradient_unit(1, 2)
-        quantise_g(0, 0, 4)
+        for s in range(1, SLOT_BLOCKS):
+            gradient_unit(0, s)
+        quantise_g(0, 0, 2)
+        quantise_g(0, 2, 4)
+        gradient_unit(1, 0)
+        gradient_unit(1, 1)
         quantise_m(0)
-        gradient_unit(1, 3)
         product(0, 0)
+        gradient_unit(1, 2)
+        gradient_unit(1, 3)
         quantise_g(1, 0, 2)
         quantise_g(1, 2, 4)
         for part in range(1, len(m_parts)):

@@ -84,7 +84,7 @@ def tile_attend_ghv_nce_kernel(tc, xT, wT, vT, wt, xm, offs, out):
             engine.memset(windows[b][:].bitcast(I32), 0)
 
         x_q = [quantised("x%d" % g, K_PASS) for g in range(ROW_PASSES)]
-        m_q = quantised("m", ROW_PASSES * D)
+        m_q = {1: quantised("m", ROW_PASSES * (D - P))}
         g_q = [quantised("g%d" % g, N) for g in range(ROW_PASSES)]
         w_q = quantised("w", N)
         v_q = quantised("v", N)
@@ -158,36 +158,42 @@ def tile_attend_ghv_nce_kernel(tc, xT, wT, vT, wt, xm, offs, out):
         quantise_x(1, 0, x_low)
         quantise_x(1, 1, x_high)
         slope[0] = tanh_half[0]
-        for t in range(PACK):
+        for t in range(3):
             slope_start(0, t)
         square(0, 0, 2, "w_plane0")
+        for t in range(2):
+            slope_finish(0, t)
+        slope_start(0, 3)
         slope_start(1, 0)
         square(0, 2, 4, "w_plane1")
-        for t in range(1, PACK):
-            slope_start(1, t)
-        square(1, 0, 2, "w_plane2")
-        square(1, 2, 4, "w_plane3")
-        for t in range(PACK):
+        for t in range(2, PACK):
             slope_finish(0, t)
+        slope_start(1, 1)
+        slope_start(1, 2)
+        square(1, 0, 2, "w_plane2")
+        slope_start(1, 3)
+        square(1, 2, 4, "w_plane3")
         for j in range(PACK - 1):
             gather(v_picked, v_planes, j)
+        slope[1] = keep.tile([P, PACK, N], F32, name="v_plane2")
+        for t in range(2):
+            slope_finish(1, t)
+        for t in range(2, PACK):
+            slope_finish_scalar(1, t)
 
         def slot_cols(s):
             return slice(s * SLOT_BLOCK, (s + 1) * SLOT_BLOCK)
 
         v_lower = [keep.tile([P, SLOT_BLOCK * PACK], BF16, name="v_lower%d" % s, align_bytes=64) for s in range(2)]
-        v_upper = keep.tile([P, 2, SLOT_BLOCK * PACK], BF16, name="v_upper", align_bytes=64)
+        v_upper = keep.tile([P, half * PACK], BF16, name="v_upper", align_bytes=64)
         gather(v_picked, v_planes, PACK - 1, 0, half)
         interleave(nc.vector.tensor_copy, v_lower[0][:], v_picked[:, :, slot_cols(0)])
         interleave(nc.scalar.copy, v_lower[1][:], v_picked[:, :, slot_cols(1)])
-        quantise(v_q, slot_cols(0), v_lower[0][:], E4M3)
         gather(v_picked, v_planes, PACK - 1, half, N)
-        for e in range(2):
-            interleave(nc.scalar.copy, v_upper[:, e, :], v_picked[:, :, slot_cols(2 + e)])
+        quantise(v_q, slot_cols(0), v_lower[0][:], E4M3)
+        interleave(nc.vector.tensor_copy, v_upper[:], v_picked[:, :, half:N])
         quantise(v_q, slot_cols(1), v_lower[1][:], E4M3)
-        slope[1] = keep.tile([P, PACK, N], F32, name="v_plane3")
-        for t in range(PACK):
-            slope_finish_scalar(1, t)
+        quantise(v_q, slice(half, N), v_upper[:], E4M3)
 
         m_parts = [(0, 1), (1, 2), (2, D_BLOCKS)]
         m_grouped = {}
@@ -202,14 +208,16 @@ def tile_attend_ghv_nce_kernel(tc, xT, wT, vT, wt, xm, offs, out):
 
         def quantise_m(part):
             lo, hi = m_parts[part]
-            quantise(m_q, slice(lo * ROW_PASSES * P, hi * ROW_PASSES * P),
+            base = min(lo, 1)
+            quantise(m_q[base], slice((lo - base) * ROW_PASSES * P, (hi - base) * ROW_PASSES * P),
                      m_grouped[part][:].rearrange("p b g c -> p (b g c)"), E4M3)
 
         acc = [out_psum.tile([P, N], F32, name="acc%d" % b) for b in range(D_BLOCKS)]
 
         def product(b, g):
-            first = (b * ROW_PASSES + g) * P
-            mx(acc[b][:], m_q, slice(first, first + P), g_q[g], whole, E5M2, g == 0, g == ROW_PASSES - 1)
+            base = min(b, 1)
+            first = ((b - base) * ROW_PASSES + g) * P
+            mx(acc[b][:], m_q[base], slice(first, first + P), g_q[g], whole, E5M2, g == 0, g == ROW_PASSES - 1)
 
         def scores(g, s):
             bank = unit_psum.tile([P, PACK, SLOT_BLOCK], F32, name="bank")
@@ -230,26 +238,34 @@ def tile_attend_ghv_nce_kernel(tc, xT, wT, vT, wt, xm, offs, out):
                 in1=slope[g][:, :, slot_cols(s)].rearrange("p t (c i) -> p c t i", i=2),
                 op=ALU.mult)
 
+        def gradient_unit_gpsimd(g, s, slot):
+            bank = scores(g, s)
+            av = keep.tile([P, SLOT_BLOCK, PACK], F32, name=slot, align_bytes=64)
+            nc.scalar.copy(out=av[:], in_=bank[:].rearrange("p t c -> p c t"))
+            nc.gpsimd.tensor_tensor(
+                out=g_cols(g, s).rearrange("p (c t) -> p c t", t=PACK),
+                in0=av[:], in1=slope[g][:, :, slot_cols(s)].rearrange("p t c -> p c t"), op=ALU.mult)
+
         def quantise_g(g, lo, hi):
             quantise(g_q[g], slice(lo * SLOT_BLOCK, hi * SLOT_BLOCK),
                      g_grouped[g][:, lo * SLOT_BLOCK * PACK:hi * SLOT_BLOCK * PACK], E5M2)
 
         gradient_unit(0, 0)
-        quantise(v_q, slice(half, N), v_upper[:].rearrange("p e c -> p (e c)"), E4M3)
+        gradient_unit_gpsimd(1, 0, "v_upper")
+        gradient_unit(1, 1)
+        gradient_unit_gpsimd(0, 1, "av_second")
         group_m(0, 0)
         group_m(0, 1)
-        for s in range(1, SLOT_BLOCKS):
-            gradient_unit(0, s)
-        quantise_g(0, 0, 2)
-        quantise_g(0, 2, 4)
-        gradient_unit(1, 0)
-        gradient_unit(1, 1)
-        quantise_m(0)
-        product(0, 0)
+        gradient_unit(0, 2)
+        gradient_unit(0, 3)
         gradient_unit(1, 2)
         gradient_unit(1, 3)
-        quantise_g(1, 0, 2)
-        quantise_g(1, 2, 4)
+        m_q[0] = (keep.tile([P, ROW_PASSES * P], U32, name="av_second", align_bytes=64),
+                  keep.tile([P, ROW_PASSES * P], U8, name="m_first_scales", align_bytes=64))
+        quantise_g(0, 0, 4)
+        quantise_m(0)
+        product(0, 0)
+        quantise_g(1, 0, 4)
         for part in range(1, len(m_parts)):
             for g in range(ROW_PASSES):
                 group_m(part, g)

@@ -30,8 +30,7 @@ def tile_attend_ghv_nce_kernel(tc, xT, wT, vT, wt, xm, offs, out):
     nc = tc.nc
     with ExitStack() as ctx:
         keep = ctx.enter_context(tc.tile_pool(name="keep", bufs=1))
-        ring = ctx.enter_context(tc.tile_pool(name="ring", bufs=3))
-        unit_psum = ctx.enter_context(tc.psum_pool(name="unit_psum", bufs=4))
+        unit_psum = ctx.enter_context(tc.psum_pool(name="unit_psum", bufs=1))
         out_psum = ctx.enter_context(tc.psum_pool(name="out_psum", bufs=1))
 
         def quantised(name, width):
@@ -84,7 +83,7 @@ def tile_attend_ghv_nce_kernel(tc, xT, wT, vT, wt, xm, offs, out):
             engine.memset(windows[b][:].bitcast(I32), 0)
 
         x_q = [quantised("x%d" % g, K_PASS) for g in range(ROW_PASSES)]
-        m_q = {1: quantised("m", ROW_PASSES * (D - P))}
+        m_q = {}
         g_q = [quantised("g%d" % g, N) for g in range(ROW_PASSES)]
         w_q = quantised("w", N)
         v_q = quantised("v", N)
@@ -121,7 +120,7 @@ def tile_attend_ghv_nce_kernel(tc, xT, wT, vT, wt, xm, offs, out):
         slope = {}
 
         def slope_start(g, t):
-            bank = unit_psum.tile([P, N], F32, name="bank")
+            bank = unit_psum.tile([P, N], F32, name="bank%d" % t)
             mx(bank[:], x_q[g], slice(t * P, (t + 1) * P), w_q, whole, E4M3, True, True)
             nc.scalar.activation(out=tanh_half[g][:, t, :], in_=bank[:], func=ACT.Tanh, scale=0.5)
 
@@ -141,10 +140,8 @@ def tile_attend_ghv_nce_kernel(tc, xT, wT, vT, wt, xm, offs, out):
 
         def slope_finish_scalar(g, t):
             nc.scalar.activation(out=slope[g][:, t, :], in_=squared[g, t], func=ACT.Identity,
-                                 scale=wt_quarter[:, g, t:t + 1], bias=wt_peak[:, g, t:t + 1])
+                                 scale=wt_quarter[:, g, t:t + 1], bias=wt_peak[:, t:t + 1])
 
-        wt_peak = keep.tile([P, ROW_PASSES, PACK], F32, name="wt_peak")
-        nc.vector.tensor_scalar(out=wt_peak[:], in0=wt_raw, scalar1=0.25, scalar2=None, op0=ALU.mult)
         wt_quarter = keep.tile([P, ROW_PASSES, PACK], F32, name="wt_quarter")
         nc.vector.tensor_scalar(out=wt_quarter[:], in0=wt_raw, scalar1=-0.25, scalar2=None, op0=ALU.mult)
         quantise_w(0)
@@ -173,13 +170,14 @@ def tile_attend_ghv_nce_kernel(tc, xT, wT, vT, wt, xm, offs, out):
         square(1, 0, 2, "w_plane2")
         slope_start(1, 3)
         square(1, 2, 4, "w_plane3")
+        warm = unit_psum.tile([P, N], F32, name="bank%d" % (PACK - 1))
+        for t in range(PACK):
+            mx(warm[:], x_q[1], slice(t * P, (t + 1) * P), w_q, whole, E4M3, True, True)
         for j in range(PACK - 1):
             gather(v_picked, v_planes, j)
         slope[1] = keep.tile([P, PACK, N], F32, name="v_plane2")
         for t in range(2):
             slope_finish(1, t)
-        for t in range(2, PACK):
-            slope_finish_scalar(1, t)
 
         def slot_cols(s):
             return slice(s * SLOT_BLOCK, (s + 1) * SLOT_BLOCK)
@@ -190,42 +188,42 @@ def tile_attend_ghv_nce_kernel(tc, xT, wT, vT, wt, xm, offs, out):
         interleave(nc.vector.tensor_copy, v_lower[0][:], v_picked[:, :, slot_cols(0)])
         interleave(nc.scalar.copy, v_lower[1][:], v_picked[:, :, slot_cols(1)])
         gather(v_picked, v_planes, PACK - 1, half, N)
+        wt_peak = keep.tile([P, PACK], F32, name="v_plane3")
+        nc.scalar.activation(out=wt_peak[:], in_=wt_raw[:, 1, :], func=ACT.Copy, scale=0.25)
+        for t in range(2, PACK):
+            slope_finish_scalar(1, t)
         quantise(v_q, slot_cols(0), v_lower[0][:], E4M3)
         interleave(nc.vector.tensor_copy, v_upper[:], v_picked[:, :, half:N])
         quantise(v_q, slot_cols(1), v_lower[1][:], E4M3)
         quantise(v_q, slice(half, N), v_upper[:], E4M3)
 
-        m_parts = [(0, 1), (1, 2), (2, D_BLOCKS)]
         m_grouped = {}
 
-        def group_m(part, g):
-            lo, hi = m_parts[part]
-            if part not in m_grouped:
-                m_grouped[part] = keep.tile([P, hi - lo, ROW_PASSES, P * PACK], BF16, name="m_grouped%d" % part,
-                                            align_bytes=64)
-            for b in range(lo, hi):
-                interleave(nc.scalar.copy, m_grouped[part][:, b - lo, g, :], m_raw[g][:, :, b * P:(b + 1) * P])
+        def group_m(copy, b, slot):
+            m_grouped[b] = keep.tile([P, ROW_PASSES, P * PACK], BF16, name=slot, align_bytes=64)
+            for g in range(ROW_PASSES):
+                interleave(copy, m_grouped[b][:, g, :], m_raw[g][:, :, b * P:(b + 1) * P])
 
-        def quantise_m(part):
-            lo, hi = m_parts[part]
-            base = min(lo, 1)
-            quantise(m_q[base], slice((lo - base) * ROW_PASSES * P, (hi - base) * ROW_PASSES * P),
-                     m_grouped[part][:].rearrange("p b g c -> p (b g c)"), E4M3)
+        def quantise_m(b, slot):
+            m_q[b] = (keep.tile([P, ROW_PASSES * P], U32, name=slot, align_bytes=64),
+                      keep.tile([P, ROW_PASSES * P], U8, name="m_scales%d" % b, align_bytes=64))
+            quantise(m_q[b], slice(0, ROW_PASSES * P), m_grouped[b][:].rearrange("p g c -> p (g c)"), E4M3)
 
         acc = [out_psum.tile([P, N], F32, name="acc%d" % b) for b in range(D_BLOCKS)]
 
         def product(b, g):
-            base = min(b, 1)
-            first = ((b - base) * ROW_PASSES + g) * P
-            mx(acc[b][:], m_q[base], slice(first, first + P), g_q[g], whole, E5M2, g == 0, g == ROW_PASSES - 1)
+            mx(acc[b][:], m_q[b], slice(g * P, (g + 1) * P), g_q[g], whole, E5M2, g == 0, g == ROW_PASSES - 1)
+
+        banks_taken = []
 
         def scores(g, s):
-            bank = unit_psum.tile([P, PACK, SLOT_BLOCK], F32, name="bank")
+            bank = unit_psum.tile([P, PACK, SLOT_BLOCK], F32, name="bank%d" % (len(banks_taken) % PACK))
+            banks_taken.append((g, s))
             for t in range(PACK):
                 mx(bank[:, t, :], x_q[g], slice(t * P, (t + 1) * P), v_q, slot_cols(s), E4M3, True, True)
             return bank
 
-        g_grouped = [keep.tile([P, N * PACK], BF16, name="g_grouped%d" % g, align_bytes=64) for g in range(ROW_PASSES)]
+        g_grouped = [keep.tile([P, N * PACK], BF16, name=slot, align_bytes=64) for slot in ("g_grouped0", "v_upper")]
 
         def g_cols(g, s):
             return g_grouped[g][:, s * SLOT_BLOCK * PACK:(s + 1) * SLOT_BLOCK * PACK]
@@ -234,8 +232,8 @@ def tile_attend_ghv_nce_kernel(tc, xT, wT, vT, wt, xm, offs, out):
             bank = scores(g, s)
             nc.vector.tensor_tensor(
                 out=g_cols(g, s).rearrange("p (c i t) -> p c t i", i=2, t=PACK),
-                in0=bank[:].rearrange("p t (c i) -> p c t i", i=2),
-                in1=slope[g][:, :, slot_cols(s)].rearrange("p t (c i) -> p c t i", i=2),
+                in0=slope[g][:, :, slot_cols(s)].rearrange("p t (c i) -> p c t i", i=2),
+                in1=bank[:].rearrange("p t (c i) -> p c t i", i=2),
                 op=ALU.mult)
 
         def gradient_unit_gpsimd(g, s, slot):
@@ -250,35 +248,41 @@ def tile_attend_ghv_nce_kernel(tc, xT, wT, vT, wt, xm, offs, out):
             quantise(g_q[g], slice(lo * SLOT_BLOCK, hi * SLOT_BLOCK),
                      g_grouped[g][:, lo * SLOT_BLOCK * PACK:hi * SLOT_BLOCK * PACK], E5M2)
 
+        gradient_unit_gpsimd(1, 0, "av_first")
         gradient_unit(0, 0)
-        gradient_unit_gpsimd(1, 0, "v_upper")
         gradient_unit(1, 1)
         gradient_unit_gpsimd(0, 1, "av_second")
-        group_m(0, 0)
-        group_m(0, 1)
+        group_m(nc.scalar.copy, 0, "m_grouped0")
+        group_m(nc.scalar.copy, 1, "m_grouped1")
         gradient_unit(0, 2)
         gradient_unit(0, 3)
         gradient_unit(1, 2)
         gradient_unit(1, 3)
-        m_q[0] = (keep.tile([P, ROW_PASSES * P], U32, name="av_second", align_bytes=64),
-                  keep.tile([P, ROW_PASSES * P], U8, name="m_first_scales", align_bytes=64))
         quantise_g(0, 0, 4)
-        quantise_m(0)
+        quantise_m(0, "av_second")
         product(0, 0)
         quantise_g(1, 0, 4)
-        for part in range(1, len(m_parts)):
-            for g in range(ROW_PASSES):
-                group_m(part, g)
+        product(0, 1)
+        quantise_m(1, "g_grouped0")
+        group_m(nc.vector.tensor_copy, 2, "v_upper")
 
-        for b in range(D_BLOCKS):
-            if b > 0:
-                product(b, 0)
-            product(b, 1)
-            if b + 1 < len(m_parts):
-                quantise_m(b + 1)
-            dense = ring.tile([P, N], F32, name="dense")
-            window = windows[b % WINDOWS]
-            for lo, hi in ([(0, half), (half, N)] if b == 0 else [(0, N)]):
-                nc.scalar.copy(out=dense[:, lo:hi], in_=acc[b][:, lo:hi])
-                nc.vector.tensor_copy(window[:].indirect(offsets[:, lo // 16:hi // 16]), dense[:, lo:hi])
-            nc.sync.dma_start(out=out[b * P:(b + 1) * P, :], in_=window[:])
+        def place(b, lo, hi, slot):
+            dense = keep.tile([P, hi - lo], F32, name=slot, align_bytes=64)
+            nc.scalar.copy(out=dense[:], in_=acc[b][:, lo:hi])
+            nc.vector.tensor_copy(windows[b][:].indirect(offsets[:, lo // 16:hi // 16]), dense[:])
+
+        def finish(b):
+            for g in range(ROW_PASSES):
+                product(b, g)
+            place(b, 0, N, "dense%d" % b)
+            nc.sync.dma_start(out=out[b * P:(b + 1) * P, :], in_=windows[b][:])
+
+        place(0, 0, half, "dense_low")
+        place(0, half, N, "dense_high")
+        nc.sync.dma_start(out=out[0:P, :], in_=windows[0][:])
+        quantise_m(2, "dense_high")
+        finish(1)
+        group_m(nc.scalar.copy, 3, "dense_low")
+        quantise_m(3, "m_codes3")
+        finish(2)
+        finish(3)

@@ -23,7 +23,7 @@ ROW_PASSES = R // K_PASS
 SLOT_BLOCK = 128
 SLOT_BLOCKS = N // SLOT_BLOCK
 D_BLOCKS = D // P
-WINDOWS = 4
+HALF = N // 2
 
 
 def tile_attend_ghv_nce_kernel(tc, xT, wT, vT, wt, xm, offs, out):
@@ -49,9 +49,12 @@ def tile_attend_ghv_nce_kernel(tc, xT, wT, vT, wt, xm, offs, out):
                 start=start, stop=stop,
             )
 
-        def interleave(copy, grouped, planes, run=2):
-            copy(out=grouped.rearrange("p (c i t) -> p c t i", i=run, t=PACK),
-                 in_=planes.rearrange("p t (c i) -> p c t i", i=run))
+        def interleave(copy, grouped, planes):
+            copy(out=grouped.rearrange("p (c i t) -> p c t i", i=2, t=PACK),
+                 in_=planes.rearrange("p t (c i) -> p c t i", i=2))
+
+        def block(index, width=P):
+            return slice(index * width, (index + 1) * width)
 
         offsets = keep.tile([P, N // 16], U16, name="offsets")
         x_raw = [keep.tile([P, PACK, K_PASS], F32, name="x_raw%d" % g) for g in range(ROW_PASSES)]
@@ -71,218 +74,188 @@ def tile_attend_ghv_nce_kernel(tc, xT, wT, vT, wt, xm, offs, out):
         for j in range(1, PACK):
             nc.sync.dma_start(out=w_planes[j][:], in_=w_rows[:, j, :])
         for g in range(ROW_PASSES):
-            nc.sync.dma_start(out=x_raw[g][:], in_=x_rows[:, :, g * K_PASS:(g + 1) * K_PASS])
+            nc.sync.dma_start(out=x_raw[g][:], in_=x_rows[:, :, block(g, K_PASS)])
         for j in range(PACK):
             nc.sync.dma_start(out=v_planes[j][:], in_=v_rows[:, j, :])
         for g in range(ROW_PASSES):
             nc.sync.dma_start(out=m_raw[g][:], in_=m_rows[g])
 
-        windows = [keep.tile([P, T], F32, name="window%d" % b) for b in range(WINDOWS)]
-        for b in range(WINDOWS):
+        windows = [keep.tile([P, T], F32, name="window%d" % b) for b in range(D_BLOCKS)]
+        for b in range(D_BLOCKS):
             engine = nc.gpsimd if b % 2 else nc.vector
             engine.memset(windows[b][:].bitcast(I32), 0)
 
+        wt_quarter = keep.tile([P, ROW_PASSES, PACK], F32, name="wt_quarter")
+        nc.vector.tensor_scalar(out=wt_quarter[:], in0=wt_raw, scalar1=-0.25, scalar2=None, op0=ALU.mult)
+
         x_q = [quantised("x%d" % g, K_PASS) for g in range(ROW_PASSES)]
-        m_q = {}
+        m_q = [[quantised("m%d_%d" % (b, g), P) for g in range(ROW_PASSES)] for b in range(D_BLOCKS)]
         g_q = [quantised("g%d" % g, N) for g in range(ROW_PASSES)]
         w_q = quantised("w", N)
         v_q = quantised("v", N)
 
-        def cast_x(copy, g, h):
-            grouped = keep.tile([P, 2 * P * PACK], BF16, name="x_grouped%d_%d" % (g, h), align_bytes=64)
-            copy(out=grouped[:].rearrange("p (t m j) -> p m j t", t=2, j=PACK),
-                 in_=x_raw[g][:].rearrange("p j (m t) -> p m j t", t=PACK)[:, :, :, 2 * h:2 * h + 2])
-            return grouped
-
-        def quantise_x(g, h, grouped):
-            quantise(x_q[g], slice(2 * h * P, (2 * h + 2) * P), grouped[:], E4M3)
+        def prepare_x(g, copies):
+            grouped = [keep.tile([P, 2 * P * PACK], BF16, name="x_grouped%d_%d" % (g, h), align_bytes=64)
+                       for h in range(2)]
+            for h in range(2):
+                target = grouped[h][:].rearrange("p (t m j) -> p m j t", t=2, j=PACK)
+                source = x_raw[g][:].rearrange("p j (m t) -> p m j t", t=PACK)[:, :, :, 2 * h:2 * h + 2]
+                for part, copy in enumerate(copies):
+                    cols = block(part, P // len(copies))
+                    copy(out=target[:, cols], in_=source[:, cols])
+            for h in range(2):
+                quantise(x_q[g], block(h, 2 * P), grouped[h][:], E4M3)
 
         def gather(picked, planes, j, lo=0, hi=N):
             nc.vector.tensor_copy(picked[:, j, lo:hi], planes[j][:].indirect(offsets[:, lo // 16:hi // 16]))
 
-        whole = slice(0, K_PASS)
-        half = N // 2
-        v_picked = keep.tile([P, PACK, N], F32, name="v_picked")
+        def last_plane(name, picked, planes, codes):
+            def group(copy, s, slot):
+                grouped = keep.tile([P, SLOT_BLOCK * PACK], BF16, name="%s_grouped%d" % (name, slot), align_bytes=64)
+                interleave(copy, grouped[:], picked[:, :, block(s)])
+                return grouped
+
+            gather(picked, planes, PACK - 1, 0, HALF)
+            first = group(nc.scalar.copy, 0, 0)
+            gather(picked, planes, PACK - 1, HALF, N)
+            last = group(nc.scalar.copy, 3, 3)
+            second = group(nc.vector.tensor_copy, 1, 1)
+            quantise(codes, block(0), first[:], E4M3)
+            quantise(codes, block(1), second[:], E4M3)
+            third = group(nc.vector.tensor_copy, 2, 0)
+            quantise(codes, block(3), last[:], E4M3)
+            quantise(codes, block(2), third[:], E4M3)
+
+        banks_taken = []
+
+        def next_bank(shape):
+            bank = unit_psum.tile(shape, F32, name="bank%d" % (len(banks_taken) % PACK))
+            banks_taken.append(bank)
+            return bank
+
+        def scores(g, s, table):
+            bank = next_bank([P, PACK, SLOT_BLOCK])
+            for t in range(PACK):
+                mx(bank[:, t, :], x_q[g], block(t), table, block(s), E4M3, True, True)
+            return bank
+
+        whole = slice(0, N)
         w_picked = keep.tile([P, PACK, N], F32, name="w_picked")
-        w_grouped = [keep.tile([P, half * PACK], BF16, name="w_grouped%d" % h, align_bytes=64) for h in range(2)]
-        for j in range(PACK - 1):
-            gather(w_picked, w_planes, j)
-        gather(w_picked, w_planes, PACK - 1, 0, half)
-        interleave(nc.scalar.copy, w_grouped[0][:], w_picked[:, :, 0:half])
-        gather(w_picked, w_planes, PACK - 1, half, N)
-        interleave(nc.vector.tensor_copy, w_grouped[1][:], w_picked[:, :, half:N])
+        v_picked = keep.tile([P, PACK, N], F32, name="v_picked")
+        slope = [keep.tile([P, PACK, N], F32, name="slope%d" % g) for g in range(ROW_PASSES)]
 
-        def quantise_w(h):
-            quantise(w_q, slice(h * half, (h + 1) * half), w_grouped[h][:], E4M3)
-
-        tanh_half = [keep.tile([P, PACK, N], F32, name="tanh_half%d" % g) for g in range(ROW_PASSES)]
-        squared = {}
-        slope = {}
-
-        def slope_start(g, t):
-            bank = unit_psum.tile([P, N], F32, name="bank%d" % t)
-            mx(bank[:], x_q[g], slice(t * P, (t + 1) * P), w_q, whole, E4M3, True, True)
-            nc.scalar.activation(out=tanh_half[g][:, t, :], in_=bank[:], func=ACT.Tanh, scale=0.5)
-
-        def square(g, lo, hi, slot):
-            tile = keep.tile([P, hi - lo, N], F32, name=slot)
-            planes = tanh_half[g][:, lo:hi, :]
-            if (g, lo) == (0, 0):
-                nc.vector.tensor_tensor(out=tile[:], in0=planes, in1=planes, op=ALU.mult)
-            else:
-                nc.scalar.activation(out=tile[:], in_=planes, func=ACT.Square)
-            for t in range(lo, hi):
-                squared[g, t] = tile[:, t - lo, :]
-
-        def slope_finish(g, t):
-            nc.vector.tensor_scalar(out=slope[g][:, t, :], in0=squared[g, t], scalar1=1.0,
+        def finish_slope(g, t):
+            nc.vector.tensor_scalar(out=slope[g][:, t, :], in0=slope[g][:, t, :], scalar1=1.0,
                                     scalar2=wt_quarter[:, g, t:t + 1], op0=ALU.subtract, op1=ALU.mult)
 
-        def slope_finish_scalar(g, t):
-            nc.scalar.activation(out=slope[g][:, t, :], in_=squared[g, t], func=ACT.Identity,
-                                 scale=wt_quarter[:, g, t:t + 1], bias=wt_peak[:, t:t + 1])
+        def tanh_half(g, t):
+            bank = next_bank([P, N])
+            mx(bank[:], x_q[g], block(t), w_q, whole, E4M3, True, True)
+            nc.scalar.activation(out=slope[g][:, t, :], in_=bank[:], func=ACT.Tanh, scale=0.5)
 
-        wt_quarter = keep.tile([P, ROW_PASSES, PACK], F32, name="wt_quarter")
-        nc.vector.tensor_scalar(out=wt_quarter[:], in0=wt_raw, scalar1=-0.25, scalar2=None, op0=ALU.mult)
-        quantise_w(0)
-        x_low = cast_x(nc.vector.tensor_copy, 0, 0)
-        x_high = cast_x(nc.scalar.copy, 0, 1)
-        quantise_w(1)
-        quantise_x(0, 0, x_low)
-        quantise_x(0, 1, x_high)
-        x_low = cast_x(nc.vector.tensor_copy, 1, 0)
-        x_high = cast_x(nc.vector.tensor_copy, 1, 1)
-        quantise_x(1, 0, x_low)
-        quantise_x(1, 1, x_high)
-        slope[0] = tanh_half[0]
-        for t in range(3):
-            slope_start(0, t)
-        square(0, 0, 2, "w_plane0")
-        for t in range(2):
-            slope_finish(0, t)
-        slope_start(0, 3)
-        slope_start(1, 0)
-        square(0, 2, 4, "w_plane1")
-        for t in range(2, PACK):
-            slope_finish(0, t)
-        slope_start(1, 1)
-        slope_start(1, 2)
-        square(1, 0, 2, "w_plane2")
-        slope_start(1, 3)
-        square(1, 2, 4, "w_plane3")
-        warm = unit_psum.tile([P, N], F32, name="bank%d" % (PACK - 1))
-        for t in range(PACK):
-            mx(warm[:], x_q[1], slice(t * P, (t + 1) * P), w_q, whole, E4M3, True, True)
+        def square(values):
+            nc.scalar.activation(out=values, in_=values, func=ACT.Square)
+
         for j in range(PACK - 1):
-            gather(v_picked, v_planes, j)
-        slope[1] = keep.tile([P, PACK, N], F32, name="v_plane2")
-        for t in range(2):
-            slope_finish(1, t)
-
-        def slot_cols(s):
-            return slice(s * SLOT_BLOCK, (s + 1) * SLOT_BLOCK)
-
-        v_lower = [keep.tile([P, SLOT_BLOCK * PACK], BF16, name="v_lower%d" % s, align_bytes=64) for s in range(2)]
-        v_upper = keep.tile([P, half * PACK], BF16, name="v_upper", align_bytes=64)
-        gather(v_picked, v_planes, PACK - 1, 0, half)
-        interleave(nc.vector.tensor_copy, v_lower[0][:], v_picked[:, :, slot_cols(0)])
-        interleave(nc.scalar.copy, v_lower[1][:], v_picked[:, :, slot_cols(1)])
-        gather(v_picked, v_planes, PACK - 1, half, N)
-        wt_peak = keep.tile([P, PACK], F32, name="v_plane3")
-        nc.scalar.activation(out=wt_peak[:], in_=wt_raw[:, 1, :], func=ACT.Copy, scale=0.25)
-        for t in range(2, PACK):
-            slope_finish_scalar(1, t)
-        quantise(v_q, slot_cols(0), v_lower[0][:], E4M3)
-        interleave(nc.vector.tensor_copy, v_upper[:], v_picked[:, :, half:N])
-        quantise(v_q, slot_cols(1), v_lower[1][:], E4M3)
-        quantise(v_q, slice(half, N), v_upper[:], E4M3)
+            gather(w_picked, w_planes, j)
+        last_plane("w", w_picked, w_planes, w_q)
+        prepare_x(0, (nc.scalar.copy, nc.vector.tensor_copy))
+        prepare_x(1, (nc.vector.tensor_copy,))
+        for t in range(PACK):
+            tanh_half(0, t)
+        lower = slope[0][:, 0:2, :]
+        nc.vector.tensor_tensor(out=lower, in0=lower, in1=lower, op=ALU.mult)
+        square(slope[0][:, 2:4, :])
+        gather(v_picked, v_planes, 0)
+        for t in range(PACK):
+            finish_slope(0, t)
+        tanh_half(1, 0)
+        tanh_half(1, 1)
+        square(slope[1][:, 0:2, :])
+        tanh_half(1, 2)
+        tanh_half(1, 3)
+        square(slope[1][:, 2, :])
+        square(slope[1][:, 3, :])
+        gather(v_picked, v_planes, 1)
+        finish_slope(1, 0)
+        finish_slope(1, 1)
+        gather(v_picked, v_planes, 2)
+        finish_slope(1, 2)
+        finish_slope(1, 3)
+        last_plane("v", v_picked, v_planes, v_q)
 
         m_grouped = {}
+        for g in range(ROW_PASSES):
+            for b in range(D_BLOCKS):
+                m_grouped[b, g] = keep.tile([P, P * PACK], BF16, name="m_grouped%d_%d" % (b, g), align_bytes=64)
+                interleave(nc.scalar.copy, m_grouped[b, g][:], m_raw[g][:, :, block(b)])
 
-        def group_m(copy, b, slot):
-            m_grouped[b] = keep.tile([P, ROW_PASSES, P * PACK], BF16, name=slot, align_bytes=64)
-            for g in range(ROW_PASSES):
-                interleave(copy, m_grouped[b][:, g, :], m_raw[g][:, :, b * P:(b + 1) * P])
-
-        def quantise_m(b, slot):
-            m_q[b] = (keep.tile([P, ROW_PASSES * P], U32, name=slot, align_bytes=64),
-                      keep.tile([P, ROW_PASSES * P], U8, name="m_scales%d" % b, align_bytes=64))
-            quantise(m_q[b], slice(0, ROW_PASSES * P), m_grouped[b][:].rearrange("p g c -> p (g c)"), E4M3)
+        def quantise_m(b, g):
+            quantise(m_q[b][g], slice(0, P), m_grouped[b, g][:], E4M3)
 
         acc = [out_psum.tile([P, N], F32, name="acc%d" % b) for b in range(D_BLOCKS)]
 
         def product(b, g):
-            mx(acc[b][:], m_q[b], slice(g * P, (g + 1) * P), g_q[g], whole, E5M2, g == 0, g == ROW_PASSES - 1)
+            mx(acc[b][:], m_q[b][g], slice(0, P), g_q[g], whole, E5M2, g == 0, g == ROW_PASSES - 1)
 
-        banks_taken = []
-
-        def scores(g, s):
-            bank = unit_psum.tile([P, PACK, SLOT_BLOCK], F32, name="bank%d" % (len(banks_taken) % PACK))
-            banks_taken.append((g, s))
-            for t in range(PACK):
-                mx(bank[:, t, :], x_q[g], slice(t * P, (t + 1) * P), v_q, slot_cols(s), E4M3, True, True)
-            return bank
-
-        g_grouped = [keep.tile([P, N * PACK], BF16, name=slot, align_bytes=64) for slot in ("g_grouped0", "v_upper")]
-
-        def g_cols(g, s):
-            return g_grouped[g][:, s * SLOT_BLOCK * PACK:(s + 1) * SLOT_BLOCK * PACK]
+        g_grouped = [keep.tile([P, N * PACK], BF16, name="g_grouped%d" % g, align_bytes=64) for g in range(ROW_PASSES)]
 
         def gradient_unit(g, s):
-            bank = scores(g, s)
+            bank = scores(g, s, v_q)
             nc.vector.tensor_tensor(
-                out=g_cols(g, s).rearrange("p (c i t) -> p c t i", i=2, t=PACK),
-                in0=slope[g][:, :, slot_cols(s)].rearrange("p t (c i) -> p c t i", i=2),
+                out=g_grouped[g][:, block(s, SLOT_BLOCK * PACK)].rearrange("p (c i t) -> p c t i", i=2, t=PACK),
+                in0=slope[g][:, :, block(s)].rearrange("p t (c i) -> p c t i", i=2),
                 in1=bank[:].rearrange("p t (c i) -> p c t i", i=2),
                 op=ALU.mult)
-
-        def gradient_unit_gpsimd(g, s, slot):
-            bank = scores(g, s)
-            av = keep.tile([P, SLOT_BLOCK, PACK], F32, name=slot, align_bytes=64)
-            nc.scalar.copy(out=av[:], in_=bank[:].rearrange("p t c -> p c t"))
-            nc.gpsimd.tensor_tensor(
-                out=g_cols(g, s).rearrange("p (c t) -> p c t", t=PACK),
-                in0=av[:], in1=slope[g][:, :, slot_cols(s)].rearrange("p t c -> p c t"), op=ALU.mult)
 
         def quantise_g(g, lo, hi):
             quantise(g_q[g], slice(lo * SLOT_BLOCK, hi * SLOT_BLOCK),
                      g_grouped[g][:, lo * SLOT_BLOCK * PACK:hi * SLOT_BLOCK * PACK], E5M2)
 
-        gradient_unit_gpsimd(1, 0, "av_first")
-        gradient_unit(0, 0)
-        gradient_unit(1, 1)
-        gradient_unit_gpsimd(0, 1, "av_second")
-        group_m(nc.scalar.copy, 0, "m_grouped0")
-        group_m(nc.scalar.copy, 1, "m_grouped1")
-        gradient_unit(0, 2)
-        gradient_unit(0, 3)
-        gradient_unit(1, 2)
-        gradient_unit(1, 3)
-        quantise_g(0, 0, 4)
-        quantise_m(0, "av_second")
-        product(0, 0)
-        quantise_g(1, 0, 4)
-        product(0, 1)
-        quantise_m(1, "g_grouped0")
-        group_m(nc.vector.tensor_copy, 2, "v_upper")
+        last = block(SLOT_BLOCKS - 1)
+        ready = (SLOT_BLOCKS - 1) * SLOT_BLOCK
+        nc.vector.memset(g_q[1][0][:, last], 0)
+        nc.vector.memset(g_q[1][1][:, last], 0)
+        zeros = keep.tile([P, SLOT_BLOCK], F32, name="zeros")
+        nc.vector.memset(zeros[:], 0.0)
 
-        def place(b, lo, hi, slot):
-            dense = keep.tile([P, hi - lo], F32, name=slot, align_bytes=64)
-            nc.scalar.copy(out=dense[:], in_=acc[b][:, lo:hi])
+        for s in (0, 1, 3, 2):
+            gradient_unit(0, s)
+        gradient_unit(1, 0)
+        quantise_g(0, 0, 4)
+        gradient_unit(1, 1)
+        quantise_m(0, 0)
+        gradient_unit(1, 2)
+        quantise_g(1, 0, 2)
+        quantise_m(0, 1)
+        quantise_g(1, 2, 3)
+        early = next_bank([P, N])
+        for g in range(ROW_PASSES):
+            mx(early[:], m_q[0][g], slice(0, P), g_q[g], whole, E5M2, g == 0, g == ROW_PASSES - 1)
+        product(0, 0)
+        gradient_unit(1, 3)
+        quantise_m(1, 0)
+        quantise_g(1, 3, 4)
+        product(0, 1)
+
+        def dense_copy(name, source):
+            dense = keep.tile([P, source.shape[1]], F32, name=name)
+            nc.scalar.copy(out=dense[:], in_=source)
+            return dense
+
+        def scatter(b, lo, hi, dense):
             nc.vector.tensor_copy(windows[b][:].indirect(offsets[:, lo // 16:hi // 16]), dense[:])
 
-        def finish(b):
+        scatter(0, 0, ready, dense_copy("dense_early", early[:, 0:ready]))
+        dense_last = dense_copy("dense_last", acc[0][:, last])
+        nc.vector.tensor_tensor(windows[0][:].indirect(offsets[:, ready // 16:N // 16]), dense_last[:], zeros[:], ALU.add)
+        nc.sync.dma_start(out=out[block(0), :], in_=windows[0][:])
+        quantise_m(1, 1)
+        for b in range(1, D_BLOCKS):
             for g in range(ROW_PASSES):
                 product(b, g)
-            place(b, 0, N, "dense%d" % b)
-            nc.sync.dma_start(out=out[b * P:(b + 1) * P, :], in_=windows[b][:])
-
-        place(0, 0, half, "dense_low")
-        place(0, half, N, "dense_high")
-        nc.sync.dma_start(out=out[0:P, :], in_=windows[0][:])
-        quantise_m(2, "dense_high")
-        finish(1)
-        group_m(nc.scalar.copy, 3, "dense_low")
-        quantise_m(3, "m_codes3")
-        finish(2)
-        finish(3)
+            if b + 1 < D_BLOCKS:
+                for g in range(ROW_PASSES):
+                    quantise_m(b + 1, g)
+            scatter(b, 0, N, dense_copy("dense%d" % b, acc[b][:]))
+            nc.sync.dma_start(out=out[block(b), :], in_=windows[b][:])

@@ -58,7 +58,8 @@ def tile_attend_ghv_nce_kernel(tc, xT, wT, vT, wt, xm, offs, out):
 
         offsets = keep.tile([P, N // 16], U16, name="offsets")
         x_raw = [keep.tile([P, PACK, K_PASS], F32, name="x_raw%d" % g) for g in range(ROW_PASSES)]
-        m_raw = [keep.tile([P, PACK, D], F32, name="m_raw%d" % g) for g in range(ROW_PASSES)]
+        m_raw = [[keep.tile([P, PACK, D // 2], F32, name="m_raw%d_%d" % (h, g)) for g in range(ROW_PASSES)]
+                 for h in range(2)]
         w_planes = [keep.tile([P, T], F32, name="w_plane%d" % j) for j in range(PACK)]
         v_planes = [keep.tile([P, T], F32, name="v_plane%d" % j) for j in range(PACK)]
         wt_padded = keep.tile([P, ROW_PASSES, 2 * PACK], F32, name="wt_padded")
@@ -77,8 +78,9 @@ def tile_attend_ghv_nce_kernel(tc, xT, wT, vT, wt, xm, offs, out):
             nc.sync.dma_start(out=x_raw[g][:], in_=x_rows[:, :, block(g, K_PASS)])
         for j in range(PACK):
             nc.sync.dma_start(out=v_planes[j][:], in_=v_rows[:, j, :])
-        for g in range(ROW_PASSES):
-            nc.sync.dma_start(out=m_raw[g][:], in_=m_rows[g])
+        for h in range(2):
+            for g in range(ROW_PASSES):
+                nc.sync.dma_start(out=m_raw[h][g][:], in_=m_rows[g][:, :, block(h, D // 2)])
 
         windows = [keep.tile([P, T], F32, name="window%d" % b) for b in range(D_BLOCKS)]
         for b in range(D_BLOCKS):
@@ -89,7 +91,6 @@ def tile_attend_ghv_nce_kernel(tc, xT, wT, vT, wt, xm, offs, out):
         nc.vector.tensor_scalar(out=wt_quarter[:], in0=wt_raw, scalar1=-0.25, scalar2=None, op0=ALU.mult)
 
         x_q = [quantised("x%d" % g, K_PASS) for g in range(ROW_PASSES)]
-        m_q = [[quantised("m%d_%d" % (b, g), P) for g in range(ROW_PASSES)] for b in range(D_BLOCKS)]
         g_q = [quantised("g%d" % g, N) for g in range(ROW_PASSES)]
         w_q = quantised("w", N)
         v_q = quantised("v", N)
@@ -144,9 +145,9 @@ def tile_attend_ghv_nce_kernel(tc, xT, wT, vT, wt, xm, offs, out):
         v_picked = keep.tile([P, PACK, N], F32, name="v_picked")
         slope = [keep.tile([P, PACK, N], F32, name="slope%d" % g) for g in range(ROW_PASSES)]
 
-        def finish_slope(g, t):
-            nc.vector.tensor_scalar(out=slope[g][:, t, :], in0=slope[g][:, t, :], scalar1=1.0,
-                                    scalar2=wt_quarter[:, g, t:t + 1], op0=ALU.subtract, op1=ALU.mult)
+        def finish_slope(t):
+            nc.vector.tensor_scalar(out=slope[0][:, t, :], in0=slope[0][:, t, :], scalar1=1.0,
+                                    scalar2=wt_quarter[:, 0, t:t + 1], op0=ALU.subtract, op1=ALU.mult)
 
         def tanh_half(g, t):
             bank = next_bank([P, N])
@@ -168,7 +169,7 @@ def tile_attend_ghv_nce_kernel(tc, xT, wT, vT, wt, xm, offs, out):
         square(slope[0][:, 2:4, :])
         gather(v_picked, v_planes, 0)
         for t in range(PACK):
-            finish_slope(0, t)
+            finish_slope(t)
         tanh_half(1, 0)
         tanh_half(1, 1)
         square(slope[1][:, 0:2, :])
@@ -177,85 +178,115 @@ def tile_attend_ghv_nce_kernel(tc, xT, wT, vT, wt, xm, offs, out):
         square(slope[1][:, 2, :])
         square(slope[1][:, 3, :])
         gather(v_picked, v_planes, 1)
-        finish_slope(1, 0)
-        finish_slope(1, 1)
         gather(v_picked, v_planes, 2)
-        finish_slope(1, 2)
-        finish_slope(1, 3)
         last_plane("v", v_picked, v_planes, v_q)
-
-        m_grouped = {}
-        for g in range(ROW_PASSES):
-            for b in range(D_BLOCKS):
-                m_grouped[b, g] = keep.tile([P, P * PACK], BF16, name="m_grouped%d_%d" % (b, g), align_bytes=64)
-                interleave(nc.scalar.copy, m_grouped[b, g][:], m_raw[g][:, :, block(b)])
-
-        def quantise_m(b, g):
-            quantise(m_q[b][g], slice(0, P), m_grouped[b, g][:], E4M3)
+        wt_peak = keep.tile([P, PACK], F32, name="v_plane%d" % (PACK - 1))
+        nc.scalar.activation(out=wt_peak[:], in_=wt_raw[:, 1, :], func=ACT.Copy, scale=0.25)
+        for t in range(PACK):
+            nc.scalar.activation(out=slope[1][:, t, :], in_=slope[1][:, t, :], func=ACT.Identity,
+                                 scale=wt_quarter[:, 1, t:t + 1], bias=wt_peak[:, t:t + 1])
 
         acc = [out_psum.tile([P, N], F32, name="acc%d" % b) for b in range(D_BLOCKS)]
+        g_pieces = {(0, 0, 4): "g_grouped0", (1, 0, 2): "g_lower", (1, 2, 3): "g_third", (1, 3, 4): "m_grouped0"}
+        g_grouped = {}
 
-        def product(b, g):
-            mx(acc[b][:], m_q[b][g], slice(0, P), g_q[g], whole, E5M2, g == 0, g == ROW_PASSES - 1)
-
-        g_grouped = [keep.tile([P, N * PACK], BF16, name="g_grouped%d" % g, align_bytes=64) for g in range(ROW_PASSES)]
+        def unit_cols(g, s):
+            piece = [piece for piece in g_pieces if piece[0] == g and piece[1] <= s < piece[2]][0]
+            if piece not in g_grouped:
+                g_grouped[piece] = keep.tile([P, (piece[2] - piece[1]) * SLOT_BLOCK * PACK], BF16,
+                                             name=g_pieces[piece], align_bytes=64)
+            return g_grouped[piece][:, block(s - piece[1], SLOT_BLOCK * PACK)]
 
         def gradient_unit(g, s):
             bank = scores(g, s, v_q)
             nc.vector.tensor_tensor(
-                out=g_grouped[g][:, block(s, SLOT_BLOCK * PACK)].rearrange("p (c i t) -> p c t i", i=2, t=PACK),
+                out=unit_cols(g, s).rearrange("p (c i t) -> p c t i", i=2, t=PACK),
                 in0=slope[g][:, :, block(s)].rearrange("p t (c i) -> p c t i", i=2),
                 in1=bank[:].rearrange("p t (c i) -> p c t i", i=2),
                 op=ALU.mult)
 
         def quantise_g(g, lo, hi):
-            quantise(g_q[g], slice(lo * SLOT_BLOCK, hi * SLOT_BLOCK),
-                     g_grouped[g][:, lo * SLOT_BLOCK * PACK:hi * SLOT_BLOCK * PACK], E5M2)
+            quantise(g_q[g], slice(lo * SLOT_BLOCK, hi * SLOT_BLOCK), g_grouped[g, lo, hi][:], E5M2)
 
-        last = block(SLOT_BLOCKS - 1)
-        ready = (SLOT_BLOCKS - 1) * SLOT_BLOCK
-        nc.vector.memset(g_q[1][0][:, last], 0)
-        nc.vector.memset(g_q[1][1][:, last], 0)
-        zeros = keep.tile([P, SLOT_BLOCK], F32, name="zeros")
-        nc.vector.memset(zeros[:], 0.0)
+        m_grouped = {}
+        m_q = {}
 
-        for s in (0, 1, 3, 2):
-            gradient_unit(0, s)
-        gradient_unit(1, 0)
-        quantise_g(0, 0, 4)
-        gradient_unit(1, 1)
-        quantise_m(0, 0)
-        gradient_unit(1, 2)
-        quantise_g(1, 0, 2)
-        quantise_m(0, 1)
-        quantise_g(1, 2, 3)
-        early = next_bank([P, N])
-        for g in range(ROW_PASSES):
-            mx(early[:], m_q[0][g], slice(0, P), g_q[g], whole, E5M2, g == 0, g == ROW_PASSES - 1)
-        product(0, 0)
-        gradient_unit(1, 3)
-        quantise_m(1, 0)
-        quantise_g(1, 3, 4)
-        product(0, 1)
+        def group_m(copy, b, passes, slot):
+            grouped = keep.tile([P, len(passes), P * PACK], BF16, name=slot, align_bytes=64)
+            m_grouped[b, passes] = grouped
+            return [lambda k=k, g=g: interleave(copy, grouped[:, k, :], m_raw[b // 2][g][:, :, block(b % 2)])
+                    for k, g in enumerate(passes)]
+
+        def quantise_m(b, passes, slot):
+            width = len(passes) * P
+            pair = (keep.tile([P, width], U32, name=slot, align_bytes=64),
+                    keep.tile([P, width], U8, name="m_scales%d_%d" % (b, passes[0]), align_bytes=64))
+            quantise(pair, slice(0, width), m_grouped[b, passes][:].rearrange("p g c -> p (g c)"), E4M3)
+            for k, g in enumerate(passes):
+                m_q[b, g] = pair, block(k)
+
+        def product(dst, b, g):
+            pair, cols = m_q[b, g]
+            mx(dst[:], pair, cols, g_q[g], whole, E5M2, g == 0, g == ROW_PASSES - 1)
 
         def dense_copy(name, source):
-            dense = keep.tile([P, source.shape[1]], F32, name=name)
+            dense = keep.tile([P, source.shape[1]], F32, name=name, align_bytes=64)
             nc.scalar.copy(out=dense[:], in_=source)
             return dense
 
         def scatter(b, lo, hi, dense):
             nc.vector.tensor_copy(windows[b][:].indirect(offsets[:, lo // 16:hi // 16]), dense[:])
 
+        def store(b):
+            nc.sync.dma_start(out=out[block(b), :], in_=windows[b][:])
+
+        last = block(SLOT_BLOCKS - 1)
+        ready = (SLOT_BLOCKS - 1) * SLOT_BLOCK
+        nc.vector.memset(g_q[1][0][:, last], 0)
+        nc.vector.memset(g_q[1][1][:, last], 0)
+        zeros = keep.tile([P, SLOT_BLOCK], F32, name="zeros", align_bytes=64)
+        nc.vector.memset(zeros[:], 0.0)
+
+        both = (0, 1)
+        for b in range(2):
+            for cast in group_m(nc.scalar.copy, b, both, "m_grouped%d" % b):
+                cast()
+        group_m(nc.scalar.copy, 2, (0,), "m_grouped2")[0]()
+        for s in (0, 1, 3, 2):
+            gradient_unit(0, s)
+        gradient_unit(1, 0)
+        quantise_g(0, 0, 4)
+        gradient_unit(1, 1)
+        quantise_m(0, both, "m_codes0")
+        early = next_bank([P, N])
+        product(early, 0, 0)
+        product(acc[0], 0, 0)
+        gradient_unit(1, 2)
+        quantise_g(1, 0, 2)
+        quantise_g(1, 2, 3)
+        product(early, 0, 1)
+        gradient_unit(1, 3)
+        quantise_m(1, both, "g_grouped0")
+        quantise_g(1, 3, 4)
+        product(acc[0], 0, 1)
         scatter(0, 0, ready, dense_copy("dense_early", early[:, 0:ready]))
+        group_m(nc.vector.tensor_copy, 2, (1,), "m_grouped0")[0]()
+        quantise_m(2, (0,), "g_third")
         dense_last = dense_copy("dense_last", acc[0][:, last])
         nc.vector.tensor_tensor(windows[0][:].indirect(offsets[:, ready // 16:N // 16]), dense_last[:], zeros[:], ALU.add)
-        nc.sync.dma_start(out=out[block(0), :], in_=windows[0][:])
-        quantise_m(1, 1)
-        for b in range(1, D_BLOCKS):
+        store(0)
+
+        for g in range(ROW_PASSES):
+            product(acc[1], 1, g)
+        dense = dense_copy("dense_early", acc[1][:])
+        quantise_m(2, (1,), "m_codes2")
+        scatter(1, 0, N, dense)
+        store(1)
+        for cast in group_m(nc.scalar.copy, 3, both, "dense_last"):
+            cast()
+        quantise_m(3, both, "m_codes3")
+        for b in range(2, D_BLOCKS):
             for g in range(ROW_PASSES):
-                product(b, g)
-            if b + 1 < D_BLOCKS:
-                for g in range(ROW_PASSES):
-                    quantise_m(b + 1, g)
+                product(acc[b], b, g)
             scatter(b, 0, N, dense_copy("dense%d" % b, acc[b][:]))
-            nc.sync.dma_start(out=out[block(b), :], in_=windows[b][:])
+            store(b)

@@ -60,8 +60,10 @@ def tile_attend_ghv_nce_kernel(tc, xT, wT, vT, wt, xm, offs, out):
         x_raw = [keep.tile([P, PACK, K_PASS], F32, name="x_raw%d" % g) for g in range(ROW_PASSES)]
         m_raw = [[keep.tile([P, PACK, D // 2], F32, name="m_raw%d_%d" % (h, g)) for g in range(ROW_PASSES)]
                  for h in range(2)]
-        w_planes = [keep.tile([P, T], F32, name="w_plane%d" % j) for j in range(PACK)]
-        v_planes = [keep.tile([P, T], F32, name="v_plane%d" % j) for j in range(PACK)]
+        plane_loads = (slice(0, 2), slice(2, 3), slice(3, 4))
+        w_tiles = [keep.tile([P, js.stop - js.start, T], F32, name="w_from%d" % js.start) for js in plane_loads]
+        w_planes = [tile[:, k, :] for tile in w_tiles for k in range(tile.shape[1])]
+        v_planes = [keep.tile([P, T], F32, name="v_plane%d" % j)[:] for j in range(PACK)]
         wt_padded = keep.tile([P, ROW_PASSES, 2 * PACK], F32, name="wt_padded")
         wt_raw = wt_padded[:, :, 0:PACK]
         x_rows = xT[0].rearrange("(p j) r -> p j r", j=PACK)
@@ -70,14 +72,14 @@ def tile_attend_ghv_nce_kernel(tc, xT, wT, vT, wt, xm, offs, out):
         m_rows = xm[0].rearrange("(g p t) d -> g p t d", p=P, t=PACK)
 
         nc.scalar.dma_start(out=wt_raw, in_=wt[0].rearrange("(g p t) o -> p g (t o)", p=P, t=PACK))
-        nc.sync.dma_start(out=w_planes[0][:], in_=w_rows[:, 0, :])
+        nc.sync.dma_start(out=w_tiles[0][:], in_=w_rows[:, plane_loads[0], :])
         nc.sync.dma_start(offsets[:], offs)
-        for j in range(1, PACK):
-            nc.sync.dma_start(out=w_planes[j][:], in_=w_rows[:, j, :])
+        for tile, js in zip(w_tiles[1:], plane_loads[1:]):
+            nc.sync.dma_start(out=tile[:], in_=w_rows[:, js, :])
         for g in range(ROW_PASSES):
             nc.sync.dma_start(out=x_raw[g][:], in_=x_rows[:, :, block(g, K_PASS)])
         for j in range(PACK):
-            nc.sync.dma_start(out=v_planes[j][:], in_=v_rows[:, j, :])
+            nc.sync.dma_start(out=v_planes[j], in_=v_rows[:, j, :])
         for h in range(2):
             for g in range(ROW_PASSES):
                 nc.sync.dma_start(out=m_raw[h][g][:], in_=m_rows[g][:, :, block(h, D // 2)])
@@ -101,14 +103,14 @@ def tile_attend_ghv_nce_kernel(tc, xT, wT, vT, wt, xm, offs, out):
             for h in range(2):
                 target = grouped[h][:].rearrange("p (t m j) -> p m j t", t=2, j=PACK)
                 source = x_raw[g][:].rearrange("p j (m t) -> p m j t", t=PACK)[:, :, :, 2 * h:2 * h + 2]
-                for part, copy in enumerate(copies):
-                    cols = block(part, P // len(copies))
+                for part, copy in enumerate(copies[h]):
+                    cols = block(part, P // len(copies[h]))
                     copy(out=target[:, cols], in_=source[:, cols])
             for h in range(2):
                 quantise(x_q[g], block(h, 2 * P), grouped[h][:], E4M3)
 
         def gather(picked, planes, j, lo=0, hi=N):
-            nc.vector.tensor_copy(picked[:, j, lo:hi], planes[j][:].indirect(offsets[:, lo // 16:hi // 16]))
+            nc.vector.tensor_copy(picked[:, j, lo:hi], planes[j].indirect(offsets[:, lo // 16:hi // 16]))
 
         def last_plane(name, picked, planes, codes):
             def group(copy, s, slot):
@@ -160,8 +162,8 @@ def tile_attend_ghv_nce_kernel(tc, xT, wT, vT, wt, xm, offs, out):
         for j in range(PACK - 1):
             gather(w_picked, w_planes, j)
         last_plane("w", w_picked, w_planes, w_q)
-        prepare_x(0, (nc.scalar.copy, nc.vector.tensor_copy))
-        prepare_x(1, (nc.vector.tensor_copy,))
+        prepare_x(0, ((nc.scalar.copy,), (nc.scalar.copy, nc.vector.tensor_copy)))
+        prepare_x(1, ((nc.vector.tensor_copy,), (nc.vector.tensor_copy,)))
         for t in range(PACK):
             tanh_half(0, t)
         lower = slope[0][:, 0:2, :]
@@ -176,18 +178,20 @@ def tile_attend_ghv_nce_kernel(tc, xT, wT, vT, wt, xm, offs, out):
         tanh_half(1, 2)
         tanh_half(1, 3)
         square(slope[1][:, 2, :])
-        square(slope[1][:, 3, :])
-        gather(v_picked, v_planes, 1)
-        gather(v_picked, v_planes, 2)
+        for j in range(1, PACK - 1):
+            gather(v_picked, v_planes, j)
         last_plane("v", v_picked, v_planes, v_q)
-        wt_peak = keep.tile([P, PACK], F32, name="v_plane%d" % (PACK - 1))
-        nc.scalar.activation(out=wt_peak[:], in_=wt_raw[:, 1, :], func=ACT.Copy, scale=0.25)
+        late = keep.tile([P, N + PACK], F32, name="v_plane%d" % (PACK - 1))
+        last_square, wt_peak = late[:, 0:N], late[:, N:N + PACK]
+        nc.scalar.activation(out=wt_peak, in_=wt_raw[:, 1, :], func=ACT.Copy, scale=0.25)
+        nc.scalar.activation(out=last_square, in_=slope[1][:, PACK - 1, :], func=ACT.Square)
         for t in range(PACK):
-            nc.scalar.activation(out=slope[1][:, t, :], in_=slope[1][:, t, :], func=ACT.Identity,
+            squared = last_square if t == PACK - 1 else slope[1][:, t, :]
+            nc.scalar.activation(out=slope[1][:, t, :], in_=squared, func=ACT.Identity,
                                  scale=wt_quarter[:, 1, t:t + 1], bias=wt_peak[:, t:t + 1])
 
         acc = [out_psum.tile([P, N], F32, name="acc%d" % b) for b in range(D_BLOCKS)]
-        g_pieces = {(0, 0, 4): "g_grouped0", (1, 0, 2): "g_lower", (1, 2, 3): "g_third", (1, 3, 4): "m_grouped0"}
+        g_pieces = {(0, 0, 2): "g_grouped0", (0, 2, 4): "g_upper", (1, 0, 2): "g_lower", (1, 2, 3): "g_third", (1, 3, 4): "m_grouped0"}
         g_grouped = {}
 
         def unit_cols(g, s):
@@ -252,10 +256,12 @@ def tile_attend_ghv_nce_kernel(tc, xT, wT, vT, wt, xm, offs, out):
             for cast in group_m(nc.scalar.copy, b, both, "m_grouped%d" % b):
                 cast()
         group_m(nc.scalar.copy, 2, (0,), "m_grouped2")[0]()
-        for s in (0, 1, 3, 2):
+        for s in (0, 1, 3):
             gradient_unit(0, s)
+        quantise_g(0, 0, 2)
+        gradient_unit(0, 2)
         gradient_unit(1, 0)
-        quantise_g(0, 0, 4)
+        quantise_g(0, 2, 4)
         gradient_unit(1, 1)
         quantise_m(0, both, "m_codes0")
         early = next_bank([P, N])
@@ -266,7 +272,7 @@ def tile_attend_ghv_nce_kernel(tc, xT, wT, vT, wt, xm, offs, out):
         quantise_g(1, 2, 3)
         product(early, 0, 1)
         gradient_unit(1, 3)
-        quantise_m(1, both, "g_grouped0")
+        quantise_m(1, both, "g_upper")
         quantise_g(1, 3, 4)
         product(acc[0], 0, 1)
         scatter(0, 0, ready, dense_copy("dense_early", early[:, 0:ready]))

@@ -103,8 +103,7 @@ def tile_attend_ghv_nce_kernel(tc, xT, wT, vT, wt, xm, offs, out):
             for h in range(2):
                 target = grouped[h][:].rearrange("p (t m j) -> p m j t", t=2, j=PACK)
                 source = x_raw[g][:].rearrange("p j (m t) -> p m j t", t=PACK)[:, :, :, 2 * h:2 * h + 2]
-                for part, copy in enumerate(copies[h]):
-                    cols = block(part, P // len(copies[h]))
+                for copy, cols in copies[h]:
                     copy(out=target[:, cols], in_=source[:, cols])
             for h in range(2):
                 quantise(x_q[g], block(h, 2 * P), grouped[h][:], E4M3)
@@ -147,47 +146,55 @@ def tile_attend_ghv_nce_kernel(tc, xT, wT, vT, wt, xm, offs, out):
         v_picked = keep.tile([P, PACK, N], F32, name="v_picked")
         slope = [keep.tile([P, PACK, N], F32, name="slope%d" % g) for g in range(ROW_PASSES)]
 
-        def finish_slope(t):
-            nc.vector.tensor_scalar(out=slope[0][:, t, :], in0=slope[0][:, t, :], scalar1=1.0,
-                                    scalar2=wt_quarter[:, 0, t:t + 1], op0=ALU.subtract, op1=ALU.mult)
+        def finish_slope(g, t):
+            nc.vector.tensor_scalar(out=slope[g][:, t, :], in0=slope[g][:, t, :], scalar1=1.0,
+                                    scalar2=wt_quarter[:, g, t:t + 1], op0=ALU.subtract, op1=ALU.mult)
 
-        def tanh_half(g, t):
+        def tanh_half(g, t, target):
             bank = next_bank([P, N])
             mx(bank[:], x_q[g], block(t), w_q, whole, E4M3, True, True)
-            nc.scalar.activation(out=slope[g][:, t, :], in_=bank[:], func=ACT.Tanh, scale=0.5)
+            nc.scalar.activation(out=target, in_=bank[:], func=ACT.Tanh, scale=0.5)
 
-        def square(values):
-            nc.scalar.activation(out=values, in_=values, func=ACT.Square)
+        def square(target, values):
+            nc.scalar.activation(out=target, in_=values, func=ACT.Square)
 
         for j in range(PACK - 1):
             gather(w_picked, w_planes, j)
-        last_plane("w", w_picked, w_planes, w_q)
-        prepare_x(0, ((nc.scalar.copy,), (nc.scalar.copy, nc.vector.tensor_copy)))
-        prepare_x(1, ((nc.vector.tensor_copy,), (nc.vector.tensor_copy,)))
+        w_grouped = [keep.tile([P, HALF * PACK], BF16, name="w_grouped%d" % h, align_bytes=64) for h in range(2)]
+        for h in range(2):
+            gather(w_picked, w_planes, PACK - 1, h * HALF, (h + 1) * HALF)
+        for s, copy in enumerate((nc.scalar.copy, nc.vector.tensor_copy, nc.vector.tensor_copy, nc.scalar.copy)):
+            interleave(copy, w_grouped[s // 2][:, block(s % 2, SLOT_BLOCK * PACK)], w_picked[:, :, block(s)])
+        for h in range(2):
+            quantise(w_q, block(h, HALF), w_grouped[h][:], E4M3)
+        prepare_x(0, [((nc.scalar.copy, slice(0, cut)), (nc.vector.tensor_copy, slice(cut, P))) for cut in (96, 64)])
+        prepare_x(1, [((nc.vector.tensor_copy, slice(0, P)),)] * 2)
         for t in range(PACK):
-            tanh_half(0, t)
+            tanh_half(0, t, slope[0][:, t, :])
         lower = slope[0][:, 0:2, :]
         nc.vector.tensor_tensor(out=lower, in0=lower, in1=lower, op=ALU.mult)
-        square(slope[0][:, 2:4, :])
+        square(slope[0][:, 2:4, :], slope[0][:, 2:4, :])
         gather(v_picked, v_planes, 0)
         for t in range(PACK):
-            finish_slope(t)
-        tanh_half(1, 0)
-        tanh_half(1, 1)
-        square(slope[1][:, 0:2, :])
-        tanh_half(1, 2)
-        tanh_half(1, 3)
-        square(slope[1][:, 2, :])
+            finish_slope(0, t)
+        squared = keep.tile([P, 2, N], F32, name="squared")
+        for t in range(2):
+            tanh_half(1, t, slope[1][:, t, :])
+        for t in range(2, PACK):
+            staged = keep.tile([P, N], F32, name="staged")
+            tanh_half(1, t, staged[:])
+            if t == 2:
+                square(slope[1][:, 0:2, :], slope[1][:, 0:2, :])
+            square(squared[:, t - 2, :], staged[:])
         for j in range(1, PACK - 1):
             gather(v_picked, v_planes, j)
+        for t in range(2):
+            finish_slope(1, t)
         last_plane("v", v_picked, v_planes, v_q)
-        late = keep.tile([P, N + PACK], F32, name="v_plane%d" % (PACK - 1))
-        last_square, wt_peak = late[:, 0:N], late[:, N:N + PACK]
-        nc.scalar.activation(out=wt_peak, in_=wt_raw[:, 1, :], func=ACT.Copy, scale=0.25)
-        nc.scalar.activation(out=last_square, in_=slope[1][:, PACK - 1, :], func=ACT.Square)
-        for t in range(PACK):
-            squared = last_square if t == PACK - 1 else slope[1][:, t, :]
-            nc.scalar.activation(out=slope[1][:, t, :], in_=squared, func=ACT.Identity,
+        wt_peak = keep.tile([P, PACK], F32, name="v_plane%d" % (PACK - 1))
+        nc.scalar.activation(out=wt_peak[:], in_=wt_raw[:, 1, :], func=ACT.Copy, scale=0.25)
+        for t in range(2, PACK):
+            nc.scalar.activation(out=slope[1][:, t, :], in_=squared[:, t - 2, :], func=ACT.Identity,
                                  scale=wt_quarter[:, 1, t:t + 1], bias=wt_peak[:, t:t + 1])
 
         acc = [out_psum.tile([P, N], F32, name="acc%d" % b) for b in range(D_BLOCKS)]
@@ -229,9 +236,9 @@ def tile_attend_ghv_nce_kernel(tc, xT, wT, vT, wt, xm, offs, out):
             for k, g in enumerate(passes):
                 m_q[b, g] = pair, block(k)
 
-        def product(dst, b, g):
+        def product(dst, b, g, first=0):
             pair, cols = m_q[b, g]
-            mx(dst[:], pair, cols, g_q[g], whole, E5M2, g == 0, g == ROW_PASSES - 1)
+            mx(dst[:], pair, cols, g_q[g], whole, E5M2, g == first, g != first)
 
         def dense_copy(name, source):
             dense = keep.tile([P, source.shape[1]], F32, name=name, align_bytes=64)
@@ -282,8 +289,8 @@ def tile_attend_ghv_nce_kernel(tc, xT, wT, vT, wt, xm, offs, out):
         nc.vector.tensor_tensor(windows[0][:].indirect(offsets[:, ready // 16:N // 16]), dense_last[:], zeros[:], ALU.add)
         store(0)
 
-        for g in range(ROW_PASSES):
-            product(acc[1], 1, g)
+        for g in (1, 0):
+            product(acc[1], 1, g, first=1)
         dense = dense_copy("dense_early", acc[1][:])
         quantise_m(2, (1,), "m_codes2")
         scatter(1, 0, N, dense)

@@ -186,6 +186,9 @@ def tile_attend_ghv_nce_kernel(tc, xT, wT, vT, wt, xm, offs, out):
             if t == 2:
                 square(slope[1][:, 0:2, :], slope[1][:, 0:2, :])
             square(squared[:, t - 2, :], staged[:])
+        warm = unit_psum.tile([P, N], F32, name="bank%d" % (PACK - 1))
+        for t in range(PACK):
+            mx(warm[:], x_q[1], block(t), w_q, whole, E4M3, True, True)
         for j in range(1, PACK - 1):
             gather(v_picked, v_planes, j)
         for t in range(2):

@@ -58,8 +58,8 @@ def tile_attend_ghv_nce_kernel(tc, xT, wT, vT, wt, xm, offs, out):
 
         offsets = keep.tile([P, N // 16], U16, name="offsets")
         x_raw = [keep.tile([P, PACK, K_PASS], F32, name="x_raw%d" % g) for g in range(ROW_PASSES)]
-        m_raw = [[keep.tile([P, PACK, D // 2], F32, name="m_raw%d_%d" % (h, g)) for g in range(ROW_PASSES)]
-                 for h in range(2)]
+        m_raw = [[keep.tile([P, PACK, P], F32, name="m_raw%d_%d" % (b, g)) for g in range(ROW_PASSES)]
+                 for b in range(D_BLOCKS)]
         plane_loads = (slice(0, 2), slice(2, 3), slice(3, 4))
         w_tiles = [keep.tile([P, js.stop - js.start, T], F32, name="w_from%d" % js.start) for js in plane_loads]
         w_planes = [tile[:, k, :] for tile in w_tiles for k in range(tile.shape[1])]
@@ -80,9 +80,9 @@ def tile_attend_ghv_nce_kernel(tc, xT, wT, vT, wt, xm, offs, out):
             nc.sync.dma_start(out=x_raw[g][:], in_=x_rows[:, :, block(g, K_PASS)])
         for j in range(PACK):
             nc.sync.dma_start(out=v_planes[j], in_=v_rows[:, j, :])
-        for h in range(2):
+        for b in range(D_BLOCKS):
             for g in range(ROW_PASSES):
-                nc.sync.dma_start(out=m_raw[h][g][:], in_=m_rows[g][:, :, block(h, D // 2)])
+                nc.sync.dma_start(out=m_raw[b][g][:], in_=m_rows[g][:, :, block(b)])
 
         windows = [keep.tile([P, T], F32, name="window%d" % b) for b in range(D_BLOCKS)]
         for b in range(D_BLOCKS):
@@ -93,7 +93,7 @@ def tile_attend_ghv_nce_kernel(tc, xT, wT, vT, wt, xm, offs, out):
         nc.vector.tensor_scalar(out=wt_quarter[:], in0=wt_raw, scalar1=-0.25, scalar2=None, op0=ALU.mult)
 
         x_q = [quantised("x%d" % g, K_PASS) for g in range(ROW_PASSES)]
-        g_q = [quantised("g%d" % g, N) for g in range(ROW_PASSES)]
+        g_q = [quantised("g%d" % g, SLOT_BLOCK + N) for g in range(ROW_PASSES)]
         w_q = quantised("w", N)
         v_q = quantised("v", N)
 
@@ -130,13 +130,15 @@ def tile_attend_ghv_nce_kernel(tc, xT, wT, vT, wt, xm, offs, out):
 
         banks_taken = []
 
-        def next_bank(shape):
-            bank = unit_psum.tile(shape, F32, name="bank%d" % (len(banks_taken) % PACK))
+        def next_bank(shape, ring):
+            bank = unit_psum.tile(shape, F32, name="bank%d" % (len(banks_taken) % ring))
             banks_taken.append(bank)
             return bank
 
+        unit_banks = [0, 1, 2, 3, 0, 1, 0, 1]
+
         def scores(g, s, table):
-            bank = next_bank([P, PACK, SLOT_BLOCK])
+            bank = unit_psum.tile([P, PACK, SLOT_BLOCK], F32, name="bank%d" % unit_banks.pop(0))
             for t in range(PACK):
                 mx(bank[:, t, :], x_q[g], block(t), table, block(s), E4M3, True, True)
             return bank
@@ -151,7 +153,7 @@ def tile_attend_ghv_nce_kernel(tc, xT, wT, vT, wt, xm, offs, out):
                                     scalar2=wt_quarter[:, g, t:t + 1], op0=ALU.subtract, op1=ALU.mult)
 
         def tanh_half(g, t, target):
-            bank = next_bank([P, N])
+            bank = next_bank([P, N], 4)
             mx(bank[:], x_q[g], block(t), w_q, whole, E4M3, True, True)
             nc.scalar.activation(out=target, in_=bank[:], func=ACT.Tanh, scale=0.5)
 
@@ -201,7 +203,8 @@ def tile_attend_ghv_nce_kernel(tc, xT, wT, vT, wt, xm, offs, out):
                                  scale=wt_quarter[:, 1, t:t + 1], bias=wt_peak[:, t:t + 1])
 
         acc = [out_psum.tile([P, N], F32, name="acc%d" % b) for b in range(D_BLOCKS)]
-        g_pieces = {(0, 0, 2): "g_grouped0", (0, 2, 4): "g_upper", (1, 0, 2): "g_lower", (1, 2, 3): "g_third", (1, 3, 4): "m_grouped0"}
+        g_pieces = {(0, 0, 2): "g_lower0", (0, 2, 3): "g_third0", (0, 3, 4): "m_grouped0_0",
+                    (1, 0, 2): "g_lower1", (1, 2, 3): "g_third1", (1, 3, 4): "g_third1"}
         g_grouped = {}
 
         def unit_cols(g, s):
@@ -219,8 +222,16 @@ def tile_attend_ghv_nce_kernel(tc, xT, wT, vT, wt, xm, offs, out):
                 in1=bank[:].rearrange("p t (c i) -> p c t i", i=2),
                 op=ALU.mult)
 
+        def gradient_unit_gpsimd(g, s):
+            bank = scores(g, s, v_q)
+            av = keep.tile([P, SLOT_BLOCK, PACK], F32, name="av", align_bytes=64)
+            nc.scalar.copy(out=av[:], in_=bank[:].rearrange("p t c -> p c t"))
+            nc.gpsimd.tensor_tensor(
+                out=unit_cols(g, s).rearrange("p (c t) -> p c t", t=PACK),
+                in0=av[:], in1=slope[g][:, :, block(s)].rearrange("p t c -> p c t"), op=ALU.mult)
+
         def quantise_g(g, lo, hi):
-            quantise(g_q[g], slice(lo * SLOT_BLOCK, hi * SLOT_BLOCK), g_grouped[g, lo, hi][:], E5M2)
+            quantise(g_q[g], slice((lo + 1) * SLOT_BLOCK, (hi + 1) * SLOT_BLOCK), g_grouped[g, lo, hi][:], E5M2)
 
         m_grouped = {}
         m_q = {}
@@ -228,7 +239,7 @@ def tile_attend_ghv_nce_kernel(tc, xT, wT, vT, wt, xm, offs, out):
         def group_m(copy, b, passes, slot):
             grouped = keep.tile([P, len(passes), P * PACK], BF16, name=slot, align_bytes=64)
             m_grouped[b, passes] = grouped
-            return [lambda k=k, g=g: interleave(copy, grouped[:, k, :], m_raw[b // 2][g][:, :, block(b % 2)])
+            return [lambda k=k, g=g: interleave(copy, grouped[:, k, :], m_raw[b][g][:])
                     for k, g in enumerate(passes)]
 
         def quantise_m(b, passes, slot):
@@ -239,9 +250,9 @@ def tile_attend_ghv_nce_kernel(tc, xT, wT, vT, wt, xm, offs, out):
             for k, g in enumerate(passes):
                 m_q[b, g] = pair, block(k)
 
-        def product(dst, b, g, first=0):
+        def product(dst, b, g, first=0, start=SLOT_BLOCK):
             pair, cols = m_q[b, g]
-            mx(dst[:], pair, cols, g_q[g], whole, E5M2, g == first, g != first)
+            mx(dst[:], pair, cols, g_q[g], slice(start, start + N), E5M2, g == first, g != first)
 
         def dense_copy(name, source):
             dense = keep.tile([P, source.shape[1]], F32, name=name, align_bytes=64)
@@ -256,38 +267,40 @@ def tile_attend_ghv_nce_kernel(tc, xT, wT, vT, wt, xm, offs, out):
 
         last = block(SLOT_BLOCKS - 1)
         ready = (SLOT_BLOCKS - 1) * SLOT_BLOCK
-        nc.vector.memset(g_q[1][0][:, last], 0)
-        nc.vector.memset(g_q[1][1][:, last], 0)
+        for codes, scales in g_q:
+            nc.vector.memset(codes[:, block(0)], 0)
+            nc.vector.memset(scales[:, block(0)], 0)
         zeros = keep.tile([P, SLOT_BLOCK], F32, name="zeros", align_bytes=64)
         nc.vector.memset(zeros[:], 0.0)
 
         both = (0, 1)
-        for b in range(2):
-            for cast in group_m(nc.scalar.copy, b, both, "m_grouped%d" % b):
+        gradient_unit(0, 0)
+        gradient_unit(0, 1)
+        gradient_unit_gpsimd(1, 1)
+        for b, passes in ((0, both), (1, (1,)), (1, (0,)), (2, both)):
+            for cast in group_m(nc.scalar.copy, b, passes, "m_grouped%d_%d" % (b, passes[0])):
                 cast()
-        group_m(nc.scalar.copy, 2, (0,), "m_grouped2")[0]()
-        for s in (0, 1, 3):
-            gradient_unit(0, s)
-        quantise_g(0, 0, 2)
         gradient_unit(0, 2)
-        gradient_unit(1, 0)
-        quantise_g(0, 2, 4)
-        gradient_unit(1, 1)
-        quantise_m(0, both, "m_codes0")
-        early = next_bank([P, N])
-        product(early, 0, 0)
-        product(acc[0], 0, 0)
         gradient_unit(1, 2)
-        quantise_g(1, 0, 2)
+        gradient_unit(1, 0)
+        quantise_g(0, 0, 2)
+        quantise_m(0, both, "m_codes0")
+        quantise_g(0, 2, 3)
         quantise_g(1, 2, 3)
-        product(early, 0, 1)
-        gradient_unit(1, 3)
-        quantise_m(1, both, "g_upper")
+        quantise_g(1, 0, 2)
+        early = unit_psum.tile([P, N], F32, name="bank3")
+        for g in both:
+            product(early, 0, g, start=0)
+        for g in both:
+            gradient_unit(g, 3)
+        quantise_g(0, 3, 4)
+        product(acc[0], 0, 0)
+        quantise_m(1, (1,), "g_lower1")
         quantise_g(1, 3, 4)
         product(acc[0], 0, 1)
-        scatter(0, 0, ready, dense_copy("dense_early", early[:, 0:ready]))
-        group_m(nc.vector.tensor_copy, 2, (1,), "m_grouped0")[0]()
-        quantise_m(2, (0,), "g_third")
+        quantise_m(1, (0,), "g_third1")
+        dense_early = dense_copy("dense_early", early[:, SLOT_BLOCK:N])
+        scatter(0, 0, ready, dense_early)
         dense_last = dense_copy("dense_last", acc[0][:, last])
         nc.vector.tensor_tensor(windows[0][:].indirect(offsets[:, ready // 16:N // 16]), dense_last[:], zeros[:], ALU.add)
         store(0)
@@ -295,7 +308,7 @@ def tile_attend_ghv_nce_kernel(tc, xT, wT, vT, wt, xm, offs, out):
         for g in (1, 0):
             product(acc[1], 1, g, first=1)
         dense = dense_copy("dense_early", acc[1][:])
-        quantise_m(2, (1,), "m_codes2")
+        quantise_m(2, both, "zeros")
         scatter(1, 0, N, dense)
         store(1)
         for cast in group_m(nc.scalar.copy, 3, both, "dense_last"):

@@ -179,7 +179,7 @@ def tile_attend_ghv_nce_kernel(tc, xT, wT, vT, wt, xm, offs, out):
         gather(v_picked, v_planes, 0)
         for t in range(PACK):
             finish_slope(0, t)
-        squared = keep.tile([P, 2, N], F32, name="squared")
+        squared = keep.tile([P, N], F32, name="squared")
         for t in range(2):
             tanh_half(1, t, slope[1][:, t, :])
         for t in range(2, PACK):
@@ -187,20 +187,19 @@ def tile_attend_ghv_nce_kernel(tc, xT, wT, vT, wt, xm, offs, out):
             tanh_half(1, t, staged[:])
             if t == 2:
                 square(slope[1][:, 0:2, :], slope[1][:, 0:2, :])
-            square(squared[:, t - 2, :], staged[:])
+            square(slope[1][:, t, :] if t == 2 else squared[:], staged[:])
         warm = unit_psum.tile([P, N], F32, name="bank%d" % (PACK - 1))
         for t in range(PACK):
             mx(warm[:], x_q[1], block(t), w_q, whole, E4M3, True, True)
         for j in range(1, PACK - 1):
             gather(v_picked, v_planes, j)
-        for t in range(2):
+        for t in range(PACK - 1):
             finish_slope(1, t)
         last_plane("v", v_picked, v_planes, v_q)
         wt_peak = keep.tile([P, PACK], F32, name="v_plane%d" % (PACK - 1))
         nc.scalar.activation(out=wt_peak[:], in_=wt_raw[:, 1, :], func=ACT.Copy, scale=0.25)
-        for t in range(2, PACK):
-            nc.scalar.activation(out=slope[1][:, t, :], in_=squared[:, t - 2, :], func=ACT.Identity,
-                                 scale=wt_quarter[:, 1, t:t + 1], bias=wt_peak[:, t:t + 1])
+        nc.scalar.activation(out=slope[1][:, PACK - 1, :], in_=squared[:], func=ACT.Identity,
+                             scale=wt_quarter[:, 1, PACK - 1:PACK], bias=wt_peak[:, PACK - 1:PACK])
 
         acc = [out_psum.tile([P, N], F32, name="acc%d" % b) for b in range(D_BLOCKS)]
         g_pieces = {(0, 0, 2): "g_lower0", (0, 2, 3): "g_third0", (0, 3, 4): "m_grouped0_0",

@@ -196,10 +196,10 @@ def tile_attend_ghv_nce_kernel(tc, xT, wT, vT, wt, xm, offs, out):
         for t in range(PACK - 1):
             finish_slope(1, t)
         last_plane("v", v_picked, v_planes, v_q)
-        wt_peak = keep.tile([P, PACK], F32, name="v_plane%d" % (PACK - 1))
-        nc.scalar.activation(out=wt_peak[:], in_=wt_raw[:, 1, :], func=ACT.Copy, scale=0.25)
+        wt_peak = keep.tile([P, 1], F32, name="v_plane%d" % (PACK - 1))
+        nc.scalar.activation(out=wt_peak[:], in_=wt_raw[:, 1, PACK - 1:PACK], func=ACT.Copy, scale=0.25)
         nc.scalar.activation(out=slope[1][:, PACK - 1, :], in_=squared[:], func=ACT.Identity,
-                             scale=wt_quarter[:, 1, PACK - 1:PACK], bias=wt_peak[:, PACK - 1:PACK])
+                             scale=wt_quarter[:, 1, PACK - 1:PACK], bias=wt_peak[:])
 
         acc = [out_psum.tile([P, N], F32, name="acc%d" % b) for b in range(D_BLOCKS)]
         g_pieces = {(0, 0, 2): "g_lower0", (0, 2, 3): "g_third0", (0, 3, 4): "m_grouped0_0",
@@ -216,9 +216,9 @@ def tile_attend_ghv_nce_kernel(tc, xT, wT, vT, wt, xm, offs, out):
         def gradient_unit(g, s):
             bank = scores(g, s, v_q)
             nc.vector.tensor_tensor(
-                out=unit_cols(g, s).rearrange("p (c i t) -> p c t i", i=2, t=PACK),
-                in0=slope[g][:, :, block(s)].rearrange("p t (c i) -> p c t i", i=2),
-                in1=bank[:].rearrange("p t (c i) -> p c t i", i=2),
+                out=unit_cols(g, s).rearrange("p (c i t) -> p c t i", i=4, t=PACK),
+                in0=slope[g][:, :, block(s)].rearrange("p t (c i) -> p c t i", i=4),
+                in1=bank[:].rearrange("p t (c i) -> p c t i", i=4),
                 op=ALU.mult)
 
         def gradient_unit_gpsimd(g, s):

@@ -95,7 +95,7 @@ def tile_attend_ghv_nce_kernel(tc, xT, wT, vT, wt, xm, offs, out):
         x_q = [quantised("x%d" % g, K_PASS) for g in range(ROW_PASSES)]
         g_q = [quantised("g%d" % g, SLOT_BLOCK + N) for g in range(ROW_PASSES)]
         w_q = quantised("w", N)
-        v_q = quantised("v", N)
+        v_q = [quantised("v%d" % s, SLOT_BLOCK) for s in range(SLOT_BLOCKS)]
 
         def prepare_x(g, copies):
             grouped = [keep.tile([P, 2 * P * PACK], BF16, name="x_grouped%d_%d" % (g, h), align_bytes=64)
@@ -111,22 +111,27 @@ def tile_attend_ghv_nce_kernel(tc, xT, wT, vT, wt, xm, offs, out):
         def gather(picked, planes, j, lo=0, hi=N):
             nc.vector.tensor_copy(picked[:, j, lo:hi], planes[j].indirect(offsets[:, lo // 16:hi // 16]))
 
-        def last_plane(name, picked, planes, codes):
-            def group(copy, s, slot):
-                grouped = keep.tile([P, SLOT_BLOCK * PACK], BF16, name="%s_grouped%d" % (name, slot), align_bytes=64)
-                interleave(copy, grouped[:], picked[:, :, block(s)])
-                return grouped
+        v_grouped = [keep.tile([P, SLOT_BLOCK, PACK], BF16, name="v_grouped%d" % s, align_bytes=64)
+                     for s in range(SLOT_BLOCKS)]
+
+        def fill_pair(copy, picked, s, first):
+            copy(out=v_grouped[s][:, :, first:first + 2],
+                 in_=picked[:, first:first + 2, block(s)].rearrange("p t c -> p c t"))
+
+        def last_plane(picked, planes, codes):
+            def quantise_block(s):
+                quantise(codes[s], block(0), v_grouped[s][:].rearrange("p c t -> p (c t)"), E4M3)
 
             gather(picked, planes, PACK - 1, 0, HALF)
-            first = group(nc.scalar.copy, 0, 0)
+            fill_pair(nc.scalar.copy, picked, 0, 2)
             gather(picked, planes, PACK - 1, HALF, N)
-            last = group(nc.scalar.copy, 3, 3)
-            second = group(nc.vector.tensor_copy, 1, 1)
-            quantise(codes, block(0), first[:], E4M3)
-            quantise(codes, block(1), second[:], E4M3)
-            third = group(nc.vector.tensor_copy, 2, 0)
-            quantise(codes, block(3), last[:], E4M3)
-            quantise(codes, block(2), third[:], E4M3)
+            fill_pair(nc.scalar.copy, picked, 3, 2)
+            fill_pair(nc.vector.tensor_copy, picked, 1, 2)
+            quantise_block(0)
+            quantise_block(1)
+            fill_pair(nc.vector.tensor_copy, picked, 2, 2)
+            quantise_block(3)
+            quantise_block(2)
 
         banks_taken = []
 
@@ -140,7 +145,7 @@ def tile_attend_ghv_nce_kernel(tc, xT, wT, vT, wt, xm, offs, out):
         def scores(g, s, table):
             bank = unit_psum.tile([P, PACK, SLOT_BLOCK], F32, name="bank%d" % unit_banks.pop(0))
             for t in range(PACK):
-                mx(bank[:, t, :], x_q[g], block(t), table, block(s), E4M3, True, True)
+                mx(bank[:, t, :], x_q[g], block(t), table[s], block(0), E4M3, True, True)
             return bank
 
         whole = slice(0, N)
@@ -191,18 +196,20 @@ def tile_attend_ghv_nce_kernel(tc, xT, wT, vT, wt, xm, offs, out):
         warm = unit_psum.tile([P, N], F32, name="bank%d" % (PACK - 1))
         for t in range(PACK):
             mx(warm[:], x_q[1], block(t), w_q, whole, E4M3, True, True)
-        for j in range(1, PACK - 1):
-            gather(v_picked, v_planes, j)
+        gather(v_picked, v_planes, 1)
+        for s in range(SLOT_BLOCKS):
+            fill_pair(nc.vector.tensor_copy, v_picked, s, 0)
+        gather(v_picked, v_planes, 2)
         for t in range(PACK - 1):
             finish_slope(1, t)
-        last_plane("v", v_picked, v_planes, v_q)
+        last_plane(v_picked, v_planes, v_q)
         wt_peak = keep.tile([P, 1], F32, name="v_plane%d" % (PACK - 1))
         nc.scalar.activation(out=wt_peak[:], in_=wt_raw[:, 1, PACK - 1:PACK], func=ACT.Copy, scale=0.25)
         nc.scalar.activation(out=slope[1][:, PACK - 1, :], in_=squared[:], func=ACT.Identity,
                              scale=wt_quarter[:, 1, PACK - 1:PACK], bias=wt_peak[:])
 
         acc = [out_psum.tile([P, N], F32, name="acc%d" % b) for b in range(D_BLOCKS)]
-        g_pieces = {(0, 0, 2): "g_lower0", (0, 2, 3): "g_third0", (0, 3, 4): "m_grouped0_0",
+        g_pieces = {(0, 0, 2): "g_lower0", (0, 2, 3): "g_third0", (0, 3, 4): "v1_codes",
                     (1, 0, 2): "g_lower1", (1, 2, 3): "g_third1", (1, 3, 4): "g_third1"}
         g_grouped = {}
 
@@ -276,12 +283,16 @@ def tile_attend_ghv_nce_kernel(tc, xT, wT, vT, wt, xm, offs, out):
         gradient_unit(0, 0)
         gradient_unit(0, 1)
         gradient_unit_gpsimd(1, 1)
-        for b, passes in ((0, both), (1, (1,)), (1, (0,)), (2, both)):
-            for cast in group_m(nc.scalar.copy, b, passes, "m_grouped%d_%d" % (b, passes[0])):
-                cast()
+        for cast in group_m(nc.scalar.copy, 0, both, "v1_codes"):
+            cast()
         gradient_unit(0, 2)
         gradient_unit(1, 2)
         gradient_unit(1, 0)
+        for passes, slot in (((1,), "v2_codes"), ((0,), "v0_codes")):
+            for cast in group_m(nc.scalar.copy, 1, passes, slot):
+                cast()
+        for cast in group_m(nc.scalar.copy, 2, both, "av"):
+            cast()
         quantise_g(0, 0, 2)
         quantise_m(0, both, "m_codes0")
         quantise_g(0, 2, 3)

@@ -1,6 +1,7 @@
 from contextlib import ExitStack
 
 import concourse.mybir as mybir
+from concourse.masks import make_identity
 
 D, R, T, N = 512, 1024, 2048, 512
 FLOPS = 3 * 2 * R * D * N
@@ -64,16 +65,18 @@ def tile_attend_ghv_nce_kernel(tc, xT, wT, vT, wt, xm, offs, out):
         w_tiles = [keep.tile([P, js.stop - js.start, T], F32, name="w_from%d" % js.start) for js in plane_loads]
         w_planes = [tile[:, k, :] for tile in w_tiles for k in range(tile.shape[1])]
         v_planes = [keep.tile([P, T], F32, name="v_plane%d" % j)[:] for j in range(PACK)]
-        wt_padded = keep.tile([P, ROW_PASSES, 2 * PACK], F32, name="wt_padded")
-        wt_raw = wt_padded[:, :, 0:PACK]
+        wt_rows = keep.tile([P, K_PASS], F32, name="wt_rows")
+        identity = keep.tile([P, P], F32, name="identity")
+        nc.gpsimd.memset(wt_rows[:], 0.0)
+        make_identity(nc, identity[:])
         x_rows = xT[0].rearrange("(p j) r -> p j r", j=PACK)
         w_rows = wT.rearrange("(p j) c -> p j c", j=PACK)
         v_rows = vT.rearrange("(p j) c -> p j c", j=PACK)
         m_rows = xm[0].rearrange("(g p t) d -> g p t d", p=P, t=PACK)
 
-        nc.scalar.dma_start(out=wt_raw, in_=wt[0].rearrange("(g p t) o -> p g (t o)", p=P, t=PACK))
         nc.sync.dma_start(out=w_tiles[0][:], in_=w_rows[:, plane_loads[0], :])
         nc.sync.dma_start(offsets[:], offs)
+        nc.sync.dma_start(out=wt_rows[0:ROW_PASSES, :], in_=wt[0].rearrange("(g k) o -> g (k o)", g=ROW_PASSES))
         for tile, js in zip(w_tiles[1:], plane_loads[1:]):
             nc.sync.dma_start(out=tile[:], in_=w_rows[:, js, :])
         for g in range(ROW_PASSES):
@@ -90,7 +93,11 @@ def tile_attend_ghv_nce_kernel(tc, xT, wT, vT, wt, xm, offs, out):
             engine.memset(windows[b][:].bitcast(I32), 0)
 
         wt_quarter = keep.tile([P, ROW_PASSES, PACK], F32, name="wt_quarter")
-        nc.vector.tensor_scalar(out=wt_quarter[:], in0=wt_raw, scalar1=-0.25, scalar2=None, op0=ALU.mult)
+        wt_turned = unit_psum.tile([P, PACK, P], F32, name="bank0")
+        for t in range(PACK):
+            nc.tensor.transpose(wt_turned[:, t, :], wt_rows[:, t::PACK], identity[:])
+        nc.scalar.activation(out=wt_quarter[:], in_=wt_turned[:, :, 0:ROW_PASSES].rearrange("p t g -> p g t"),
+                             func=ACT.Copy, scale=-0.25)
 
         x_q = [quantised("x%d" % g, K_PASS) for g in range(ROW_PASSES)]
         g_q = [quantised("g%d" % g, SLOT_BLOCK + N) for g in range(ROW_PASSES)]
@@ -204,7 +211,7 @@ def tile_attend_ghv_nce_kernel(tc, xT, wT, vT, wt, xm, offs, out):
             finish_slope(1, t)
         last_plane(v_picked, v_planes, v_q)
         wt_peak = keep.tile([P, 1], F32, name="v_plane%d" % (PACK - 1))
-        nc.scalar.activation(out=wt_peak[:], in_=wt_raw[:, 1, PACK - 1:PACK], func=ACT.Copy, scale=0.25)
+        nc.scalar.activation(out=wt_peak[:], in_=wt_quarter[:, 1, PACK - 1:PACK], func=ACT.Copy, scale=-1.0)
         nc.scalar.activation(out=slope[1][:, PACK - 1, :], in_=squared[:], func=ACT.Identity,
                              scale=wt_quarter[:, 1, PACK - 1:PACK], bias=wt_peak[:])
 

@@ -25,19 +25,27 @@ SLOT_BLOCK = 128
 SLOT_BLOCKS = N // SLOT_BLOCK
 D_BLOCKS = D // P
 HALF = N // 2
+SHARED_SLOTS = 64
 
 
 def tile_attend_ghv_nce_kernel(tc, xT, wT, vT, wt, xm, offs, out):
     nc = tc.nc
     with ExitStack() as ctx:
         keep = ctx.enter_context(tc.tile_pool(name="keep", bufs=1))
-        unit_psum = ctx.enter_context(tc.psum_pool(name="unit_psum", bufs=1))
-        out_psum = ctx.enter_context(tc.psum_pool(name="out_psum", bufs=1))
+        psum = ctx.enter_context(tc.psum_pool(name="psum", bufs=1))
+
+        def block(index, width=P):
+            return slice(index * width, (index + 1) * width)
+
+        def bank(number, shape):
+            return psum.tile(shape, F32, name="bank%d" % number)
+
+        def words(name, width):
+            return keep.tile([P, width], U32, name=name, align_bytes=64)
 
         def quantised(name, width):
-            codes = keep.tile([P, width], U32, name=name + "_codes", align_bytes=64)
-            scales = keep.tile([P, width], U8, name=name + "_scales", align_bytes=64)
-            return codes, scales
+            return (words(name + "_codes", width)[:],
+                    keep.tile([P, width], U8, name=name + "_scales", align_bytes=64)[:])
 
         def quantise(pair, cols, grouped, fmt):
             nc.vector.quantize_mx(out=pair[0][:, cols].bitcast(fmt), scales=pair[1][:, cols], in_=grouped)
@@ -54,8 +62,8 @@ def tile_attend_ghv_nce_kernel(tc, xT, wT, vT, wt, xm, offs, out):
             copy(out=grouped.rearrange("p (c i t) -> p c t i", i=2, t=PACK),
                  in_=planes.rearrange("p t (c i) -> p c t i", i=2))
 
-        def block(index, width=P):
-            return slice(index * width, (index + 1) * width)
+        def listed(lo, hi):
+            return offsets[:, lo // 16:hi // 16]
 
         offsets = keep.tile([P, N // 16], U16, name="offsets")
         x_raw = [keep.tile([P, PACK, K_PASS], F32, name="x_raw%d" % g) for g in range(ROW_PASSES)]
@@ -93,14 +101,15 @@ def tile_attend_ghv_nce_kernel(tc, xT, wT, vT, wt, xm, offs, out):
             engine.memset(windows[b][:].bitcast(I32), 0)
 
         wt_quarter = keep.tile([P, ROW_PASSES, PACK], F32, name="wt_quarter")
-        wt_turned = unit_psum.tile([P, PACK, P], F32, name="bank0")
+        wt_peak = keep.tile([P, 1], F32, name="wt_peak")
+        wt_turned = bank(4, [P, PACK, P])
         for t in range(PACK):
             nc.tensor.transpose(wt_turned[:, t, :], wt_rows[:, t::PACK], identity[:])
         nc.scalar.activation(out=wt_quarter[:], in_=wt_turned[:, :, 0:ROW_PASSES].rearrange("p t g -> p g t"),
                              func=ACT.Copy, scale=-0.25)
+        nc.scalar.activation(out=wt_peak[:], in_=wt_turned[:, PACK - 1, 1:2], func=ACT.Copy, scale=0.25)
 
         x_q = [quantised("x%d" % g, K_PASS) for g in range(ROW_PASSES)]
-        g_q = [quantised("g%d" % g, SLOT_BLOCK + N) for g in range(ROW_PASSES)]
         w_q = quantised("w", N)
         v_q = [quantised("v%d" % s, SLOT_BLOCK) for s in range(SLOT_BLOCKS)]
 
@@ -116,44 +125,17 @@ def tile_attend_ghv_nce_kernel(tc, xT, wT, vT, wt, xm, offs, out):
                 quantise(x_q[g], block(h, 2 * P), grouped[h][:], E4M3)
 
         def gather(picked, planes, j, lo=0, hi=N):
-            nc.vector.tensor_copy(picked[:, j, lo:hi], planes[j].indirect(offsets[:, lo // 16:hi // 16]))
+            nc.vector.tensor_copy(picked[:, j, lo:hi], planes[j].indirect(listed(lo, hi)))
 
         v_grouped = [keep.tile([P, SLOT_BLOCK, PACK], BF16, name="v_grouped%d" % s, align_bytes=64)
                      for s in range(SLOT_BLOCKS)]
 
-        def fill_pair(copy, picked, s, first):
+        def fill_pair(copy, s, first):
             copy(out=v_grouped[s][:, :, first:first + 2],
-                 in_=picked[:, first:first + 2, block(s)].rearrange("p t c -> p c t"))
+                 in_=v_picked[:, first:first + 2, block(s)].rearrange("p t c -> p c t"))
 
-        def last_plane(picked, planes, codes):
-            def quantise_block(s):
-                quantise(codes[s], block(0), v_grouped[s][:].rearrange("p c t -> p (c t)"), E4M3)
-
-            gather(picked, planes, PACK - 1, 0, HALF)
-            fill_pair(nc.scalar.copy, picked, 0, 2)
-            gather(picked, planes, PACK - 1, HALF, N)
-            fill_pair(nc.scalar.copy, picked, 3, 2)
-            fill_pair(nc.vector.tensor_copy, picked, 1, 2)
-            quantise_block(0)
-            quantise_block(1)
-            fill_pair(nc.vector.tensor_copy, picked, 2, 2)
-            quantise_block(3)
-            quantise_block(2)
-
-        banks_taken = []
-
-        def next_bank(shape, ring):
-            bank = unit_psum.tile(shape, F32, name="bank%d" % (len(banks_taken) % ring))
-            banks_taken.append(bank)
-            return bank
-
-        unit_banks = [0, 1, 2, 3, 0, 1, 0, 1]
-
-        def scores(g, s, table):
-            bank = unit_psum.tile([P, PACK, SLOT_BLOCK], F32, name="bank%d" % unit_banks.pop(0))
-            for t in range(PACK):
-                mx(bank[:, t, :], x_q[g], block(t), table[s], block(0), E4M3, True, True)
-            return bank
+        def quantise_v(s):
+            quantise(v_q[s], block(0), v_grouped[s][:].rearrange("p c t -> p (c t)"), E4M3)
 
         whole = slice(0, N)
         w_picked = keep.tile([P, PACK, N], F32, name="w_picked")
@@ -165,9 +147,9 @@ def tile_attend_ghv_nce_kernel(tc, xT, wT, vT, wt, xm, offs, out):
                                     scalar2=wt_quarter[:, g, t:t + 1], op0=ALU.subtract, op1=ALU.mult)
 
         def tanh_half(g, t, target):
-            bank = next_bank([P, N], 4)
-            mx(bank[:], x_q[g], block(t), w_q, whole, E4M3, True, True)
-            nc.scalar.activation(out=target, in_=bank[:], func=ACT.Tanh, scale=0.5)
+            scores = bank(t, [P, N])
+            mx(scores[:], x_q[g], block(t), w_q, whole, E4M3, True, True)
+            nc.scalar.activation(out=target, in_=scores[:], func=ACT.Tanh, scale=0.5)
 
         def square(target, values):
             nc.scalar.activation(out=target, in_=values, func=ACT.Square)
@@ -191,148 +173,137 @@ def tile_attend_ghv_nce_kernel(tc, xT, wT, vT, wt, xm, offs, out):
         gather(v_picked, v_planes, 0)
         for t in range(PACK):
             finish_slope(0, t)
-        squared = keep.tile([P, N], F32, name="squared")
-        for t in range(2):
+        for t in range(PACK - 1):
             tanh_half(1, t, slope[1][:, t, :])
-        for t in range(2, PACK):
-            staged = keep.tile([P, N], F32, name="staged")
-            tanh_half(1, t, staged[:])
-            if t == 2:
-                square(slope[1][:, 0:2, :], slope[1][:, 0:2, :])
-            square(slope[1][:, t, :] if t == 2 else squared[:], staged[:])
-        warm = unit_psum.tile([P, N], F32, name="bank%d" % (PACK - 1))
-        for t in range(PACK):
-            mx(warm[:], x_q[1], block(t), w_q, whole, E4M3, True, True)
+        square(slope[1][:, 0:2, :], slope[1][:, 0:2, :])
+        square(slope[1][:, 2, :], slope[1][:, 2, :])
         gather(v_picked, v_planes, 1)
         for s in range(SLOT_BLOCKS):
-            fill_pair(nc.vector.tensor_copy, v_picked, s, 0)
+            fill_pair(nc.vector.tensor_copy, s, 0)
         gather(v_picked, v_planes, 2)
+        staged = keep.tile([P, N], F32, name="v_plane2")
+        tanh_half(1, PACK - 1, staged[:])
+        warm = bank(PACK - 1, [P, N])
+        for t in range(2):
+            mx(warm[:], x_q[1], block(t), w_q, whole, E4M3, True, True)
+        squared = v_picked[:, 1::2, HALF:N]
+        square(squared, staged[:].rearrange("p (h c) -> p h c", h=2))
+        nc.scalar.activation(out=slope[1][:, PACK - 1, :].rearrange("p (h c) -> p h c", h=2), in_=squared, func=ACT.Identity,
+                             scale=wt_quarter[:, 1, PACK - 1:PACK], bias=wt_peak[:])
         for t in range(PACK - 1):
             finish_slope(1, t)
-        last_plane(v_picked, v_planes, v_q)
-        wt_peak = keep.tile([P, 1], F32, name="v_plane%d" % (PACK - 1))
-        nc.scalar.activation(out=wt_peak[:], in_=wt_quarter[:, 1, PACK - 1:PACK], func=ACT.Copy, scale=-1.0)
-        nc.scalar.activation(out=slope[1][:, PACK - 1, :], in_=squared[:], func=ACT.Identity,
-                             scale=wt_quarter[:, 1, PACK - 1:PACK], bias=wt_peak[:])
 
-        acc = [out_psum.tile([P, N], F32, name="acc%d" % b) for b in range(D_BLOCKS)]
-        g_pieces = {(0, 0, 2): "g_lower0", (0, 2, 3): "g_third0", (0, 3, 4): "v1_codes",
-                    (1, 0, 2): "g_lower1", (1, 2, 3): "g_third1", (1, 3, 4): "g_third1"}
-        g_grouped = {}
+        last_plane = PACK - 1
+        for s in range(2):
+            gather(v_picked, v_planes, last_plane, s * SLOT_BLOCK, (s + 1) * SLOT_BLOCK)
+        nc.scalar.activation(v_picked[:, last_plane, HALF:N], v_planes[last_plane].indirect(listed(HALF, N)), ACT.Copy)
+        for s in range(SLOT_BLOCKS):
+            fill_pair(nc.vector.tensor_copy if s < 2 else nc.scalar.copy, s, 2)
+        for s in range(SLOT_BLOCKS):
+            quantise_v(s)
 
-        def unit_cols(g, s):
-            piece = [piece for piece in g_pieces if piece[0] == g and piece[1] <= s < piece[2]][0]
-            if piece not in g_grouped:
-                g_grouped[piece] = keep.tile([P, (piece[2] - piece[1]) * SLOT_BLOCK * PACK], BF16,
-                                             name=g_pieces[piece], align_bytes=64)
-            return g_grouped[piece][:, block(s - piece[1], SLOT_BLOCK * PACK)]
+        def scores(g, s, number):
+            unit = bank(number, [P, PACK, SLOT_BLOCK])
+            for t in range(PACK):
+                mx(unit[:, t, :], x_q[g], block(t), v_q[s], block(0), E4M3, True, True)
+            return unit
 
-        def gradient_unit(g, s):
-            bank = scores(g, s, v_q)
+        g_grouped = {(g, s): keep.tile([P, SLOT_BLOCK * PACK], BF16, name="g_grouped%d_%d" % (g, s), align_bytes=64)
+                     for g in range(ROW_PASSES) for s in range(SLOT_BLOCKS)}
+        av = keep.tile([P, SLOT_BLOCK + SHARED_SLOTS, PACK], F32, name="av", align_bytes=64)
+
+        def gradient_vector(g, s, unit, lo=0):
             nc.vector.tensor_tensor(
-                out=unit_cols(g, s).rearrange("p (c i t) -> p c t i", i=4, t=PACK),
-                in0=slope[g][:, :, block(s)].rearrange("p t (c i) -> p c t i", i=4),
-                in1=bank[:].rearrange("p t (c i) -> p c t i", i=4),
+                out=g_grouped[g, s][:, lo * PACK:].rearrange("p (c i t) -> p c t i", i=4, t=PACK),
+                in0=slope[g][:, :, s * SLOT_BLOCK + lo:(s + 1) * SLOT_BLOCK].rearrange("p t (c i) -> p c t i", i=4),
+                in1=unit[:, :, lo:].rearrange("p t (c i) -> p c t i", i=4),
                 op=ALU.mult)
 
-        def gradient_unit_gpsimd(g, s):
-            bank = scores(g, s, v_q)
-            av = keep.tile([P, SLOT_BLOCK, PACK], F32, name="av", align_bytes=64)
-            nc.scalar.copy(out=av[:], in_=bank[:].rearrange("p t c -> p c t"))
+        def gradient_gpsimd(g, s, unit, staging):
+            width = staging.shape[1]
+            nc.scalar.copy(out=staging, in_=unit[:, :, 0:width].rearrange("p t c -> p c t"))
             nc.gpsimd.tensor_tensor(
-                out=unit_cols(g, s).rearrange("p (c t) -> p c t", t=PACK),
-                in0=av[:], in1=slope[g][:, :, block(s)].rearrange("p t c -> p c t"), op=ALU.mult)
-
-        def quantise_g(g, lo, hi):
-            quantise(g_q[g], slice((lo + 1) * SLOT_BLOCK, (hi + 1) * SLOT_BLOCK), g_grouped[g, lo, hi][:], E5M2)
+                out=g_grouped[g, s][:, 0:width * PACK].rearrange("p (c t) -> p c t", t=PACK),
+                in0=staging,
+                in1=slope[g][:, :, s * SLOT_BLOCK:s * SLOT_BLOCK + width].rearrange("p t c -> p c t"), op=ALU.mult)
 
         m_grouped = {}
         m_q = {}
 
-        def group_m(copy, b, passes, slot):
-            grouped = keep.tile([P, len(passes), P * PACK], BF16, name=slot, align_bytes=64)
-            m_grouped[b, passes] = grouped
-            return [lambda k=k, g=g: interleave(copy, grouped[:, k, :], m_raw[b][g][:])
-                    for k, g in enumerate(passes)]
+        def cast_m(b, g, slot):
+            m_grouped[b, g] = keep.tile([P, P * PACK], BF16, name=slot, align_bytes=64)
+            interleave(nc.scalar.copy, m_grouped[b, g][:], m_raw[b][g][:])
 
-        def quantise_m(b, passes, slot):
-            width = len(passes) * P
-            pair = (keep.tile([P, width], U32, name=slot, align_bytes=64),
-                    keep.tile([P, width], U8, name="m_scales%d_%d" % (b, passes[0]), align_bytes=64))
-            quantise(pair, slice(0, width), m_grouped[b, passes][:].rearrange("p g c -> p (g c)"), E4M3)
-            for k, g in enumerate(passes):
-                m_q[b, g] = pair, block(k)
+        def quantise_m(b, g, pair):
+            m_q[b, g] = pair
+            quantise(pair, block(0), m_grouped[b, g][:], E4M3)
 
-        def product(dst, b, g, first=0, start=SLOT_BLOCK):
-            pair, cols = m_q[b, g]
-            mx(dst[:], pair, cols, g_q[g], slice(start, start + N), E5M2, g == first, g != first)
+        def held(name, slot):
+            return words(slot, P)[:], keep.tile([P, P], U8, name=name, align_bytes=64)[:]
+
+        def product(dst, b, g, cols):
+            mx(dst[:], m_q[b, g], block(0), g_q[g], cols, E5M2, g == 0, g == ROW_PASSES - 1)
 
         def dense_copy(name, source):
             dense = keep.tile([P, source.shape[1]], F32, name=name, align_bytes=64)
-            nc.scalar.copy(out=dense[:], in_=source)
+            nc.scalar.copy(out=dense[:], in_=source[:])
             return dense
-
-        def scatter(b, lo, hi, dense):
-            nc.vector.tensor_copy(windows[b][:].indirect(offsets[:, lo // 16:hi // 16]), dense[:])
 
         def store(b):
             nc.sync.dma_start(out=out[block(b), :], in_=windows[b][:])
 
-        last = block(SLOT_BLOCKS - 1)
-        ready = (SLOT_BLOCKS - 1) * SLOT_BLOCK
-        for codes, scales in g_q:
-            nc.vector.memset(codes[:, block(0)], 0)
-            nc.vector.memset(scales[:, block(0)], 0)
         zeros = keep.tile([P, SLOT_BLOCK], F32, name="zeros", align_bytes=64)
-        nc.vector.memset(zeros[:], 0.0)
+        nc.gpsimd.memset(zeros[:], 0.0)
 
-        both = (0, 1)
-        gradient_unit(0, 0)
-        gradient_unit(0, 1)
-        gradient_unit_gpsimd(1, 1)
-        for cast in group_m(nc.scalar.copy, 0, both, "v1_codes"):
-            cast()
-        gradient_unit(0, 2)
-        gradient_unit(1, 2)
-        gradient_unit(1, 0)
-        for passes, slot in (((1,), "v2_codes"), ((0,), "v0_codes")):
-            for cast in group_m(nc.scalar.copy, 1, passes, slot):
-                cast()
-        for cast in group_m(nc.scalar.copy, 2, both, "av"):
-            cast()
-        quantise_g(0, 0, 2)
-        quantise_m(0, both, "m_codes0")
-        quantise_g(0, 2, 3)
-        quantise_g(1, 2, 3)
-        quantise_g(1, 0, 2)
-        early = unit_psum.tile([P, N], F32, name="bank3")
-        for g in both:
-            product(early, 0, g, start=0)
-        for g in both:
-            gradient_unit(g, 3)
-        quantise_g(0, 3, 4)
-        product(acc[0], 0, 0)
-        quantise_m(1, (1,), "g_lower1")
-        quantise_g(1, 3, 4)
-        product(acc[0], 0, 1)
-        quantise_m(1, (0,), "g_third1")
-        dense_early = dense_copy("dense_early", early[:, SLOT_BLOCK:N])
-        scatter(0, 0, ready, dense_early)
-        dense_last = dense_copy("dense_last", acc[0][:, last])
-        nc.vector.tensor_tensor(windows[0][:].indirect(offsets[:, ready // 16:N // 16]), dense_last[:], zeros[:], ALU.add)
+        gradient_vector(0, 0, scores(0, 0, 0))
+        gradient_gpsimd(0, 1, scores(0, 1, 1), av[:, 0:SLOT_BLOCK, :])
+        gradient_vector(0, 2, scores(0, 2, 2))
+        shared = scores(1, 1, 4)
+        gradient_gpsimd(1, 1, shared, av[:, SLOT_BLOCK:, :])
+        cast_m(0, 0, "m_grouped0")
+        cast_m(0, 1, "v1_codes")
+        gradient_vector(0, 3, scores(0, 3, 5))
+        gradient_vector(1, 0, scores(1, 0, 6))
+        gradient_vector(1, 2, scores(1, 2, 2))
+        gradient_vector(1, 1, shared, SHARED_SLOTS)
+        gradient_vector(1, 3, scores(1, 3, 6))
+        cast_m(1, 0, "v0_codes")
+        cast_m(1, 1, "v2_codes")
+        cast_m(2, 0, "v3_codes")
+        cast_m(2, 1, "m_grouped0")
+
+        late_scales = keep.tile([P, ROW_PASSES * (N + P)], U8, name="av", align_bytes=64)
+        g_q = [(words("g%d_codes" % g, N)[:], late_scales[:, block(g, N)]) for g in range(ROW_PASSES)]
+        for g in range(ROW_PASSES):
+            quantise_m(0, g, (words("m0_codes%d" % g, P)[:], late_scales[:, ROW_PASSES * N:][:, block(g)]))
+        pieces = []
+        for s, number in enumerate((7, 3, 0, 1)):
+            piece = bank(number, [P, SLOT_BLOCK])
+            for g in range(ROW_PASSES):
+                quantise(g_q[g], block(s), g_grouped[g, s][:], E5M2)
+                product(piece, 0, g, block(s))
+            pieces.append(dense_copy("dense0_%d" % s, piece))
+        for g in range(ROW_PASSES):
+            quantise_m(1, g, held("m1_scales%d" % g, "g_grouped%d_2" % g))
+        for s, dense in enumerate(pieces):
+            nc.vector.tensor_tensor(windows[0][:].indirect(listed(s * SLOT_BLOCK, (s + 1) * SLOT_BLOCK)),
+                                    dense[:], zeros[:], ALU.add)
         store(0)
 
-        for g in (1, 0):
-            product(acc[1], 1, g, first=1)
-        dense = dense_copy("dense_early", acc[1][:])
-        quantise_m(2, both, "zeros")
-        scatter(1, 0, N, dense)
-        store(1)
-        for cast in group_m(nc.scalar.copy, 3, both, "dense_last"):
-            cast()
-        quantise_m(3, both, "m_codes3")
-        for b in range(2, D_BLOCKS):
+        def finish_block(b, number):
+            sums = bank(number, [P, N])
             for g in range(ROW_PASSES):
-                product(acc[b], b, g)
-            scatter(b, 0, N, dense_copy("dense%d" % b, acc[b][:]))
+                product(sums, b, g, whole)
+            dense = dense_copy("dense%d" % b, sums)
+            nc.vector.tensor_copy(windows[b][:].indirect(offsets[:]), dense[:])
             store(b)
+
+        quantise_m(2, 0, held("m2_scales0", "zeros"))
+        quantise_m(2, 1, held("m2_scales1", "dense0_3"))
+        finish_block(1, 2)
+        cast_m(3, 0, "dense0_1")
+        cast_m(3, 1, "dense1")
+        finish_block(2, 4)
+        for g in range(ROW_PASSES):
+            quantise_m(3, g, quantised("m3_%d" % g, P))
+        finish_block(3, 5)

@@ -181,7 +181,7 @@ def tile_attend_ghv_nce_kernel(tc, xT, wT, vT, wt, xm, offs, out):
         for s in range(SLOT_BLOCKS):
             fill_pair(nc.vector.tensor_copy, s, 0)
         gather(v_picked, v_planes, 2)
-        staged = keep.tile([P, N], F32, name="v_plane2")
+        staged = keep.tile([P, N], F32, name="staged")
         tanh_half(1, PACK - 1, staged[:])
         warm = bank(PACK - 1, [P, N])
         for t in range(2):

@@ -25,7 +25,6 @@ SLOT_BLOCK = 128
 SLOT_BLOCKS = N // SLOT_BLOCK
 D_BLOCKS = D // P
 HALF = N // 2
-SHARED_SLOTS = 64
 
 
 def tile_attend_ghv_nce_kernel(tc, xT, wT, vT, wt, xm, offs, out):
@@ -100,14 +99,13 @@ def tile_attend_ghv_nce_kernel(tc, xT, wT, vT, wt, xm, offs, out):
             engine = nc.gpsimd if b % 2 else nc.vector
             engine.memset(windows[b][:].bitcast(I32), 0)
 
-        wt_quarter = keep.tile([P, ROW_PASSES, PACK], F32, name="wt_quarter")
-        wt_peak = keep.tile([P, 1], F32, name="wt_peak")
+        wt_quarter = keep.tile([P, ROW_PASSES * PACK - 1], F32, name="wt_quarter")
         wt_turned = bank(4, [P, PACK, P])
         for t in range(PACK):
             nc.tensor.transpose(wt_turned[:, t, :], wt_rows[:, t::PACK], identity[:])
-        nc.scalar.activation(out=wt_quarter[:], in_=wt_turned[:, :, 0:ROW_PASSES].rearrange("p t g -> p g t"),
-                             func=ACT.Copy, scale=-0.25)
-        nc.scalar.activation(out=wt_peak[:], in_=wt_turned[:, PACK - 1, 1:2], func=ACT.Copy, scale=0.25)
+        for g, tiles in enumerate((PACK, PACK - 1)):
+            nc.scalar.activation(out=wt_quarter[:, g * PACK:g * PACK + tiles], in_=wt_turned[:, 0:tiles, g],
+                                 func=ACT.Copy, scale=-0.25)
 
         x_q = [quantised("x%d" % g, K_PASS) for g in range(ROW_PASSES)]
         w_q = quantised("w", N)
@@ -142,9 +140,11 @@ def tile_attend_ghv_nce_kernel(tc, xT, wT, vT, wt, xm, offs, out):
         v_picked = keep.tile([P, PACK, N], F32, name="v_picked")
         slope = [keep.tile([P, PACK, N], F32, name="slope%d" % g) for g in range(ROW_PASSES)]
 
-        def finish_slope(g, t):
+        def finish_slope(g, t, weight=None):
+            if weight is None:
+                weight = wt_quarter[:, g * PACK + t:g * PACK + t + 1]
             nc.vector.tensor_scalar(out=slope[g][:, t, :], in0=slope[g][:, t, :], scalar1=1.0,
-                                    scalar2=wt_quarter[:, g, t:t + 1], op0=ALU.subtract, op1=ALU.mult)
+                                    scalar2=weight, op0=ALU.subtract, op1=ALU.mult)
 
         def tanh_half(g, t, target):
             scores = bank(t, [P, N])
@@ -181,15 +181,11 @@ def tile_attend_ghv_nce_kernel(tc, xT, wT, vT, wt, xm, offs, out):
         for s in range(SLOT_BLOCKS):
             fill_pair(nc.vector.tensor_copy, s, 0)
         gather(v_picked, v_planes, 2)
-        staged = keep.tile([P, N], F32, name="staged")
-        tanh_half(1, PACK - 1, staged[:])
+        tanh_half(1, PACK - 1, slope[1][:, PACK - 1, :])
         warm = bank(PACK - 1, [P, N])
         for t in range(2):
             mx(warm[:], x_q[1], block(t), w_q, whole, E4M3, True, True)
-        squared = v_picked[:, 1::2, HALF:N]
-        square(squared, staged[:].rearrange("p (h c) -> p h c", h=2))
-        nc.scalar.activation(out=slope[1][:, PACK - 1, :].rearrange("p (h c) -> p h c", h=2), in_=squared, func=ACT.Identity,
-                             scale=wt_quarter[:, 1, PACK - 1:PACK], bias=wt_peak[:])
+        square(slope[1][:, PACK - 1, :], slope[1][:, PACK - 1, :])
         for t in range(PACK - 1):
             finish_slope(1, t)
 
@@ -197,10 +193,15 @@ def tile_attend_ghv_nce_kernel(tc, xT, wT, vT, wt, xm, offs, out):
         for s in range(2):
             gather(v_picked, v_planes, last_plane, s * SLOT_BLOCK, (s + 1) * SLOT_BLOCK)
         nc.scalar.activation(v_picked[:, last_plane, HALF:N], v_planes[last_plane].indirect(listed(HALF, N)), ACT.Copy)
-        for s in range(SLOT_BLOCKS):
-            fill_pair(nc.vector.tensor_copy if s < 2 else nc.scalar.copy, s, 2)
+        for s in range(2):
+            fill_pair(nc.vector.tensor_copy, s, 2)
+        fill_pair(nc.scalar.copy, 2, 2)
+        last_weight = keep.tile([P, 1], F32, name="v_plane%d" % last_plane)
+        nc.scalar.activation(out=last_weight[:], in_=wt_turned[:, PACK - 1, 1:2], func=ACT.Copy, scale=-0.25)
+        fill_pair(nc.scalar.copy, 3, 2)
         for s in range(SLOT_BLOCKS):
             quantise_v(s)
+        finish_slope(1, PACK - 1, last_weight[:])
 
         def scores(g, s, number):
             unit = bank(number, [P, PACK, SLOT_BLOCK])
@@ -210,7 +211,7 @@ def tile_attend_ghv_nce_kernel(tc, xT, wT, vT, wt, xm, offs, out):
 
         g_grouped = {(g, s): keep.tile([P, SLOT_BLOCK * PACK], BF16, name="g_grouped%d_%d" % (g, s), align_bytes=64)
                      for g in range(ROW_PASSES) for s in range(SLOT_BLOCKS)}
-        av = keep.tile([P, SLOT_BLOCK + SHARED_SLOTS, PACK], F32, name="av", align_bytes=64)
+        av = keep.tile([P, SLOT_BLOCK, PACK], F32, name="av", align_bytes=64)
 
         def gradient_vector(g, s, unit, lo=0):
             nc.vector.tensor_tensor(
@@ -256,18 +257,16 @@ def tile_attend_ghv_nce_kernel(tc, xT, wT, vT, wt, xm, offs, out):
         nc.gpsimd.memset(zeros[:], 0.0)
 
         gradient_vector(0, 0, scores(0, 0, 0))
-        gradient_gpsimd(0, 1, scores(0, 1, 1), av[:, 0:SLOT_BLOCK, :])
-        gradient_vector(0, 2, scores(0, 2, 2))
-        shared = scores(1, 1, 4)
-        gradient_gpsimd(1, 1, shared, av[:, SLOT_BLOCK:, :])
+        gradient_vector(0, 2, scores(0, 2, 1))
+        gradient_gpsimd(0, 1, scores(0, 1, 2), av[:])
         cast_m(0, 0, "m_grouped0")
-        cast_m(0, 1, "v1_codes")
         gradient_vector(0, 3, scores(0, 3, 5))
         gradient_vector(1, 0, scores(1, 0, 6))
-        gradient_vector(1, 2, scores(1, 2, 2))
-        gradient_vector(1, 1, shared, SHARED_SLOTS)
-        gradient_vector(1, 3, scores(1, 3, 6))
-        cast_m(1, 0, "v0_codes")
+        gradient_vector(1, 1, scores(1, 1, 0))
+        gradient_vector(1, 2, scores(1, 2, 1))
+        gradient_vector(1, 3, scores(1, 3, 5))
+        cast_m(0, 1, "v0_codes")
+        cast_m(1, 0, "v1_codes")
         cast_m(1, 1, "v2_codes")
         cast_m(2, 0, "v3_codes")
         cast_m(2, 1, "m_grouped0")
@@ -277,17 +276,18 @@ def tile_attend_ghv_nce_kernel(tc, xT, wT, vT, wt, xm, offs, out):
         for g in range(ROW_PASSES):
             quantise_m(0, g, (words("m0_codes%d" % g, P)[:], late_scales[:, ROW_PASSES * N:][:, block(g)]))
         pieces = []
-        for s, number in enumerate((7, 3, 0, 1)):
+        for s, number in enumerate((7, 3, 2, 6)):
             piece = bank(number, [P, SLOT_BLOCK])
             for g in range(ROW_PASSES):
                 quantise(g_q[g], block(s), g_grouped[g, s][:], E5M2)
                 product(piece, 0, g, block(s))
             pieces.append(dense_copy("dense0_%d" % s, piece))
-        for g in range(ROW_PASSES):
-            quantise_m(1, g, held("m1_scales%d" % g, "g_grouped%d_2" % g))
+        quantise_m(1, 0, held("m1_scales0", "g_grouped0_2"))
         for s, dense in enumerate(pieces):
             nc.vector.tensor_tensor(windows[0][:].indirect(listed(s * SLOT_BLOCK, (s + 1) * SLOT_BLOCK)),
                                     dense[:], zeros[:], ALU.add)
+            if s == 0:
+                quantise_m(1, 1, held("m1_scales1", "dense0_0"))
         store(0)
 
         def finish_block(b, number):
@@ -300,10 +300,10 @@ def tile_attend_ghv_nce_kernel(tc, xT, wT, vT, wt, xm, offs, out):
 
         quantise_m(2, 0, held("m2_scales0", "zeros"))
         quantise_m(2, 1, held("m2_scales1", "dense0_3"))
-        finish_block(1, 2)
+        finish_block(1, 0)
         cast_m(3, 0, "dense0_1")
         cast_m(3, 1, "dense1")
-        finish_block(2, 4)
+        finish_block(2, 1)
         for g in range(ROW_PASSES):
             quantise_m(3, g, quantised("m3_%d" % g, P))
         finish_block(3, 5)

@@ -99,13 +99,12 @@ def tile_attend_ghv_nce_kernel(tc, xT, wT, vT, wt, xm, offs, out):
             engine = nc.gpsimd if b % 2 else nc.vector
             engine.memset(windows[b][:].bitcast(I32), 0)
 
-        wt_quarter = keep.tile([P, ROW_PASSES * PACK - 1], F32, name="wt_quarter")
+        wt_quarter = keep.tile([P, ROW_PASSES, PACK], F32, name="wt_quarter")
         wt_turned = bank(4, [P, PACK, P])
         for t in range(PACK):
             nc.tensor.transpose(wt_turned[:, t, :], wt_rows[:, t::PACK], identity[:])
-        for g, tiles in enumerate((PACK, PACK - 1)):
-            nc.scalar.activation(out=wt_quarter[:, g * PACK:g * PACK + tiles], in_=wt_turned[:, 0:tiles, g],
-                                 func=ACT.Copy, scale=-0.25)
+        nc.scalar.activation(out=wt_quarter[:], in_=wt_turned[:, :, 0:ROW_PASSES].rearrange("p t g -> p g t"),
+                             func=ACT.Copy, scale=-0.25)
 
         x_q = [quantised("x%d" % g, K_PASS) for g in range(ROW_PASSES)]
         w_q = quantised("w", N)
@@ -140,11 +139,9 @@ def tile_attend_ghv_nce_kernel(tc, xT, wT, vT, wt, xm, offs, out):
         v_picked = keep.tile([P, PACK, N], F32, name="v_picked")
         slope = [keep.tile([P, PACK, N], F32, name="slope%d" % g) for g in range(ROW_PASSES)]
 
-        def finish_slope(g, t, weight=None):
-            if weight is None:
-                weight = wt_quarter[:, g * PACK + t:g * PACK + t + 1]
+        def finish_slope(g, t):
             nc.vector.tensor_scalar(out=slope[g][:, t, :], in0=slope[g][:, t, :], scalar1=1.0,
-                                    scalar2=weight, op0=ALU.subtract, op1=ALU.mult)
+                                    scalar2=wt_quarter[:, g, t:t + 1], op0=ALU.subtract, op1=ALU.mult)
 
         def tanh_half(g, t, target):
             scores = bank(t, [P, N])
@@ -192,16 +189,18 @@ def tile_attend_ghv_nce_kernel(tc, xT, wT, vT, wt, xm, offs, out):
         last_plane = PACK - 1
         for s in range(2):
             gather(v_picked, v_planes, last_plane, s * SLOT_BLOCK, (s + 1) * SLOT_BLOCK)
-        nc.scalar.activation(v_picked[:, last_plane, HALF:N], v_planes[last_plane].indirect(listed(HALF, N)), ACT.Copy)
-        for s in range(2):
-            fill_pair(nc.vector.tensor_copy, s, 2)
-        fill_pair(nc.scalar.copy, 2, 2)
-        last_weight = keep.tile([P, 1], F32, name="v_plane%d" % last_plane)
-        nc.scalar.activation(out=last_weight[:], in_=wt_turned[:, PACK - 1, 1:2], func=ACT.Copy, scale=-0.25)
+        fill_pair(nc.vector.tensor_copy, 0, 2)
+        fill_pair(nc.scalar.copy, 1, 2)
+        gather(v_picked, v_planes, last_plane, HALF, N)
+        quantise_v(0)
+        fill_pair(nc.vector.tensor_copy, 2, 2)
         fill_pair(nc.scalar.copy, 3, 2)
-        for s in range(SLOT_BLOCKS):
+        for s in (1, 3, 2):
             quantise_v(s)
-        finish_slope(1, PACK - 1, last_weight[:])
+        wt_peak = keep.tile([P, 1], F32, name="v_plane%d" % last_plane)
+        nc.scalar.activation(out=wt_peak[:], in_=wt_quarter[:, 1, PACK - 1:PACK], func=ACT.Copy, scale=-1.0)
+        nc.scalar.activation(out=slope[1][:, PACK - 1, :], in_=slope[1][:, PACK - 1, :], func=ACT.Identity,
+                             scale=wt_quarter[:, 1, PACK - 1:PACK], bias=wt_peak[:])
 
         def scores(g, s, number):
             unit = bank(number, [P, PACK, SLOT_BLOCK])
@@ -232,12 +231,12 @@ def tile_attend_ghv_nce_kernel(tc, xT, wT, vT, wt, xm, offs, out):
         m_q = {}
 
         def cast_m(b, g, slot):
-            m_grouped[b, g] = keep.tile([P, P * PACK], BF16, name=slot, align_bytes=64)
-            interleave(nc.scalar.copy, m_grouped[b, g][:], m_raw[b][g][:])
+            m_grouped[b, g] = keep.tile([P, P * PACK], BF16, name=slot, align_bytes=64)[:]
+            interleave(nc.scalar.copy, m_grouped[b, g], m_raw[b][g][:])
 
         def quantise_m(b, g, pair):
             m_q[b, g] = pair
-            quantise(pair, block(0), m_grouped[b, g][:], E4M3)
+            quantise(pair, block(0), m_grouped[b, g], E4M3)
 
         def held(name, slot):
             return words(slot, P)[:], keep.tile([P, P], U8, name=name, align_bytes=64)[:]
@@ -253,14 +252,11 @@ def tile_attend_ghv_nce_kernel(tc, xT, wT, vT, wt, xm, offs, out):
         def store(b):
             nc.sync.dma_start(out=out[block(b), :], in_=windows[b][:])
 
-        zeros = keep.tile([P, SLOT_BLOCK], F32, name="zeros", align_bytes=64)
-        nc.gpsimd.memset(zeros[:], 0.0)
-
         gradient_vector(0, 0, scores(0, 0, 0))
-        gradient_vector(0, 2, scores(0, 2, 1))
-        gradient_gpsimd(0, 1, scores(0, 1, 2), av[:])
+        gradient_vector(0, 1, scores(0, 1, 1))
+        gradient_gpsimd(0, 3, scores(0, 3, 2), av[:])
         cast_m(0, 0, "m_grouped0")
-        gradient_vector(0, 3, scores(0, 3, 5))
+        gradient_vector(0, 2, scores(0, 2, 5))
         gradient_vector(1, 0, scores(1, 0, 6))
         gradient_vector(1, 1, scores(1, 1, 0))
         gradient_vector(1, 2, scores(1, 2, 1))
@@ -275,19 +271,17 @@ def tile_attend_ghv_nce_kernel(tc, xT, wT, vT, wt, xm, offs, out):
         g_q = [(words("g%d_codes" % g, N)[:], late_scales[:, block(g, N)]) for g in range(ROW_PASSES)]
         for g in range(ROW_PASSES):
             quantise_m(0, g, (words("m0_codes%d" % g, P)[:], late_scales[:, ROW_PASSES * N:][:, block(g)]))
-        pieces = []
+        halves = [keep.tile([P, HALF], F32, name="dense0_%d" % h, align_bytes=64) for h in range(2)]
         for s, number in enumerate((7, 3, 2, 6)):
             piece = bank(number, [P, SLOT_BLOCK])
             for g in range(ROW_PASSES):
                 quantise(g_q[g], block(s), g_grouped[g, s][:], E5M2)
                 product(piece, 0, g, block(s))
-            pieces.append(dense_copy("dense0_%d" % s, piece))
-        quantise_m(1, 0, held("m1_scales0", "g_grouped0_2"))
-        for s, dense in enumerate(pieces):
-            nc.vector.tensor_tensor(windows[0][:].indirect(listed(s * SLOT_BLOCK, (s + 1) * SLOT_BLOCK)),
-                                    dense[:], zeros[:], ALU.add)
-            if s == 0:
-                quantise_m(1, 1, held("m1_scales1", "dense0_0"))
+            nc.scalar.copy(out=halves[s // 2][:, block(s % 2)], in_=piece[:])
+        for g in range(ROW_PASSES):
+            quantise_m(1, g, held("m1_scales%d" % g, "g_grouped%d_2" % g))
+        for h in range(2):
+            nc.vector.tensor_copy(windows[0][:].indirect(listed(h * HALF, (h + 1) * HALF)), halves[h][:])
         store(0)
 
         def finish_block(b, number):
@@ -298,11 +292,15 @@ def tile_attend_ghv_nce_kernel(tc, xT, wT, vT, wt, xm, offs, out):
             nc.vector.tensor_copy(windows[b][:].indirect(offsets[:]), dense[:])
             store(b)
 
-        quantise_m(2, 0, held("m2_scales0", "zeros"))
-        quantise_m(2, 1, held("m2_scales1", "dense0_3"))
+        late_codes = words("dense0_1", ROW_PASSES * P)
+        for g in range(ROW_PASSES):
+            scales = keep.tile([P, P], U8, name="m2_scales%d" % g, align_bytes=64)
+            quantise_m(2, g, (late_codes[:, block(g)], scales[:]))
         finish_block(1, 0)
-        cast_m(3, 0, "dense0_1")
-        cast_m(3, 1, "dense1")
+        late_grouped = keep.tile([P, ROW_PASSES, P * PACK], BF16, name="dense0_0", align_bytes=64)
+        for g in range(ROW_PASSES):
+            m_grouped[3, g] = late_grouped[:, g, :]
+            interleave(nc.scalar.copy, late_grouped[:, g, :], m_raw[3][g][:])
         finish_block(2, 1)
         for g in range(ROW_PASSES):
             quantise_m(3, g, quantised("m3_%d" % g, P))

@@ -178,11 +178,16 @@ def tile_attend_ghv_nce_kernel(tc, xT, wT, vT, wt, xm, offs, out):
         for s in range(SLOT_BLOCKS):
             fill_pair(nc.vector.tensor_copy, s, 0)
         gather(v_picked, v_planes, 2)
-        tanh_half(1, PACK - 1, slope[1][:, PACK - 1, :])
-        warm = bank(PACK - 1, [P, N])
-        for t in range(2):
-            mx(warm[:], x_q[1], block(t), w_q, whole, E4M3, True, True)
-        square(slope[1][:, PACK - 1, :], slope[1][:, PACK - 1, :])
+        staged = keep.tile([P, N], F32, name="staged")
+        tanh_half(1, PACK - 1, staged[:])
+        square(slope[1][:, PACK - 1, :], staged[:])
+        wt_peak = keep.tile([P, 1], F32, name="staged")
+        nc.scalar.activation(out=wt_peak[:], in_=wt_turned[:, PACK - 1, 1:2], func=ACT.Copy, scale=0.25)
+        nc.scalar.activation(out=slope[1][:, PACK - 1, :], in_=slope[1][:, PACK - 1, :], func=ACT.Identity,
+                             scale=wt_quarter[:, 1, PACK - 1:PACK], bias=wt_peak[:])
+        warm = bank(4, [P, N])
+        for t, width in enumerate((512, 512, 128, 64)):
+            mx(warm[:, 0:width], x_q[1], block(t), w_q, slice(0, width), E4M3, True, True)
         for t in range(PACK - 1):
             finish_slope(1, t)
 
@@ -197,10 +202,6 @@ def tile_attend_ghv_nce_kernel(tc, xT, wT, vT, wt, xm, offs, out):
         fill_pair(nc.scalar.copy, 3, 2)
         for s in (1, 3, 2):
             quantise_v(s)
-        wt_peak = keep.tile([P, 1], F32, name="v_plane%d" % last_plane)
-        nc.scalar.activation(out=wt_peak[:], in_=wt_quarter[:, 1, PACK - 1:PACK], func=ACT.Copy, scale=-1.0)
-        nc.scalar.activation(out=slope[1][:, PACK - 1, :], in_=slope[1][:, PACK - 1, :], func=ACT.Identity,
-                             scale=wt_quarter[:, 1, PACK - 1:PACK], bias=wt_peak[:])
 
         def scores(g, s, number):
             unit = bank(number, [P, PACK, SLOT_BLOCK])
@@ -230,9 +231,9 @@ def tile_attend_ghv_nce_kernel(tc, xT, wT, vT, wt, xm, offs, out):
         m_grouped = {}
         m_q = {}
 
-        def cast_m(b, g, slot):
+        def cast_m(b, g, slot, copy=nc.scalar.copy):
             m_grouped[b, g] = keep.tile([P, P * PACK], BF16, name=slot, align_bytes=64)[:]
-            interleave(nc.scalar.copy, m_grouped[b, g], m_raw[b][g][:])
+            interleave(copy, m_grouped[b, g], m_raw[b][g][:])
 
         def quantise_m(b, g, pair):
             m_q[b, g] = pair
@@ -254,13 +255,13 @@ def tile_attend_ghv_nce_kernel(tc, xT, wT, vT, wt, xm, offs, out):
 
         gradient_vector(0, 0, scores(0, 0, 0))
         gradient_vector(0, 1, scores(0, 1, 1))
-        gradient_gpsimd(0, 3, scores(0, 3, 2), av[:])
         cast_m(0, 0, "m_grouped0")
-        gradient_vector(0, 2, scores(0, 2, 5))
+        gradient_vector(0, 3, scores(0, 3, 2))
+        gradient_gpsimd(0, 2, scores(0, 2, 5), av[:])
         gradient_vector(1, 0, scores(1, 0, 6))
         gradient_vector(1, 1, scores(1, 1, 0))
         gradient_vector(1, 2, scores(1, 2, 1))
-        gradient_vector(1, 3, scores(1, 3, 5))
+        gradient_vector(1, 3, scores(1, 3, 2))
         cast_m(0, 1, "v0_codes")
         cast_m(1, 0, "v1_codes")
         cast_m(1, 1, "v2_codes")
@@ -272,7 +273,7 @@ def tile_attend_ghv_nce_kernel(tc, xT, wT, vT, wt, xm, offs, out):
         for g in range(ROW_PASSES):
             quantise_m(0, g, (words("m0_codes%d" % g, P)[:], late_scales[:, ROW_PASSES * N:][:, block(g)]))
         halves = [keep.tile([P, HALF], F32, name="dense0_%d" % h, align_bytes=64) for h in range(2)]
-        for s, number in enumerate((7, 3, 2, 6)):
+        for s, number in enumerate((7, 3, 5, 6)):
             piece = bank(number, [P, SLOT_BLOCK])
             for g in range(ROW_PASSES):
                 quantise(g_q[g], block(s), g_grouped[g, s][:], E5M2)
@@ -296,12 +297,16 @@ def tile_attend_ghv_nce_kernel(tc, xT, wT, vT, wt, xm, offs, out):
         for g in range(ROW_PASSES):
             scales = keep.tile([P, P], U8, name="m2_scales%d" % g, align_bytes=64)
             quantise_m(2, g, (late_codes[:, block(g)], scales[:]))
-        finish_block(1, 0)
-        late_grouped = keep.tile([P, ROW_PASSES, P * PACK], BF16, name="dense0_0", align_bytes=64)
-        for g in range(ROW_PASSES):
-            m_grouped[3, g] = late_grouped[:, g, :]
-            interleave(nc.scalar.copy, late_grouped[:, g, :], m_raw[3][g][:])
-        finish_block(2, 1)
+        for h, number in enumerate((0, 4)):
+            sums = bank(number, [P, HALF])
+            for g in range(ROW_PASSES):
+                product(sums, 1, g, block(h, HALF))
+            dense = dense_copy("dense1_%d" % h, sums)
+            nc.vector.tensor_copy(windows[1][:].indirect(listed(h * HALF, (h + 1) * HALF)), dense[:])
+        store(1)
+        cast_m(3, 0, "dense1_0")
+        cast_m(3, 1, "dense1_1", nc.vector.tensor_copy)
         for g in range(ROW_PASSES):
             quantise_m(3, g, quantised("m3_%d" % g, P))
-        finish_block(3, 5)
+        finish_block(2, 1)
+        finish_block(3, 2)

@@ -106,6 +106,9 @@ def tile_attend_ghv_nce_kernel(tc, xT, wT, vT, wt, xm, offs, out):
         nc.scalar.activation(out=wt_quarter[:], in_=wt_turned[:, :, 0:ROW_PASSES].rearrange("p t g -> p g t"),
                              func=ACT.Copy, scale=-0.25)
 
+        wt_peak = keep.tile([P, 2], F32, name="wt_peak")
+        nc.scalar.activation(out=wt_peak[:], in_=wt_turned[:, 1::2, 1], func=ACT.Copy, scale=0.25)
+
         x_q = [quantised("x%d" % g, K_PASS) for g in range(ROW_PASSES)]
         w_q = quantised("w", N)
         v_q = [quantised("v%d" % s, SLOT_BLOCK) for s in range(SLOT_BLOCKS)]
@@ -143,6 +146,10 @@ def tile_attend_ghv_nce_kernel(tc, xT, wT, vT, wt, xm, offs, out):
             nc.vector.tensor_scalar(out=slope[g][:, t, :], in0=slope[g][:, t, :], scalar1=1.0,
                                     scalar2=wt_quarter[:, g, t:t + 1], op0=ALU.subtract, op1=ALU.mult)
 
+        def finish_slope_scalar(t):
+            nc.scalar.activation(out=slope[1][:, t, :], in_=slope[1][:, t, :], func=ACT.Identity,
+                                 scale=wt_quarter[:, 1, t:t + 1], bias=wt_peak[:, t // 2:t // 2 + 1])
+
         def tanh_half(g, t, target):
             scores = bank(t, [P, N])
             mx(scores[:], x_q[g], block(t), w_q, whole, E4M3, True, True)
@@ -178,17 +185,14 @@ def tile_attend_ghv_nce_kernel(tc, xT, wT, vT, wt, xm, offs, out):
         for s in range(SLOT_BLOCKS):
             fill_pair(nc.vector.tensor_copy, s, 0)
         gather(v_picked, v_planes, 2)
-        staged = keep.tile([P, N], F32, name="staged")
-        tanh_half(1, PACK - 1, staged[:])
-        square(slope[1][:, PACK - 1, :], staged[:])
-        wt_peak = keep.tile([P, 1], F32, name="staged")
-        nc.scalar.activation(out=wt_peak[:], in_=wt_turned[:, PACK - 1, 1:2], func=ACT.Copy, scale=0.25)
-        nc.scalar.activation(out=slope[1][:, PACK - 1, :], in_=slope[1][:, PACK - 1, :], func=ACT.Identity,
-                             scale=wt_quarter[:, 1, PACK - 1:PACK], bias=wt_peak[:])
-        warm = bank(4, [P, N])
+        finish_slope_scalar(1)
+        tanh_half(1, PACK - 1, slope[1][:, PACK - 1, :])
+        warm = bank(PACK - 1, [P, N])
         for t, width in enumerate((512, 512, 128, 64)):
             mx(warm[:, 0:width], x_q[1], block(t), w_q, slice(0, width), E4M3, True, True)
-        for t in range(PACK - 1):
+        square(slope[1][:, PACK - 1, :], slope[1][:, PACK - 1, :])
+        finish_slope_scalar(3)
+        for t in (0, 2):
             finish_slope(1, t)
 
         last_plane = PACK - 1
@@ -200,7 +204,7 @@ def tile_attend_ghv_nce_kernel(tc, xT, wT, vT, wt, xm, offs, out):
         quantise_v(0)
         fill_pair(nc.vector.tensor_copy, 2, 2)
         fill_pair(nc.scalar.copy, 3, 2)
-        for s in (1, 3, 2):
+        for s in range(1, SLOT_BLOCKS):
             quantise_v(s)
 
         def scores(g, s, number):
@@ -256,8 +260,8 @@ def tile_attend_ghv_nce_kernel(tc, xT, wT, vT, wt, xm, offs, out):
         gradient_vector(0, 0, scores(0, 0, 0))
         gradient_vector(0, 1, scores(0, 1, 1))
         cast_m(0, 0, "m_grouped0")
-        gradient_vector(0, 3, scores(0, 3, 2))
-        gradient_gpsimd(0, 2, scores(0, 2, 5), av[:])
+        gradient_vector(0, 2, scores(0, 2, 2))
+        gradient_gpsimd(0, 3, scores(0, 3, 5), av[:])
         gradient_vector(1, 0, scores(1, 0, 6))
         gradient_vector(1, 1, scores(1, 1, 0))
         gradient_vector(1, 2, scores(1, 2, 1))

@@ -99,15 +99,16 @@ def tile_attend_ghv_nce_kernel(tc, xT, wT, vT, wt, xm, offs, out):
             engine = nc.gpsimd if b % 2 else nc.vector
             engine.memset(windows[b][:].bitcast(I32), 0)
 
-        wt_quarter = keep.tile([P, ROW_PASSES, PACK], F32, name="wt_quarter")
+        wt_quarter = keep.tile([P, ROW_PASSES * PACK - 1], F32, name="wt_quarter")
         wt_turned = bank(4, [P, PACK, P])
         for t in range(PACK):
             nc.tensor.transpose(wt_turned[:, t, :], wt_rows[:, t::PACK], identity[:])
-        nc.scalar.activation(out=wt_quarter[:], in_=wt_turned[:, :, 0:ROW_PASSES].rearrange("p t g -> p g t"),
-                             func=ACT.Copy, scale=-0.25)
+        for g, tiles in enumerate((PACK, PACK - 1)):
+            nc.scalar.activation(out=wt_quarter[:, g * PACK:g * PACK + tiles], in_=wt_turned[:, 0:tiles, g],
+                                 func=ACT.Copy, scale=-0.25)
 
-        wt_peak = keep.tile([P, 2], F32, name="wt_peak")
-        nc.scalar.activation(out=wt_peak[:], in_=wt_turned[:, 1::2, 1], func=ACT.Copy, scale=0.25)
+        wt_peak = keep.tile([P, 1], F32, name="wt_peak")
+        nc.scalar.activation(out=wt_peak[:], in_=wt_turned[:, 1, 1:2], func=ACT.Copy, scale=0.25)
 
         x_q = [quantised("x%d" % g, K_PASS) for g in range(ROW_PASSES)]
         w_q = quantised("w", N)
@@ -142,13 +143,16 @@ def tile_attend_ghv_nce_kernel(tc, xT, wT, vT, wt, xm, offs, out):
         v_picked = keep.tile([P, PACK, N], F32, name="v_picked")
         slope = [keep.tile([P, PACK, N], F32, name="slope%d" % g) for g in range(ROW_PASSES)]
 
-        def finish_slope(g, t):
+        def weight(g, t):
+            return wt_quarter[:, g * PACK + t:g * PACK + t + 1]
+
+        def finish_slope(g, t, factor):
             nc.vector.tensor_scalar(out=slope[g][:, t, :], in0=slope[g][:, t, :], scalar1=1.0,
-                                    scalar2=wt_quarter[:, g, t:t + 1], op0=ALU.subtract, op1=ALU.mult)
+                                    scalar2=factor, op0=ALU.subtract, op1=ALU.mult)
 
         def finish_slope_scalar(t):
             nc.scalar.activation(out=slope[1][:, t, :], in_=slope[1][:, t, :], func=ACT.Identity,
-                                 scale=wt_quarter[:, 1, t:t + 1], bias=wt_peak[:, t // 2:t // 2 + 1])
+                                 scale=weight(1, t), bias=wt_peak[:])
 
         def tanh_half(g, t, target):
             scores = bank(t, [P, N])
@@ -176,7 +180,7 @@ def tile_attend_ghv_nce_kernel(tc, xT, wT, vT, wt, xm, offs, out):
         square(slope[0][:, 2:4, :], slope[0][:, 2:4, :])
         gather(v_picked, v_planes, 0)
         for t in range(PACK):
-            finish_slope(0, t)
+            finish_slope(0, t, weight(0, t))
         for t in range(PACK - 1):
             tanh_half(1, t, slope[1][:, t, :])
         square(slope[1][:, 0:2, :], slope[1][:, 0:2, :])
@@ -191,9 +195,8 @@ def tile_attend_ghv_nce_kernel(tc, xT, wT, vT, wt, xm, offs, out):
         for t, width in enumerate((512, 512, 128, 64)):
             mx(warm[:, 0:width], x_q[1], block(t), w_q, slice(0, width), E4M3, True, True)
         square(slope[1][:, PACK - 1, :], slope[1][:, PACK - 1, :])
-        finish_slope_scalar(3)
         for t in (0, 2):
-            finish_slope(1, t)
+            finish_slope(1, t, weight(1, t))
 
         last_plane = PACK - 1
         for s in range(2):
@@ -203,9 +206,12 @@ def tile_attend_ghv_nce_kernel(tc, xT, wT, vT, wt, xm, offs, out):
         gather(v_picked, v_planes, last_plane, HALF, N)
         quantise_v(0)
         fill_pair(nc.vector.tensor_copy, 2, 2)
+        last_weight = keep.tile([P, 1], F32, name="v_plane%d" % last_plane)
+        nc.scalar.activation(out=last_weight[:], in_=wt_turned[:, PACK - 1, 1:2], func=ACT.Copy, scale=-0.25)
         fill_pair(nc.scalar.copy, 3, 2)
         for s in range(1, SLOT_BLOCKS):
             quantise_v(s)
+        finish_slope(1, PACK - 1, last_weight[:])
 
         def scores(g, s, number):
             unit = bank(number, [P, PACK, SLOT_BLOCK])
@@ -214,7 +220,7 @@ def tile_attend_ghv_nce_kernel(tc, xT, wT, vT, wt, xm, offs, out):
             return unit
 
         g_grouped = {(g, s): keep.tile([P, SLOT_BLOCK * PACK], BF16, name="g_grouped%d_%d" % (g, s), align_bytes=64)
-                     for g in range(ROW_PASSES) for s in range(SLOT_BLOCKS)}
+                     for g in range(ROW_PASSES) for s in range(SLOT_BLOCKS - g)}
         av = keep.tile([P, SLOT_BLOCK, PACK], F32, name="av", align_bytes=64)
 
         def gradient_vector(g, s, unit, lo=0):
@@ -257,15 +263,18 @@ def tile_attend_ghv_nce_kernel(tc, xT, wT, vT, wt, xm, offs, out):
         def store(b):
             nc.sync.dma_start(out=out[block(b), :], in_=windows[b][:])
 
+        zeros = keep.tile([P, SLOT_BLOCK], F32, name="zeros", align_bytes=64)
+        nc.gpsimd.memset(zeros[:], 0.0)
+
         gradient_vector(0, 0, scores(0, 0, 0))
         gradient_vector(0, 1, scores(0, 1, 1))
+        gradient_gpsimd(0, 2, scores(0, 2, 2), av[:])
         cast_m(0, 0, "m_grouped0")
-        gradient_vector(0, 2, scores(0, 2, 2))
-        gradient_gpsimd(0, 3, scores(0, 3, 5), av[:])
+        gradient_vector(0, 3, scores(0, 3, 5))
         gradient_vector(1, 0, scores(1, 0, 6))
         gradient_vector(1, 1, scores(1, 1, 0))
         gradient_vector(1, 2, scores(1, 2, 1))
-        gradient_vector(1, 3, scores(1, 3, 2))
+        last_unit = scores(1, 3, 6)
         cast_m(0, 1, "v0_codes")
         cast_m(1, 0, "v1_codes")
         cast_m(1, 1, "v2_codes")
@@ -276,17 +285,27 @@ def tile_attend_ghv_nce_kernel(tc, xT, wT, vT, wt, xm, offs, out):
         g_q = [(words("g%d_codes" % g, N)[:], late_scales[:, block(g, N)]) for g in range(ROW_PASSES)]
         for g in range(ROW_PASSES):
             quantise_m(0, g, (words("m0_codes%d" % g, P)[:], late_scales[:, ROW_PASSES * N:][:, block(g)]))
-        halves = [keep.tile([P, HALF], F32, name="dense0_%d" % h, align_bytes=64) for h in range(2)]
-        for s, number in enumerate((7, 3, 5, 6)):
+        last = SLOT_BLOCKS - 1
+        ready = last * SLOT_BLOCK
+        early = keep.tile([P, ready], F32, name="dense_early", align_bytes=64)
+        for s, number in enumerate((7, 3, 2)):
             piece = bank(number, [P, SLOT_BLOCK])
             for g in range(ROW_PASSES):
                 quantise(g_q[g], block(s), g_grouped[g, s][:], E5M2)
                 product(piece, 0, g, block(s))
-            nc.scalar.copy(out=halves[s // 2][:, block(s % 2)], in_=piece[:])
-        for g in range(ROW_PASSES):
-            quantise_m(1, g, held("m1_scales%d" % g, "g_grouped%d_2" % g))
-        for h in range(2):
-            nc.vector.tensor_copy(windows[0][:].indirect(listed(h * HALF, (h + 1) * HALF)), halves[h][:])
+            nc.scalar.copy(out=early[:, block(s)], in_=piece[:])
+        piece = bank(5, [P, SLOT_BLOCK])
+        g_grouped[1, last] = keep.tile([P, SLOT_BLOCK * PACK], BF16, name="g_grouped0_0", align_bytes=64)
+        gradient_vector(1, last, last_unit)
+        quantise(g_q[0], block(last), g_grouped[0, last][:], E5M2)
+        product(piece, 0, 0, block(last))
+        quantise_m(1, 0, held("m1_scales0", "g_grouped0_2"))
+        quantise(g_q[1], block(last), g_grouped[1, last][:], E5M2)
+        product(piece, 0, 1, block(last))
+        dense_last = dense_copy("dense_last", piece)
+        quantise_m(1, 1, held("m1_scales1", "g_grouped0_0"))
+        nc.vector.tensor_copy(windows[0][:].indirect(listed(0, ready)), early[:])
+        nc.vector.tensor_tensor(windows[0][:].indirect(listed(ready, N)), dense_last[:], zeros[:], ALU.add)
         store(0)
 
         def finish_block(b, number):
@@ -297,7 +316,7 @@ def tile_attend_ghv_nce_kernel(tc, xT, wT, vT, wt, xm, offs, out):
             nc.vector.tensor_copy(windows[b][:].indirect(offsets[:]), dense[:])
             store(b)
 
-        late_codes = words("dense0_1", ROW_PASSES * P)
+        late_codes = words("zeros", ROW_PASSES * P)
         for g in range(ROW_PASSES):
             scales = keep.tile([P, P], U8, name="m2_scales%d" % g, align_bytes=64)
             quantise_m(2, g, (late_codes[:, block(g)], scales[:]))

@@ -201,15 +201,14 @@ def tile_attend_ghv_nce_kernel(tc, xT, wT, vT, wt, xm, offs, out):
         last_plane = PACK - 1
         for s in range(2):
             gather(v_picked, v_planes, last_plane, s * SLOT_BLOCK, (s + 1) * SLOT_BLOCK)
-        fill_pair(nc.vector.tensor_copy, 0, 2)
-        fill_pair(nc.scalar.copy, 1, 2)
-        gather(v_picked, v_planes, last_plane, HALF, N)
-        quantise_v(0)
-        fill_pair(nc.vector.tensor_copy, 2, 2)
+        nc.scalar.activation(v_picked[:, last_plane, HALF:N], v_planes[last_plane].indirect(listed(HALF, N)), ACT.Copy)
+        for s in range(2):
+            fill_pair(nc.vector.tensor_copy, s, 2)
+        fill_pair(nc.scalar.copy, 2, 2)
         last_weight = keep.tile([P, 1], F32, name="v_plane%d" % last_plane)
         nc.scalar.activation(out=last_weight[:], in_=wt_turned[:, PACK - 1, 1:2], func=ACT.Copy, scale=-0.25)
         fill_pair(nc.scalar.copy, 3, 2)
-        for s in range(1, SLOT_BLOCKS):
+        for s in range(SLOT_BLOCKS):
             quantise_v(s)
         finish_slope(1, PACK - 1, last_weight[:])
 
@@ -252,8 +251,8 @@ def tile_attend_ghv_nce_kernel(tc, xT, wT, vT, wt, xm, offs, out):
         def held(name, slot):
             return words(slot, P)[:], keep.tile([P, P], U8, name=name, align_bytes=64)[:]
 
-        def product(dst, b, g, cols):
-            mx(dst[:], m_q[b, g], block(0), g_q[g], cols, E5M2, g == 0, g == ROW_PASSES - 1)
+        def product(dst, b, g, cols, first=0):
+            mx(dst[:], m_q[b, g], block(0), g_q[g], cols, E5M2, g == first, g != first)
 
         def dense_copy(name, source):
             dense = keep.tile([P, source.shape[1]], F32, name=name, align_bytes=64)
@@ -299,11 +298,11 @@ def tile_attend_ghv_nce_kernel(tc, xT, wT, vT, wt, xm, offs, out):
         gradient_vector(1, last, last_unit)
         quantise(g_q[0], block(last), g_grouped[0, last][:], E5M2)
         product(piece, 0, 0, block(last))
-        quantise_m(1, 0, held("m1_scales0", "g_grouped0_2"))
+        quantise_m(1, 1, held("m1_scales1", "g_grouped1_2"))
         quantise(g_q[1], block(last), g_grouped[1, last][:], E5M2)
         product(piece, 0, 1, block(last))
         dense_last = dense_copy("dense_last", piece)
-        quantise_m(1, 1, held("m1_scales1", "g_grouped0_0"))
+        quantise_m(1, 0, held("m1_scales0", "g_grouped0_3"))
         nc.vector.tensor_copy(windows[0][:].indirect(listed(0, ready)), early[:])
         nc.vector.tensor_tensor(windows[0][:].indirect(listed(ready, N)), dense_last[:], zeros[:], ALU.add)
         store(0)
@@ -322,8 +321,8 @@ def tile_attend_ghv_nce_kernel(tc, xT, wT, vT, wt, xm, offs, out):
             quantise_m(2, g, (late_codes[:, block(g)], scales[:]))
         for h, number in enumerate((0, 4)):
             sums = bank(number, [P, HALF])
-            for g in range(ROW_PASSES):
-                product(sums, 1, g, block(h, HALF))
+            for g in (1, 0):
+                product(sums, 1, g, block(h, HALF), first=1)
             dense = dense_copy("dense1_%d" % h, sums)
             nc.vector.tensor_copy(windows[1][:].indirect(listed(h * HALF, (h + 1) * HALF)), dense[:])
         store(1)

@@ -272,13 +272,12 @@ def tile_attend_ghv_nce_kernel(tc, xT, wT, vT, wt, xm, offs, out):
         gradient_vector(0, 3, scores(0, 3, 5))
         gradient_vector(1, 0, scores(1, 0, 6))
         gradient_vector(1, 1, scores(1, 1, 0))
-        gradient_vector(1, 2, scores(1, 2, 1))
-        last_unit = scores(1, 3, 6)
+        gradient_vector(1, 2, scores(1, 2, 5))
+        last_unit = scores(1, 3, 5)
         cast_m(0, 1, "v0_codes")
         cast_m(1, 0, "v1_codes")
         cast_m(1, 1, "v2_codes")
         cast_m(2, 0, "v3_codes")
-        cast_m(2, 1, "m_grouped0")
 
         late_scales = keep.tile([P, ROW_PASSES * (N + P)], U8, name="av", align_bytes=64)
         g_q = [(words("g%d_codes" % g, N)[:], late_scales[:, block(g, N)]) for g in range(ROW_PASSES)]
@@ -293,7 +292,7 @@ def tile_attend_ghv_nce_kernel(tc, xT, wT, vT, wt, xm, offs, out):
                 quantise(g_q[g], block(s), g_grouped[g, s][:], E5M2)
                 product(piece, 0, g, block(s))
             nc.scalar.copy(out=early[:, block(s)], in_=piece[:])
-        piece = bank(5, [P, SLOT_BLOCK])
+        piece = bank(1, [P, SLOT_BLOCK])
         g_grouped[1, last] = keep.tile([P, SLOT_BLOCK * PACK], BF16, name="g_grouped0_0", align_bytes=64)
         gradient_vector(1, last, last_unit)
         quantise(g_q[0], block(last), g_grouped[0, last][:], E5M2)
@@ -315,10 +314,9 @@ def tile_attend_ghv_nce_kernel(tc, xT, wT, vT, wt, xm, offs, out):
             nc.vector.tensor_copy(windows[b][:].indirect(offsets[:]), dense[:])
             store(b)
 
-        late_codes = words("zeros", ROW_PASSES * P)
-        for g in range(ROW_PASSES):
-            scales = keep.tile([P, P], U8, name="m2_scales%d" % g, align_bytes=64)
-            quantise_m(2, g, (late_codes[:, block(g)], scales[:]))
+        cast_m(2, 1, "zeros", nc.vector.tensor_copy)
+        quantise_m(2, 0, held("m2_scales0", "dense_last"))
+        quantise_m(2, 1, quantised("m2_1", P))
         for h, number in enumerate((0, 4)):
             sums = bank(number, [P, HALF])
             for g in (1, 0):
@@ -330,5 +328,5 @@ def tile_attend_ghv_nce_kernel(tc, xT, wT, vT, wt, xm, offs, out):
         cast_m(3, 1, "dense1_1", nc.vector.tensor_copy)
         for g in range(ROW_PASSES):
             quantise_m(3, g, quantised("m3_%d" % g, P))
-        finish_block(2, 1)
+        finish_block(2, 6)
         finish_block(3, 2)

@@ -146,12 +146,12 @@ def tile_attend_ghv_nce_kernel(tc, xT, wT, vT, wt, xm, offs, out):
         def weight(g, t):
             return wt_quarter[:, g * PACK + t:g * PACK + t + 1]
 
-        def finish_slope(g, t, factor):
-            nc.vector.tensor_scalar(out=slope[g][:, t, :], in0=slope[g][:, t, :], scalar1=1.0,
+        def finish_slope(g, t, factor, cols=whole):
+            nc.vector.tensor_scalar(out=slope[g][:, t, cols], in0=slope[g][:, t, cols], scalar1=1.0,
                                     scalar2=factor, op0=ALU.subtract, op1=ALU.mult)
 
-        def finish_slope_scalar(t):
-            nc.scalar.activation(out=slope[1][:, t, :], in_=slope[1][:, t, :], func=ACT.Identity,
+        def finish_slope_scalar(t, cols):
+            nc.scalar.activation(out=slope[1][:, t, cols], in_=slope[1][:, t, cols], func=ACT.Identity,
                                  scale=weight(1, t), bias=wt_peak[:])
 
         def tanh_half(g, t, target):
@@ -189,14 +189,15 @@ def tile_attend_ghv_nce_kernel(tc, xT, wT, vT, wt, xm, offs, out):
         for s in range(SLOT_BLOCKS):
             fill_pair(nc.vector.tensor_copy, s, 0)
         gather(v_picked, v_planes, 2)
-        finish_slope_scalar(1)
+        finish_slope_scalar(1, block(0, HALF))
         tanh_half(1, PACK - 1, slope[1][:, PACK - 1, :])
         warm = bank(PACK - 1, [P, N])
         for t, width in enumerate((512, 512, 128, 64)):
             mx(warm[:, 0:width], x_q[1], block(t), w_q, slice(0, width), E4M3, True, True)
         square(slope[1][:, PACK - 1, :], slope[1][:, PACK - 1, :])
-        for t in (0, 2):
-            finish_slope(1, t, weight(1, t))
+        finish_slope(1, 0, weight(1, 0))
+        finish_slope(1, 1, weight(1, 1), block(1, HALF))
+        finish_slope(1, 2, weight(1, 2))
 
         last_plane = PACK - 1
         for s in range(2):

@@ -315,9 +315,7 @@ def tile_attend_ghv_nce_kernel(tc, xT, wT, vT, wt, xm, offs, out):
             nc.vector.tensor_copy(windows[b][:].indirect(offsets[:]), dense[:])
             store(b)
 
-        cast_m(2, 1, "zeros", nc.vector.tensor_copy)
-        quantise_m(2, 0, held("m2_scales0", "dense_last"))
-        quantise_m(2, 1, quantised("m2_1", P))
+        cast_m(2, 1, "zeros")
         for h, number in enumerate((0, 4)):
             sums = bank(number, [P, HALF])
             for g in (1, 0):
@@ -325,8 +323,10 @@ def tile_attend_ghv_nce_kernel(tc, xT, wT, vT, wt, xm, offs, out):
             dense = dense_copy("dense1_%d" % h, sums)
             nc.vector.tensor_copy(windows[1][:].indirect(listed(h * HALF, (h + 1) * HALF)), dense[:])
         store(1)
+        quantise_m(2, 0, held("m2_scales0", "dense_last"))
+        quantise_m(2, 1, quantised("m2_1", P))
         cast_m(3, 0, "dense1_0")
-        cast_m(3, 1, "dense1_1", nc.vector.tensor_copy)
+        cast_m(3, 1, "dense1_1")
         for g in range(ROW_PASSES):
             quantise_m(3, g, quantised("m3_%d" % g, P))
         finish_block(2, 6)

from contextlib import ExitStack

import concourse.mybir as mybir
from concourse.masks import make_identity

D, R, T, N = 512, 1024, 2048, 512
FLOPS = 3 * 2 * R * D * N

F32 = mybir.dt.float32
BF16 = mybir.dt.bfloat16
U32 = mybir.dt.uint32
I32 = mybir.dt.int32
U16 = mybir.dt.uint16
U8 = mybir.dt.uint8
E4M3 = mybir.dt.float8_e4m3fn_x4
E5M2 = mybir.dt.float8_e5m2_x4
ALU = mybir.AluOpType
ACT = mybir.ActivationFunctionType

P = 128
PACK = 4
K_PASS = P * PACK
ROW_PASSES = R // K_PASS
SLOT_BLOCK = 128
SLOT_BLOCKS = N // SLOT_BLOCK
D_BLOCKS = D // P
HALF = N // 2


def tile_attend_ghv_nce_kernel(tc, xT, wT, vT, wt, xm, offs, out):
    nc = tc.nc
    with ExitStack() as ctx:
        keep = ctx.enter_context(tc.tile_pool(name="keep", bufs=1))
        psum = ctx.enter_context(tc.psum_pool(name="psum", bufs=1))

        def block(index, width=P):
            return slice(index * width, (index + 1) * width)

        def bank(number, shape):
            return psum.tile(shape, F32, name="bank%d" % number)

        def words(name, width):
            return keep.tile([P, width], U32, name=name, align_bytes=64)

        def quantised(name, width):
            return (words(name + "_codes", width)[:],
                    keep.tile([P, width], U8, name=name + "_scales", align_bytes=64)[:])

        def quantise(pair, cols, grouped, fmt):
            nc.vector.quantize_mx(out=pair[0][:, cols].bitcast(fmt), scales=pair[1][:, cols], in_=grouped)

        def mx(dst, lhs, lhs_cols, rhs, rhs_cols, rhs_fmt, start, stop):
            nc.tensor.matmul_mx(
                out=dst,
                lhsT=lhs[0][:, lhs_cols].bitcast(E4M3), lhsT_scale=lhs[1][:, lhs_cols],
                rhs=rhs[0][:, rhs_cols].bitcast(rhs_fmt), rhs_scale=rhs[1][:, rhs_cols],
                start=start, stop=stop,
            )

        def interleave(copy, grouped, planes):
            copy(out=grouped.rearrange("p (c i t) -> p c t i", i=2, t=PACK),
                 in_=planes.rearrange("p t (c i) -> p c t i", i=2))

        def listed(lo, hi):
            return offsets[:, lo // 16:hi // 16]

        offsets = keep.tile([P, N // 16], U16, name="offsets")
        x_raw = [keep.tile([P, PACK, K_PASS], F32, name="x_raw%d" % g) for g in range(ROW_PASSES)]
        m_raw = [[keep.tile([P, PACK, P], F32, name="m_raw%d_%d" % (b, g)) for g in range(ROW_PASSES)]
                 for b in range(D_BLOCKS)]
        plane_loads = (slice(0, 2), slice(2, 3), slice(3, 4))
        w_tiles = [keep.tile([P, js.stop - js.start, T], F32, name="w_from%d" % js.start) for js in plane_loads]
        w_planes = [tile[:, k, :] for tile in w_tiles for k in range(tile.shape[1])]
        v_planes = [keep.tile([P, T], F32, name="v_plane%d" % j)[:] for j in range(PACK)]
        wt_rows = keep.tile([P, K_PASS], F32, name="wt_rows")
        identity = keep.tile([P, P], F32, name="identity")
        nc.gpsimd.memset(wt_rows[:], 0.0)
        make_identity(nc, identity[:])
        x_rows = xT[0].rearrange("(p j) r -> p j r", j=PACK)
        w_rows = wT.rearrange("(p j) c -> p j c", j=PACK)
        v_rows = vT.rearrange("(p j) c -> p j c", j=PACK)
        m_rows = xm[0].rearrange("(g p t) d -> g p t d", p=P, t=PACK)

        nc.sync.dma_start(out=w_tiles[0][:], in_=w_rows[:, plane_loads[0], :])
        nc.sync.dma_start(offsets[:], offs)
        nc.sync.dma_start(out=wt_rows[0:ROW_PASSES, :], in_=wt[0].rearrange("(g k) o -> g (k o)", g=ROW_PASSES))
        for tile, js in zip(w_tiles[1:], plane_loads[1:]):
            nc.sync.dma_start(out=tile[:], in_=w_rows[:, js, :])
        for g in range(ROW_PASSES):
            nc.sync.dma_start(out=x_raw[g][:], in_=x_rows[:, :, block(g, K_PASS)])
        for j in range(PACK):
            nc.sync.dma_start(out=v_planes[j], in_=v_rows[:, j, :])
        for b in range(D_BLOCKS):
            for g in range(ROW_PASSES):
                nc.sync.dma_start(out=m_raw[b][g][:], in_=m_rows[g][:, :, block(b)])

        windows = [keep.tile([P, T], F32, name="window%d" % b) for b in range(D_BLOCKS)]
        for b in range(D_BLOCKS):
            engine = nc.gpsimd if b % 2 else nc.vector
            engine.memset(windows[b][:].bitcast(I32), 0)

        wt_quarter = keep.tile([P, ROW_PASSES * PACK - 1], F32, name="wt_quarter")
        wt_turned = bank(4, [P, PACK, P])
        for t in range(PACK):
            nc.tensor.transpose(wt_turned[:, t, :], wt_rows[:, t::PACK], identity[:])
        for g, tiles in enumerate((PACK, PACK - 1)):
            nc.scalar.activation(out=wt_quarter[:, g * PACK:g * PACK + tiles], in_=wt_turned[:, 0:tiles, g],
                                 func=ACT.Copy, scale=-0.25)

        wt_peak = keep.tile([P, 1], F32, name="wt_peak")
        nc.scalar.activation(out=wt_peak[:], in_=wt_turned[:, 1, 1:2], func=ACT.Copy, scale=0.25)

        x_q = [quantised("x%d" % g, K_PASS) for g in range(ROW_PASSES)]
        w_q = quantised("w", N)
        v_q = [quantised("v%d" % s, SLOT_BLOCK) for s in range(SLOT_BLOCKS)]

        def prepare_x(g, copies):
            grouped = [keep.tile([P, 2 * P * PACK], BF16, name="x_grouped%d_%d" % (g, h), align_bytes=64)
                       for h in range(2)]
            for h in range(2):
                target = grouped[h][:].rearrange("p (t m j) -> p m j t", t=2, j=PACK)
                source = x_raw[g][:].rearrange("p j (m t) -> p m j t", t=PACK)[:, :, :, 2 * h:2 * h + 2]
                for copy, cols in copies[h]:
                    copy(out=target[:, cols], in_=source[:, cols])
            for h in range(2):
                quantise(x_q[g], block(h, 2 * P), grouped[h][:], E4M3)

        def gather(picked, planes, j, lo=0, hi=N):
            nc.vector.tensor_copy(picked[:, j, lo:hi], planes[j].indirect(listed(lo, hi)))

        v_grouped = [keep.tile([P, SLOT_BLOCK, PACK], BF16, name="v_grouped%d" % s, align_bytes=64)
                     for s in range(SLOT_BLOCKS)]

        def fill_pair(copy, s, first):
            copy(out=v_grouped[s][:, :, first:first + 2],
                 in_=v_picked[:, first:first + 2, block(s)].rearrange("p t c -> p c t"))

        def quantise_v(s):
            quantise(v_q[s], block(0), v_grouped[s][:].rearrange("p c t -> p (c t)"), E4M3)

        whole = slice(0, N)
        w_picked = keep.tile([P, PACK, N], F32, name="w_picked")
        v_picked = keep.tile([P, PACK, N], F32, name="v_picked")
        slope = [keep.tile([P, PACK, N], F32, name="slope%d" % g) for g in range(ROW_PASSES)]

        def weight(g, t):
            return wt_quarter[:, g * PACK + t:g * PACK + t + 1]

        def finish_slope(g, t, factor, cols=whole):
            nc.vector.tensor_scalar(out=slope[g][:, t, cols], in0=slope[g][:, t, cols], scalar1=1.0,
                                    scalar2=factor, op0=ALU.subtract, op1=ALU.mult)

        def finish_slope_scalar(t, cols):
            nc.scalar.activation(out=slope[1][:, t, cols], in_=slope[1][:, t, cols], func=ACT.Identity,
                                 scale=weight(1, t), bias=wt_peak[:])

        def tanh_half(g, t, target):
            scores = bank(t, [P, N])
            mx(scores[:], x_q[g], block(t), w_q, whole, E4M3, True, True)
            nc.scalar.activation(out=target, in_=scores[:], func=ACT.Tanh, scale=0.5)

        def square(target, values):
            nc.scalar.activation(out=target, in_=values, func=ACT.Square)

        for j in range(PACK - 1):
            gather(w_picked, w_planes, j)
        w_grouped = [keep.tile([P, HALF * PACK], BF16, name="w_grouped%d" % h, align_bytes=64) for h in range(2)]
        for h in range(2):
            gather(w_picked, w_planes, PACK - 1, h * HALF, (h + 1) * HALF)
        for s, copy in enumerate((nc.scalar.copy, nc.vector.tensor_copy, nc.vector.tensor_copy, nc.scalar.copy)):
            interleave(copy, w_grouped[s // 2][:, block(s % 2, SLOT_BLOCK * PACK)], w_picked[:, :, block(s)])
        for h in range(2):
            quantise(w_q, block(h, HALF), w_grouped[h][:], E4M3)
        prepare_x(0, [((nc.scalar.copy, slice(0, cut)), (nc.vector.tensor_copy, slice(cut, P))) for cut in (96, 64)])
        prepare_x(1, [((nc.vector.tensor_copy, slice(0, P)),)] * 2)
        for t in range(PACK):
            tanh_half(0, t, slope[0][:, t, :])
        lower = slope[0][:, 0:2, :]
        nc.vector.tensor_tensor(out=lower, in0=lower, in1=lower, op=ALU.mult)
        square(slope[0][:, 2:4, :], slope[0][:, 2:4, :])
        gather(v_picked, v_planes, 0)
        for t in range(PACK):
            finish_slope(0, t, weight(0, t))
        for t in range(PACK - 1):
            tanh_half(1, t, slope[1][:, t, :])
        square(slope[1][:, 0:2, :], slope[1][:, 0:2, :])
        square(slope[1][:, 2, :], slope[1][:, 2, :])
        gather(v_picked, v_planes, 1)
        for s in range(SLOT_BLOCKS):
            fill_pair(nc.vector.tensor_copy, s, 0)
        gather(v_picked, v_planes, 2)
        finish_slope_scalar(1, block(0, HALF))
        tanh_half(1, PACK - 1, slope[1][:, PACK - 1, :])
        warm = bank(PACK - 1, [P, N])
        for t, width in enumerate((512, 512, 128, 64)):
            mx(warm[:, 0:width], x_q[1], block(t), w_q, slice(0, width), E4M3, True, True)
        square(slope[1][:, PACK - 1, :], slope[1][:, PACK - 1, :])
        finish_slope(1, 0, weight(1, 0))
        finish_slope(1, 1, weight(1, 1), block(1, HALF))
        finish_slope(1, 2, weight(1, 2))

        last_plane = PACK - 1
        for s in range(2):
            gather(v_picked, v_planes, last_plane, s * SLOT_BLOCK, (s + 1) * SLOT_BLOCK)
        nc.scalar.activation(v_picked[:, last_plane, HALF:N], v_planes[last_plane].indirect(listed(HALF, N)), ACT.Copy)
        for s in range(2):
            fill_pair(nc.vector.tensor_copy, s, 2)
        fill_pair(nc.scalar.copy, 2, 2)
        last_weight = keep.tile([P, 1], F32, name="v_plane%d" % last_plane)
        nc.scalar.activation(out=last_weight[:], in_=wt_turned[:, PACK - 1, 1:2], func=ACT.Copy, scale=-0.25)
        fill_pair(nc.scalar.copy, 3, 2)
        for s in range(SLOT_BLOCKS):
            quantise_v(s)
        finish_slope(1, PACK - 1, last_weight[:])

        def scores(g, s, number):
            unit = bank(number, [P, PACK, SLOT_BLOCK])
            for t in range(PACK):
                mx(unit[:, t, :], x_q[g], block(t), v_q[s], block(0), E4M3, True, True)
            return unit

        g_grouped = {(g, s): keep.tile([P, SLOT_BLOCK * PACK], BF16, name="g_grouped%d_%d" % (g, s), align_bytes=64)
                     for g in range(ROW_PASSES) for s in range(SLOT_BLOCKS - g)}
        av = keep.tile([P, SLOT_BLOCK, PACK], F32, name="av", align_bytes=64)

        def gradient_vector(g, s, unit, lo=0):
            nc.vector.tensor_tensor(
                out=g_grouped[g, s][:, lo * PACK:].rearrange("p (c i t) -> p c t i", i=4, t=PACK),
                in0=slope[g][:, :, s * SLOT_BLOCK + lo:(s + 1) * SLOT_BLOCK].rearrange("p t (c i) -> p c t i", i=4),
                in1=unit[:, :, lo:].rearrange("p t (c i) -> p c t i", i=4),
                op=ALU.mult)

        def gradient_gpsimd(g, s, unit, staging):
            width = staging.shape[1]
            nc.scalar.copy(out=staging, in_=unit[:, :, 0:width].rearrange("p t c -> p c t"))
            nc.gpsimd.tensor_tensor(
                out=g_grouped[g, s][:, 0:width * PACK].rearrange("p (c t) -> p c t", t=PACK),
                in0=staging,
                in1=slope[g][:, :, s * SLOT_BLOCK:s * SLOT_BLOCK + width].rearrange("p t c -> p c t"), op=ALU.mult)

        m_grouped = {}
        m_q = {}

        def cast_m(b, g, slot, copy=nc.scalar.copy):
            m_grouped[b, g] = keep.tile([P, P * PACK], BF16, name=slot, align_bytes=64)[:]
            interleave(copy, m_grouped[b, g], m_raw[b][g][:])

        def quantise_m(b, g, pair):
            m_q[b, g] = pair
            quantise(pair, block(0), m_grouped[b, g], E4M3)

        def held(name, slot):
            return words(slot, P)[:], keep.tile([P, P], U8, name=name, align_bytes=64)[:]

        def product(dst, b, g, cols, first=0):
            mx(dst[:], m_q[b, g], block(0), g_q[g], cols, E5M2, g == first, g != first)

        def dense_copy(name, source):
            dense = keep.tile([P, source.shape[1]], F32, name=name, align_bytes=64)
            nc.scalar.copy(out=dense[:], in_=source[:])
            return dense

        def store(b):
            nc.sync.dma_start(out=out[block(b), :], in_=windows[b][:])

        zeros = keep.tile([P, SLOT_BLOCK], F32, name="zeros", align_bytes=64)
        nc.gpsimd.memset(zeros[:], 0.0)

        gradient_vector(0, 0, scores(0, 0, 0))
        gradient_vector(0, 1, scores(0, 1, 1))
        gradient_gpsimd(0, 2, scores(0, 2, 2), av[:])
        cast_m(0, 0, "m_grouped0")
        gradient_vector(0, 3, scores(0, 3, 5))
        gradient_vector(1, 0, scores(1, 0, 6))
        gradient_vector(1, 1, scores(1, 1, 0))
        gradient_vector(1, 2, scores(1, 2, 5))
        last_unit = scores(1, 3, 5)
        cast_m(0, 1, "v0_codes")
        cast_m(1, 0, "v1_codes")
        cast_m(1, 1, "v2_codes")
        cast_m(2, 0, "v3_codes")

        late_scales = keep.tile([P, ROW_PASSES * (N + P)], U8, name="av", align_bytes=64)
        g_q = [(words("g%d_codes" % g, N)[:], late_scales[:, block(g, N)]) for g in range(ROW_PASSES)]
        for g in range(ROW_PASSES):
            quantise_m(0, g, (words("m0_codes%d" % g, P)[:], late_scales[:, ROW_PASSES * N:][:, block(g)]))
        last = SLOT_BLOCKS - 1
        ready = last * SLOT_BLOCK
        early = keep.tile([P, ready], F32, name="dense_early", align_bytes=64)
        for s, number in enumerate((7, 3, 2)):
            piece = bank(number, [P, SLOT_BLOCK])
            for g in range(ROW_PASSES):
                quantise(g_q[g], block(s), g_grouped[g, s][:], E5M2)
                product(piece, 0, g, block(s))
            nc.scalar.copy(out=early[:, block(s)], in_=piece[:])
        piece = bank(1, [P, SLOT_BLOCK])
        g_grouped[1, last] = keep.tile([P, SLOT_BLOCK * PACK], BF16, name="g_grouped0_0", align_bytes=64)
        gradient_vector(1, last, last_unit)
        quantise(g_q[0], block(last), g_grouped[0, last][:], E5M2)
        product(piece, 0, 0, block(last))
        quantise_m(1, 1, held("m1_scales1", "g_grouped1_2"))
        quantise(g_q[1], block(last), g_grouped[1, last][:], E5M2)
        product(piece, 0, 1, block(last))
        dense_last = dense_copy("dense_last", piece)
        quantise_m(1, 0, held("m1_scales0", "g_grouped0_3"))
        nc.vector.tensor_copy(windows[0][:].indirect(listed(0, ready)), early[:])
        nc.vector.tensor_tensor(windows[0][:].indirect(listed(ready, N)), dense_last[:], zeros[:], ALU.add)
        store(0)

        def finish_block(b, number):
            sums = bank(number, [P, N])
            for g in range(ROW_PASSES):
                product(sums, b, g, whole)
            dense = dense_copy("dense%d" % b, sums)
            nc.vector.tensor_copy(windows[b][:].indirect(offsets[:]), dense[:])
            store(b)

        cast_m(2, 1, "zeros")
        for h, number in enumerate((0, 4)):
            sums = bank(number, [P, HALF])
            for g in (1, 0):
                product(sums, 1, g, block(h, HALF), first=1)
            dense = dense_copy("dense1_%d" % h, sums)
            nc.vector.tensor_copy(windows[1][:].indirect(listed(h * HALF, (h + 1) * HALF)), dense[:])
        store(1)
        quantise_m(2, 0, held("m2_scales0", "dense_last"))
        quantise_m(2, 1, quantised("m2_1", P))
        cast_m(3, 0, "dense1_0")
        cast_m(3, 1, "dense1_1")
        for g in range(ROW_PASSES):
            quantise_m(3, g, quantised("m3_%d" % g, P))
        finish_block(2, 6)
        finish_block(3, 2)
